import numpy as np
import ml_dtypes


def mxq(x, axis, fmt="e4m3"):
    dtype, down = {"e4m3": (ml_dtypes.float8_e4m3fn, 7), "e5m2": (ml_dtypes.float8_e5m2, 14)}[fmt]
    v = np.moveaxis(np.asarray(x, np.float32).astype(ml_dtypes.bfloat16).astype(np.float64), axis, -1)
    blocks = v.reshape(v.shape[:-1] + (-1, 32))
    amax = np.abs(blocks).max(-1, keepdims=True)
    byte = np.maximum(np.where(amax > 0, np.frexp(amax)[1] - 1 + 127, 0) - down, 1)
    scale = np.exp2(byte - 127.0)
    codes = (blocks / scale).astype(np.float32).astype(dtype).astype(np.float64)
    return np.moveaxis((codes * scale).reshape(v.shape), -1, axis)


WIDE = False


def mx_kscale(k):
    if not WIDE:
        return np.ones(k)
    levels = np.array([10, -10, 5, -5, 0])
    if k % 512:
        return np.exp2(np.random.permutation(np.resize(levels, k // 32))).repeat(32)
    a = np.empty((k // 512, 16))
    for p in range(k // 512):
        a[p, :8] = np.random.permutation(np.resize(levels, 8))
        for g in range(8):
            far = levels[np.abs(levels - a[p, g]) >= 10]
            a[p, g + 8] = far[np.random.randint(len(far))]
    return np.exp2(a.ravel()).repeat(32)


def f64(x):
    return np.asarray(x).astype(np.float64)


def striped(idx):
    return np.tile(idx.reshape(-1, 16).T, (8, 1)).astype(np.uint16)


def unstriped(offs):
    return offs[:16].T.reshape(-1).astype(np.int64)


E2M1 = np.array([0.0, 0.5, 1.0, 1.5, 2.0, 3.0, 4.0, 6.0, -0.0, -0.5, -1.0, -1.5, -2.0, -3.0, -4.0, -6.0])


def pack_weight(w, fmt):
    k, n = w.shape
    w = f64(np.asarray(w, np.float32).astype(ml_dtypes.bfloat16)).reshape(k // 32, 32, n)
    amax = np.abs(w).max(1)
    if fmt == "e4m3":
        byte = np.frexp(amax)[1] - 1 + 127 - 7
    else:
        mant, ex = np.frexp(amax / 6.0)
        byte = np.where(mant > 0.5, ex, ex - 1) + 127
    byte = np.clip(np.where(amax > 0, byte, 1), 1, 254)
    scaled = (w * np.exp2(127.0 - byte)[:, None, :]).reshape(k, n).astype(np.float32)
    by_word = np.ascontiguousarray(scaled.reshape(k // 512, 128, 4, n).transpose(0, 1, 3, 2))
    if fmt == "e4m3":
        words = by_word.astype(ml_dtypes.float8_e4m3fn).view(np.uint8)
    else:
        c = by_word.astype(ml_dtypes.float4_e2m1fn).view(np.uint8) & 0xF
        words = (c[..., 0::2] | (c[..., 1::2] << 4)).reshape(k // 512, 128, 2 * n)
    return np.ascontiguousarray(words), np.ascontiguousarray(byte.astype(np.uint8).reshape(k // 512, 16, n))


def unpack_weight(words, scales, fmt):
    g, _, n = scales.shape
    words = np.ascontiguousarray(words).reshape(g, 128, n, -1)
    if fmt == "e4m3":
        vals = words.view(ml_dtypes.float8_e4m3fn).astype(np.float64)
    else:
        nib = np.empty((g, 128, n, 4), np.uint8)
        nib[..., 0::2] = words & 0xF
        nib[..., 1::2] = words >> 4
        vals = E2M1[nib]
    vals = vals * np.repeat(np.exp2(scales.astype(np.float64) - 127.0), 8, axis=1)[..., None]
    return vals.transpose(0, 1, 3, 2).reshape(g * 512, n)


def gelu(v):
    return 0.5 * v * (1.0 + np.tanh(np.sqrt(2.0 / np.pi) * (v + 0.044715 * v**3)))


def striped8(idx):
    return np.concatenate([v.reshape(-1, 16).T for v in idx]).astype(np.uint16)


def unstriped8(offs):
    return np.stack([offs[16 * g:16 * g + 16].T.reshape(-1) for g in range(8)]).astype(np.int64)


def runs(v, idx8):
    k = np.arange(v.shape[0])
    return v[k[:, None], idx8[k % 512 // 64]]


def put_heads(h, wgs, idx8, t2):
    r = np.arange(h.shape[0])
    page = np.zeros((h.shape[0], t2))
    page[r[:, None], idx8[r % 512 // 64]] = wgs[r // 4 % 128] * h
    return page


K, H, N, T, S, T2 = 512, 1024, 512, 2048, 1024, 2048

def setup_inputs():
    n = np.random.standard_normal
    s = mx_kscale(K)[:, None]
    u = mx_kscale(H)[:, None]
    tab_words, tab_scales = pack_weight(n((K, T)) * s, "e4m3")
    wa = (1.5 * n((K, H)) / np.sqrt(K) / s).astype(np.float32)
    wb_words, wb_scales = pack_weight(n((K, H)) / np.sqrt(K) / s * u.T, "e2m1")
    wc_words, wc_scales = pack_weight(1.5 * n((K, N)) / np.sqrt(K) / s, "e4m3")
    wd = (n((H, N)) / np.sqrt(H) / u).astype(np.float32)
    we_words, we_scales = pack_weight(n((H, N)) / np.sqrt(H) / u, "e2m1")
    offs = striped8(np.stack([np.random.permutation(T)[:S] for _ in range(8)]))
    offs2 = striped8(np.stack([np.random.permutation(T2)[:S] for _ in range(8)]))
    wgo = np.repeat(np.random.uniform(0.5, 2.0, (8, S)), 16, axis=0).astype(np.float32)
    return {"tab_words": tab_words, "tab_scales": tab_scales, "offs": offs,
            "wa": wa, "wb_words": wb_words, "wb_scales": wb_scales,
            "wc_words": wc_words, "wc_scales": wc_scales, "wd": wd,
            "we_words": we_words, "we_scales": we_scales,
            "offs2": offs2, "wgo": wgo}

def reference(tab_words, tab_scales, offs, wa, wb_words, wb_scales, wc_words, wc_scales,
              wd, we_words, we_scales, offs2, wgo):
    v = runs(unpack_weight(tab_words, tab_scales, "e4m3"), unstriped8(offs))
    a = mxq(f64(wa), 0, "e4m3").T @ v
    b = unpack_weight(wb_words, wb_scales, "e2m1").T @ v
    h = a / (1.0 + np.exp(-a)) * b
    c = unpack_weight(wc_words, wc_scales, "e4m3").T @ v
    mix = 1.0 / (1.0 + np.exp(-c))
    hq = mxq(h, 0, "e4m3")
    d = mxq(f64(wd), 0, "e4m3").T @ hq
    e = unpack_weight(we_words, we_scales, "e2m1").T @ hq
    y = e + mix * (d - e)
    return put_heads(y, f64(wgo), unstriped8(offs2), T2)

@@ -1,0 +1,283 @@
+from contextlib import ExitStack
+
+import concourse.mybir as mybir
+from concourse.masks import make_identity
+
+K, H, N, T, S, T2 = 512, 1024, 512, 2048, 1024, 2048
+FLOPS = 2 * S * (2 * K * H + K * N + 2 * H * N)
+
+F32 = mybir.dt.float32
+BF16 = mybir.dt.bfloat16
+I32 = mybir.dt.int32
+U32 = mybir.dt.uint32
+U16 = mybir.dt.uint16
+U8 = mybir.dt.uint8
+FP8X4 = mybir.dt.float8_e4m3fn_x4
+FP4X4 = mybir.dt.float4_e2m1fn_x4
+ACT = mybir.ActivationFunctionType
+ALU = mybir.AluOpType
+
+P = 128
+PACK = 4
+KP = P * PACK
+HB = H // KP
+JT = S // P
+LIST_COLS = P // 16
+
+
+def tile_list_sniff_correction_kernel(
+    tc, tab_words, tab_scales, offs, wa, wb_words, wb_scales, wc_words, wc_scales,
+    wd, we_words, we_scales, offs2, wgo, out,
+):
+    nc = tc.nc
+    with ExitStack() as ctx:
+        keep = ctx.enter_context(tc.tile_pool(name="keep", bufs=1))
+        ring = ctx.enter_context(tc.tile_pool(name="ring", bufs=2))
+        psum = ctx.enter_context(tc.psum_pool(name="psum", bufs=1))
+
+        def held(shape, dtype, name, tag=None):
+            return keep.tile(shape, dtype, name=name, tag=tag or name, align_bytes=64)
+
+        pick = held([P, S // 16], U16, "pick")
+        place = held([P, S // 16], U16, "place")
+        tab_w = held([P, T], U32, "tab_w", "slot_b")
+        tab_s = held([P, T], U8, "tab_s", "slot_a")
+        wb_s_raw = held([P, H], U8, "wb_s_raw", "slot_e")
+        warm = held([P, 8], F32, "warm")
+        warm_out = held([P, 8], F32, "warm_out")
+        pages = [held([P, T2], F32, "page%d" % i) for i in range(2)]
+
+        nc.gpsimd.memset(tab_s[:].bitcast(I32), 0)
+        nc.vector.memset(wb_s_raw[:].bitcast(I32), 0)
+        nc.vector.memset(warm[:], 0.0)
+
+        def load_scale_rows(queue, plane, rows):
+            passes = rows.shape[0]
+            dst = plane.bitcast(I32).rearrange("p (a w) -> p a w", a=passes)
+            src = rows.bitcast(I32)
+            for q in range(4):
+                queue.dma_start(
+                    out=dst[32 * q : 32 * q + 4, :, :],
+                    in_=src[:, 4 * q : 4 * q + 4, :].rearrange("a r w -> r a w"),
+                )
+
+        wa_rows = wa.rearrange("(p i) c -> p i c", i=PACK)
+        wa_raw0 = held([P, PACK, KP], F32, "wa_raw0", "slot_c")
+        wb_raw = held([P, 2 * H], U8, "wb_raw", "slot_d")
+
+        nc.sync.dma_start(pick[:], offs)
+        nc.sync.dma_start(
+            out=tab_w[:].bitcast(I32),
+            in_=tab_words[0].rearrange("p t i -> p (t i)").bitcast(I32),
+        )
+        tab_rows = tab_scales[0].bitcast(I32)
+        for e in range(2):
+            nc.scalar.dma_start(out=tab_s[:].bitcast(I32)[e:P:16, :], in_=tab_rows[e:16:2, :])
+        nc.scalar.activation(warm_out[:], warm[:], ACT.Silu)
+        nc.sync.dma_start(out=wa_raw0[:], in_=wa_rows[:, :, 0:KP])
+        nc.sync.dma_start(out=wb_raw[:].bitcast(I32), in_=wb_words[0].bitcast(I32))
+        load_scale_rows(nc.gpsimd, wb_s_raw[:], wb_scales)
+        nc.sync.dma_start(place[:], offs2)
+
+        for page in pages:
+            nc.vector.memset(page[:], 0.0)
+
+        got_s = held([P, S], U8, "got_s", "slot_f")
+        v_s = held([P, S], U8, "v_s")
+        nc.vector.tensor_copy(got_s[:], tab_s[:].indirect(pick[:]))
+        nc.vector.tensor_copy(v_s[:].bitcast(I32), got_s[:].bitcast(I32))
+        for e in range(2):
+            nc.scalar.dma_start(
+                out=v_s[:].bitcast(I32)[2 + e : P : 32, :],
+                in_=got_s[:].bitcast(I32)[16 + e : P : 32, :],
+            )
+        wa_raw1 = held([P, PACK, KP], F32, "wa_raw1", "slot_a")
+        nc.sync.dma_start(out=wa_raw1[:], in_=wa_rows[:, :, KP : 2 * KP])
+        wa_raw = [wa_raw0, wa_raw1]
+        half = S // 2
+        v_w = [held([P, half], U32, "v_w%d" % u) for u in range(2)]
+        for u in range(2):
+            cols = slice(u * half // 16, (u + 1) * half // 16)
+            nc.vector.tensor_copy(v_w[u][:], tab_w[:].indirect(pick[:, cols]))
+
+        wa_bf = [held([P, KP * PACK], BF16, "wa_bf%d" % b) for b in range(HB)]
+        wa_q = [held([P, KP], U32, "wa_q%d" % b) for b in range(HB)]
+        wa_s = [held([P, KP], U8, "wa_s%d" % b) for b in range(HB)]
+        wd_bf = [held([P, N * PACK], BF16, "wd_bf%d" % b) for b in range(HB)]
+        wd_q = [held([P, N], U32, "wd_q%d" % b) for b in range(HB)]
+        wd_s = [held([P, N], U8, "wd_s%d" % b) for b in range(HB)]
+
+        def prepare_wa(b):
+            dst = wa_bf[b][:].rearrange("p (t m i) -> p m i t", t=PACK, i=PACK)
+            src = wa_raw[b][:].rearrange("p i (m t) -> p m i t", t=PACK)
+            nc.scalar.copy(dst[:, 0:64], src[:, 0:64])
+            nc.vector.tensor_copy(dst[:, 64:128], src[:, 64:128])
+            nc.vector.quantize_mx(
+                out=wa_q[b][:].bitcast(FP8X4), scales=wa_s[b][:], in_=wa_bf[b][:]
+            )
+
+        prepare_wa(0)
+        wb_w = held([P, 2 * H], U8, "wb_w")
+        wb_s = held([P, H], U8, "wb_s")
+        nc.vector.tensor_copy(
+            wb_w[:].bitcast(U16).rearrange("p (b t m) -> p b t m", b=HB, t=PACK),
+            wb_raw[:].bitcast(U16).rearrange("p (b m t) -> p b t m", b=HB, t=PACK),
+        )
+        nc.vector.tensor_copy(
+            wb_s[:].rearrange("p (b t m) -> p b t m", b=HB, t=PACK),
+            wb_s_raw[:].rearrange("p (b m t) -> p b t m", b=HB, t=PACK),
+        )
+        prepare_wa(1)
+
+        wd_raw = [held([P, PACK, N], F32, "wd_raw%d" % b, ("slot_b", "slot_c")[b]) for b in range(HB)]
+        for b in range(HB):
+            nc.sync.dma_start(
+                out=wd_raw[b][:],
+                in_=wd[b * KP : (b + 1) * KP, :].rearrange("(p i) n -> p i n", i=PACK),
+            )
+        late_s = held([P, (1 + HB) * N], U8, "late_s", "slot_f")
+        nc.vector.memset(late_s[:].bitcast(I32), 0)
+        wc_s = late_s[:, 0:N]
+        we_s = late_s[:, N : (1 + HB) * N]
+        wc_w = held([P, N], U32, "wc_w", "wa_bf0")
+        we_w = held([P, HB * 2 * N], U8, "we_w", "slot_e")
+        wg = held([P, S], F32, "wg", "slot_a")
+        load_scale_rows(nc.sync, wc_s, wc_scales)
+        load_scale_rows(nc.sync, we_s, we_scales)
+        nc.sync.dma_start(
+            out=wc_w[:].bitcast(I32),
+            in_=wc_words[0].rearrange("p c i -> p (c i)").bitcast(I32),
+        )
+        nc.sync.dma_start(
+            out=we_w[:].bitcast(I32).rearrange("p (a w) -> p a w", a=HB),
+            in_=we_words.bitcast(I32).rearrange("a p w -> p a w"),
+        )
+        nc.sync.dma_start(out=wg[:], in_=wgo)
+        pages.append(held([P, T2], F32, "page2", "slot_d"))
+        nc.vector.memset(pages[2][:], 0.0)
+
+        def prepare_wd(b):
+            dst = wd_bf[b][:].rearrange("p (c u i) -> p c i u", u=4, i=PACK)
+            src = wd_raw[b][:].rearrange("p i (c u) -> p c i u", u=4)
+            for part in range(2):
+                cols = slice(64 * part, 64 * (part + 1))
+                nc.scalar.activation(dst[:, cols], src[:, cols], ACT.Copy, scale=-1.0)
+            nc.vector.quantize_mx(
+                out=wd_q[b][:].bitcast(FP8X4), scales=wd_s[b][:], in_=wd_bf[b][:]
+            )
+
+        ident = held([P, P], F32, "ident")
+        make_identity(nc, ident[:])
+
+        y = held([P, PACK, S], F32, "y")
+        h_q = [held([P, HB * P], U32, "h_q%d" % j) for j in range(JT)]
+        h_s = [held([P, HB * P], U8, "h_s%d" % j) for j in range(JT)]
+        gate = [held([P, PACK, P], F32, "gate%d" % j) for j in range(JT)]
+
+        def v_cols(j):
+            u, c = divmod(j * P, half)
+            return v_w[u][:, c : c + P].bitcast(FP8X4), v_s[:, j * P : (j + 1) * P]
+
+        def hidden(j):
+            codes, scales = v_cols(j)
+            h_bf = ring.tile([P, HB, P, PACK], BF16, name="h_bf", align_bytes=64)
+            for b in range(HB):
+                a_ps = psum.tile([P, PACK, P], F32, name="a_ps", bufs=2)
+                b_ps = psum.tile([P, PACK, P], F32, name="b_ps", bufs=2)
+                for t in range(PACK):
+                    m = slice(t * P, (t + 1) * P)
+                    nc.tensor.matmul_mx(
+                        out=a_ps[:, t, :], lhsT=wa_q[b][:, m].bitcast(FP8X4), lhsT_scale=wa_s[b][:, m],
+                        rhs=codes, rhs_scale=scales, start=True, stop=True,
+                    )
+                for t in range(PACK):
+                    c0 = b * KP + t * P
+                    nc.tensor.matmul_mx(
+                        out=b_ps[:, t, :], lhsT=wb_w[:, 2 * c0 : 2 * (c0 + P)].bitcast(FP4X4),
+                        lhsT_scale=wb_s[:, c0 : c0 + P],
+                        rhs=codes, rhs_scale=scales, start=True, stop=True,
+                    )
+                act = ring.tile([P, P, PACK], F32, name="act", bufs=3)
+                nc.scalar.activation(act[:], a_ps[:].rearrange("p t j -> p j t"), ACT.Silu)
+                nc.vector.tensor_tensor(
+                    h_bf[:, b], b_ps[:].rearrange("p t j -> p j t"), act[:], ALU.mult
+                )
+            nc.vector.quantize_mx(
+                out=h_q[j][:].bitcast(FP8X4), scales=h_s[j][:],
+                in_=h_bf[:].rearrange("p b j t -> p (b j t)"),
+            )
+
+        def gate_of(j):
+            codes, scales = v_cols(j)
+            c_ps = psum.tile([P, N], F32, name="c_ps")
+            nc.tensor.matmul_mx(
+                out=c_ps[:], lhsT=codes, lhsT_scale=scales,
+                rhs=wc_w[:].bitcast(FP8X4), rhs_scale=wc_s, start=True, stop=True,
+            )
+            nc.scalar.activation(
+                gate[j][:], c_ps[:].rearrange("j (p i) -> j i p", i=PACK), ACT.Tanh, scale=0.5
+            )
+
+        def responses(j):
+            e_ps = psum.tile([P, N], F32, name="e_ps")
+            d_ps = psum.tile([P, N], F32, name="d_ps")
+            for b in range(HB):
+                m = slice(b * P, (b + 1) * P)
+                nc.tensor.matmul_mx(
+                    out=e_ps[:], lhsT=h_q[j][:, m].bitcast(FP8X4), lhsT_scale=h_s[j][:, m],
+                    rhs=we_w[:, 2 * b * N : 2 * (b + 1) * N].bitcast(FP4X4),
+                    rhs_scale=we_s[:, b * N : (b + 1) * N], start=(b == 0), stop=(b == HB - 1),
+                )
+            for b in range(HB):
+                m = slice(b * P, (b + 1) * P)
+                nc.tensor.matmul_mx(
+                    out=d_ps[:], lhsT=h_q[j][:, m].bitcast(FP8X4), lhsT_scale=h_s[j][:, m],
+                    rhs=wd_q[b][:].bitcast(FP8X4), rhs_scale=wd_s[b][:],
+                    start=(b == 0), stop=(b == HB - 1),
+                )
+            e_part = ring.tile([P, PACK, P], F32, name="e_part")
+            d_part = ring.tile([P, PACK, P], F32, name="d_part")
+            nc.vector.scalar_tensor_tensor(
+                e_part[:], gate[j][:], 1.0, e_ps[:].rearrange("j (p i) -> j i p", i=PACK),
+                ALU.subtract, ALU.mult,
+            )
+            nc.vector.scalar_tensor_tensor(
+                d_part[:], gate[j][:], 1.0, d_ps[:].rearrange("j (p i) -> j i p", i=PACK),
+                ALU.add, ALU.mult,
+            )
+            y_ps = psum.tile([P, PACK, P], F32, name="y_ps")
+            for i in range(PACK):
+                nc.tensor.matmul(y_ps[:, i, :], e_part[:, i, :], ident[:], start=True, stop=False, is_transpose=True)
+                nc.tensor.matmul(y_ps[:, i, :], d_part[:, i, :], ident[:], start=False, stop=True, is_transpose=True)
+            nc.scalar.activation(y[:, :, j * P : (j + 1) * P], y_ps[:], ACT.Copy, scale=-0.5)
+
+        out_rows = out.rearrange("(p i) t -> p i t", i=PACK)
+
+        def put(page, i, j0, j1):
+            cols = slice(j0 * P, j1 * P)
+            nc.vector.tensor_tensor(
+                page[:].indirect(place[:, j0 * LIST_COLS : j1 * LIST_COLS]),
+                y[:, i, cols], wg[:, cols], ALU.mult,
+            )
+
+        hidden(0)
+        prepare_wd(0)
+        hidden(1)
+        prepare_wd(1)
+        gate_of(0)
+        for j in range(JT):
+            if j + 2 < JT:
+                hidden(j + 2)
+            if j + 1 < JT:
+                gate_of(j + 1)
+            responses(j)
+            if j > 0:
+                for i in range(2):
+                    put(pages[i], i, j - 1, j)
+        for i in range(2):
+            put(pages[i], i, JT - 1, JT)
+            nc.sync.dma_start(out=out_rows[:, i, :], in_=pages[i][:])
+        put(pages[2], 2, 0, JT)
+        nc.sync.dma_start(out=out_rows[:, 2, :], in_=pages[2][:])
+        put(pages[0], 3, 0, JT)
+        nc.sync.dma_start(out=out_rows[:, 3, :], in_=pages[0][:])

@@ -23,6 +23,7 @@ KP = P * PACK
 HB = H // KP
 JT = S // P
 LIST_COLS = P // 16
+JOINED = (1, 3, 5)
 
 
 def tile_list_sniff_correction_kernel(
@@ -32,91 +33,73 @@ def tile_list_sniff_correction_kernel(
     nc = tc.nc
     with ExitStack() as ctx:
         keep = ctx.enter_context(tc.tile_pool(name="keep", bufs=1))
+        stage = ctx.enter_context(tc.tile_pool(name="stage", bufs=1))
         ring = ctx.enter_context(tc.tile_pool(name="ring", bufs=2))
         psum = ctx.enter_context(tc.psum_pool(name="psum", bufs=1))
 
         def held(shape, dtype, name, tag=None):
             return keep.tile(shape, dtype, name=name, tag=tag or name, align_bytes=64)
 
+        def staged(shape, dtype, name, offset):
+            return stage.tile(shape, dtype, name=name, align_bytes=64, offset=offset)
+
         pick = held([P, S // 16], U16, "pick")
         place = held([P, S // 16], U16, "place")
         tab_w = held([P, T], U32, "tab_w", "slot_b")
         tab_s = held([P, T], U8, "tab_s", "slot_a")
         wb_s_raw = held([P, H], U8, "wb_s_raw", "slot_e")
+        v_s = held([P, S], U8, "v_s")
         warm = held([P, 8], F32, "warm")
         warm_out = held([P, 8], F32, "warm_out")
         pages = [held([P, T2], F32, "page%d" % i) for i in range(2)]
 
-        nc.gpsimd.memset(tab_s[:].bitcast(I32), 0)
-        nc.vector.memset(wb_s_raw[:].bitcast(I32), 0)
         nc.vector.memset(warm[:], 0.0)
+        nc.vector.memset(v_s[:].bitcast(I32), 0)
 
         def load_scale_rows(queue, plane, rows):
             passes = rows.shape[0]
             dst = plane.bitcast(I32).rearrange("p (a w) -> p a w", a=passes)
             src = rows.bitcast(I32)
-            for q in range(4):
-                queue.dma_start(
-                    out=dst[32 * q : 32 * q + 4, :, :],
-                    in_=src[:, 4 * q : 4 * q + 4, :].rearrange("a r w -> r a w"),
-                )
+            for a in range(passes):
+                for r in range(4):
+                    queue.dma_start(
+                        out=dst[r:P:4, a, :],
+                        in_=src[a, r:16:4, :].unsqueeze(1).to_broadcast([4, 8, src.shape[2]]),
+                    )
 
         wa_rows = wa.rearrange("(p i) c -> p i c", i=PACK)
-        wa_raw0 = held([P, PACK, KP], F32, "wa_raw0", "slot_c")
+        wa_raw0 = staged([P, PACK, KP], F32, "wa_raw0", 7680)
         wb_raw = held([P, 2 * H], U8, "wb_raw", "slot_d")
 
         nc.sync.dma_start(pick[:], offs)
         nc.sync.dma_start(
+            out=tab_s[:].bitcast(I32),
+            in_=tab_scales[0].bitcast(I32).unsqueeze(1).to_broadcast([16, 8, T // 4]),
+        )
+        nc.sync.dma_start(out=wa_raw0[:], in_=wa_rows[:, :, 0:KP])
+        nc.sync.dma_start(out=wb_raw[:].bitcast(I32), in_=wb_words[0].bitcast(I32))
+        nc.sync.dma_start(
             out=tab_w[:].bitcast(I32),
             in_=tab_words[0].rearrange("p t i -> p (t i)").bitcast(I32),
         )
-        tab_rows = tab_scales[0].bitcast(I32)
-        for e in range(2):
-            nc.scalar.dma_start(out=tab_s[:].bitcast(I32)[e:P:16, :], in_=tab_rows[e:16:2, :])
+        load_scale_rows(nc.scalar, wb_s_raw[:], wb_scales)
+        wa_raw1 = held([P, PACK, KP], F32, "wa_raw1", "slot_g")
+        nc.sync.dma_start(out=wa_raw1[:], in_=wa_rows[:, :, KP : 2 * KP])
         nc.scalar.activation(warm_out[:], warm[:], ACT.Silu)
-        nc.sync.dma_start(out=wa_raw0[:], in_=wa_rows[:, :, 0:KP])
-        nc.sync.dma_start(out=wb_raw[:].bitcast(I32), in_=wb_words[0].bitcast(I32))
-        load_scale_rows(nc.gpsimd, wb_s_raw[:], wb_scales)
         nc.sync.dma_start(place[:], offs2)
 
         for page in pages:
             nc.vector.memset(page[:], 0.0)
 
         got_s = held([P, S], U8, "got_s", "slot_f")
-        v_s = held([P, S], U8, "v_s")
         nc.vector.tensor_copy(got_s[:], tab_s[:].indirect(pick[:]))
-        nc.vector.tensor_copy(v_s[:].bitcast(I32), got_s[:].bitcast(I32))
-        for e in range(2):
+        for r in range(4):
             nc.scalar.dma_start(
-                out=v_s[:].bitcast(I32)[2 + e : P : 32, :],
-                in_=got_s[:].bitcast(I32)[16 + e : P : 32, :],
+                out=v_s[:].bitcast(I32)[r:P:32, :],
+                in_=got_s[:].bitcast(I32)[8 * r : P : 32, :],
             )
-        wa_raw1 = held([P, PACK, KP], F32, "wa_raw1", "slot_a")
-        nc.sync.dma_start(out=wa_raw1[:], in_=wa_rows[:, :, KP : 2 * KP])
         wa_raw = [wa_raw0, wa_raw1]
-        half = S // 2
-        v_w = [held([P, half], U32, "v_w%d" % u) for u in range(2)]
-        for u in range(2):
-            cols = slice(u * half // 16, (u + 1) * half // 16)
-            nc.vector.tensor_copy(v_w[u][:], tab_w[:].indirect(pick[:, cols]))
 
-        wa_bf = [held([P, KP * PACK], BF16, "wa_bf%d" % b) for b in range(HB)]
-        wa_q = [held([P, KP], U32, "wa_q%d" % b) for b in range(HB)]
-        wa_s = [held([P, KP], U8, "wa_s%d" % b) for b in range(HB)]
-        wd_bf = [held([P, N * PACK], BF16, "wd_bf%d" % b) for b in range(HB)]
-        wd_q = [held([P, N], U32, "wd_q%d" % b) for b in range(HB)]
-        wd_s = [held([P, N], U8, "wd_s%d" % b) for b in range(HB)]
-
-        def prepare_wa(b):
-            dst = wa_bf[b][:].rearrange("p (t m i) -> p m i t", t=PACK, i=PACK)
-            src = wa_raw[b][:].rearrange("p i (m t) -> p m i t", t=PACK)
-            nc.scalar.copy(dst[:, 0:64], src[:, 0:64])
-            nc.vector.tensor_copy(dst[:, 64:128], src[:, 64:128])
-            nc.vector.quantize_mx(
-                out=wa_q[b][:].bitcast(FP8X4), scales=wa_s[b][:], in_=wa_bf[b][:]
-            )
-
-        prepare_wa(0)
         wb_w = held([P, 2 * H], U8, "wb_w")
         wb_s = held([P, H], U8, "wb_s")
         nc.vector.tensor_copy(
@@ -127,41 +110,78 @@ def tile_list_sniff_correction_kernel(
             wb_s[:].rearrange("p (b t m) -> p b t m", b=HB, t=PACK),
             wb_s_raw[:].rearrange("p (b m t) -> p b t m", b=HB, t=PACK),
         )
-        prepare_wa(1)
 
-        wd_raw = [held([P, PACK, N], F32, "wd_raw%d" % b, ("slot_b", "slot_c")[b]) for b in range(HB)]
+        wa_bf = [held([P, KP * PACK], BF16, "wa_bf%d" % b) for b in range(HB)]
+        wa_q = [held([P, KP], U32, "wa_q%d" % b) for b in range(HB)]
+        wa_s = [held([P, KP], U8, "wa_s%d" % b) for b in range(HB)]
+        wd_bf = [held([P, N * PACK], BF16, "wd_bf%d" % b) for b in range(HB)]
+        wd_q = [held([P, N], U32, "wd_q%d" % b) for b in range(HB)]
+        wd_s = [held([P, N], U8, "wd_s%d" % b) for b in range(HB)]
+
+        def prepare_wa(b, share):
+            dst = wa_bf[b][:].rearrange("p (t m i) -> p m i t", t=PACK, i=PACK)
+            src = wa_raw[b][:].rearrange("p i (m t) -> p m i t", t=PACK)
+            nc.scalar.copy(dst[:, 0:share], src[:, 0:share])
+            if share < P:
+                nc.vector.tensor_copy(dst[:, share:P], src[:, share:P])
+            nc.vector.quantize_mx(
+                out=wa_q[b][:].bitcast(FP8X4), scales=wa_s[b][:], in_=wa_bf[b][:]
+            )
+
+        spans = [(0, 2), (2, 4), (4, 8)]
+        v_w = [held([P, (j1 - j0) * P], U32, "v_w%d" % j0) for j0, j1 in spans]
+
+        def gather_words(u):
+            j0, j1 = spans[u]
+            nc.vector.tensor_copy(v_w[u][:], tab_w[:].indirect(pick[:, j0 * LIST_COLS : j1 * LIST_COLS]))
+
+        prepare_wa(0, P)
+        gather_words(0)
+        gather_words(1)
+        gather_words(2)
+        prepare_wa(1, P)
+
+        wc_w = staged([P, N], U32, "wc_w", 8192)
+        we_w = staged([P, HB * 2 * N], U8, "we_w", 10240)
+        nc.sync.dma_start(
+            out=wc_w[:].bitcast(I32),
+            in_=wc_words[0].rearrange("p c i -> p (c i)").bitcast(I32),
+        )
+        wd_raw = [staged([P, PACK, N], F32, "wd_raw%d" % b, (0, 15360)[b]) for b in range(HB)]
         for b in range(HB):
             nc.sync.dma_start(
                 out=wd_raw[b][:],
                 in_=wd[b * KP : (b + 1) * KP, :].rearrange("(p i) n -> p i n", i=PACK),
             )
-        late_s = held([P, (1 + HB) * N], U8, "late_s", "slot_f")
-        nc.vector.memset(late_s[:].bitcast(I32), 0)
+        late_s = staged([P, (1 + HB) * N], U8, "late_s", 12288)
+        nc.gpsimd.memset(late_s[:].bitcast(I32), 0)
         wc_s = late_s[:, 0:N]
         we_s = late_s[:, N : (1 + HB) * N]
-        wc_w = held([P, N], U32, "wc_w", "wa_bf0")
-        we_w = held([P, HB * 2 * N], U8, "we_w", "slot_e")
-        wg = held([P, S], F32, "wg", "slot_a")
-        load_scale_rows(nc.sync, wc_s, wc_scales)
-        load_scale_rows(nc.sync, we_s, we_scales)
-        nc.sync.dma_start(
-            out=wc_w[:].bitcast(I32),
-            in_=wc_words[0].rearrange("p c i -> p (c i)").bitcast(I32),
-        )
+        wg = held([P, S], F32, "wg", "slot_g")
+        for plane, rows in ((wc_s, wc_scales), (we_s, we_scales)):
+            dst = plane.bitcast(I32).rearrange("p (a w) -> p a w", a=rows.shape[0])
+            for q in range(4):
+                nc.sync.dma_start(
+                    out=dst[32 * q : 32 * q + 4, :, :],
+                    in_=rows.bitcast(I32)[:, 4 * q : 4 * q + 4, :].rearrange("a r w -> r a w"),
+                )
         nc.sync.dma_start(
             out=we_w[:].bitcast(I32).rearrange("p (a w) -> p a w", a=HB),
             in_=we_words.bitcast(I32).rearrange("a p w -> p a w"),
         )
         nc.sync.dma_start(out=wg[:], in_=wgo)
-        pages.append(held([P, T2], F32, "page2", "slot_d"))
+        pages.append(held([P, T2], F32, "page2", "wa_bf0"))
         nc.vector.memset(pages[2][:], 0.0)
 
         def prepare_wd(b):
             dst = wd_bf[b][:].rearrange("p (c u i) -> p c i u", u=4, i=PACK)
             src = wd_raw[b][:].rearrange("p i (c u) -> p c i u", u=4)
-            for part in range(2):
-                cols = slice(64 * part, 64 * (part + 1))
-                nc.scalar.activation(dst[:, cols], src[:, cols], ACT.Copy, scale=-1.0)
+            if b == 0:
+                for part in range(2):
+                    cols = slice(64 * part, 64 * (part + 1))
+                    nc.scalar.activation(dst[:, cols], src[:, cols], ACT.Copy, scale=-1.0)
+            else:
+                nc.vector.tensor_scalar(dst, src, -1.0, None, ALU.mult)
             nc.vector.quantize_mx(
                 out=wd_q[b][:].bitcast(FP8X4), scales=wd_s[b][:], in_=wd_bf[b][:]
             )
@@ -170,41 +190,48 @@ def tile_list_sniff_correction_kernel(
         make_identity(nc, ident[:])
 
         y = held([P, PACK, S], F32, "y")
+        h_bf = [held([P, HB, P, PACK], BF16, "h_bf%d" % j) for j in range(JT)]
         h_q = [held([P, HB * P], U32, "h_q%d" % j) for j in range(JT)]
         h_s = [held([P, HB * P], U8, "h_s%d" % j) for j in range(JT)]
         gate = [held([P, PACK, P], F32, "gate%d" % j) for j in range(JT)]
+        pending = {}
 
         def v_cols(j):
-            u, c = divmod(j * P, half)
+            u = [k for k, (j0, j1) in enumerate(spans) if j0 <= j < j1][0]
+            c = (j - spans[u][0]) * P
             return v_w[u][:, c : c + P].bitcast(FP8X4), v_s[:, j * P : (j + 1) * P]
 
-        def hidden(j):
+        def first_products(j, b):
             codes, scales = v_cols(j)
-            h_bf = ring.tile([P, HB, P, PACK], BF16, name="h_bf", align_bytes=64)
-            for b in range(HB):
-                a_ps = psum.tile([P, PACK, P], F32, name="a_ps", bufs=2)
-                b_ps = psum.tile([P, PACK, P], F32, name="b_ps", bufs=2)
-                for t in range(PACK):
-                    m = slice(t * P, (t + 1) * P)
-                    nc.tensor.matmul_mx(
-                        out=a_ps[:, t, :], lhsT=wa_q[b][:, m].bitcast(FP8X4), lhsT_scale=wa_s[b][:, m],
-                        rhs=codes, rhs_scale=scales, start=True, stop=True,
-                    )
-                for t in range(PACK):
-                    c0 = b * KP + t * P
-                    nc.tensor.matmul_mx(
-                        out=b_ps[:, t, :], lhsT=wb_w[:, 2 * c0 : 2 * (c0 + P)].bitcast(FP4X4),
-                        lhsT_scale=wb_s[:, c0 : c0 + P],
-                        rhs=codes, rhs_scale=scales, start=True, stop=True,
-                    )
-                act = ring.tile([P, P, PACK], F32, name="act", bufs=3)
-                nc.scalar.activation(act[:], a_ps[:].rearrange("p t j -> p j t"), ACT.Silu)
-                nc.vector.tensor_tensor(
-                    h_bf[:, b], b_ps[:].rearrange("p t j -> p j t"), act[:], ALU.mult
+            a_ps = psum.tile([P, PACK, P], F32, name="a_ps", bufs=2)
+            b_ps = psum.tile([P, PACK, P], F32, name="b_ps", bufs=2)
+            for t in range(PACK):
+                m = slice(t * P, (t + 1) * P)
+                nc.tensor.matmul_mx(
+                    out=a_ps[:, t, :], lhsT=wa_q[b][:, m].bitcast(FP8X4), lhsT_scale=wa_s[b][:, m],
+                    rhs=codes, rhs_scale=scales, start=True, stop=True,
                 )
+            for t in range(PACK):
+                c0 = b * KP + t * P
+                nc.tensor.matmul_mx(
+                    out=b_ps[:, t, :], lhsT=wb_w[:, 2 * c0 : 2 * (c0 + P)].bitcast(FP4X4),
+                    lhsT_scale=wb_s[:, c0 : c0 + P],
+                    rhs=codes, rhs_scale=scales, start=True, stop=True,
+                )
+            act = ring.tile([P, P, PACK], F32, name="act", bufs=3)
+            nc.scalar.activation(act[:], a_ps[:].rearrange("p t j -> p j t"), ACT.Silu)
+            pending[j, b] = (b_ps, act)
+
+        def hidden(j, b):
+            b_ps, act = pending[j, b]
+            nc.vector.tensor_tensor(
+                h_bf[j][:, b], b_ps[:].rearrange("p t j -> p j t"), act[:], ALU.mult
+            )
+
+        def quantize_hidden(j):
             nc.vector.quantize_mx(
                 out=h_q[j][:].bitcast(FP8X4), scales=h_s[j][:],
-                in_=h_bf[:].rearrange("p b j t -> p (b j t)"),
+                in_=h_bf[j][:].rearrange("p b j t -> p (b j t)"),
             )
 
         def gate_of(j):
@@ -218,29 +245,50 @@ def tile_list_sniff_correction_kernel(
                 gate[j][:], c_ps[:].rearrange("j (p i) -> j i p", i=PACK), ACT.Tanh, scale=0.5
             )
 
-        def responses(j):
-            e_ps = psum.tile([P, N], F32, name="e_ps")
-            d_ps = psum.tile([P, N], F32, name="d_ps")
-            for b in range(HB):
-                m = slice(b * P, (b + 1) * P)
-                nc.tensor.matmul_mx(
-                    out=e_ps[:], lhsT=h_q[j][:, m].bitcast(FP8X4), lhsT_scale=h_s[j][:, m],
-                    rhs=we_w[:, 2 * b * N : 2 * (b + 1) * N].bitcast(FP4X4),
-                    rhs_scale=we_s[:, b * N : (b + 1) * N], start=(b == 0), stop=(b == HB - 1),
-                )
+        def second_products(j):
+            if j % 3 == 0:
+                e_ps = psum.tile([P, N], F32, name="e_ps")
+                d_ps = psum.tile([P, N], F32, name="d_ps")
+            else:
+                e_ps = psum.tile([P, N], F32, name="e_late", tag="a_ps", bufs=2)
+                d_ps = psum.tile([P, N], F32, name="d_late", tag="b_ps", bufs=2)
+
+            def e_passes(bank, first, last):
+                for b in range(HB):
+                    m = slice(b * P, (b + 1) * P)
+                    nc.tensor.matmul_mx(
+                        out=bank[:], lhsT=h_q[j][:, m].bitcast(FP8X4), lhsT_scale=h_s[j][:, m],
+                        rhs=we_w[:, 2 * b * N : 2 * (b + 1) * N].bitcast(FP4X4),
+                        rhs_scale=we_s[:, b * N : (b + 1) * N],
+                        start=(first and b == 0), stop=(last and b == HB - 1),
+                    )
+
+            joined = j in JOINED
+            e_passes(e_ps, True, True)
             for b in range(HB):
                 m = slice(b * P, (b + 1) * P)
                 nc.tensor.matmul_mx(
                     out=d_ps[:], lhsT=h_q[j][:, m].bitcast(FP8X4), lhsT_scale=h_s[j][:, m],
                     rhs=wd_q[b][:].bitcast(FP8X4), rhs_scale=wd_s[b][:],
-                    start=(b == 0), stop=(b == HB - 1),
+                    start=(b == 0), stop=(b == HB - 1 and not joined),
                 )
+            if joined:
+                e_passes(d_ps, False, True)
+            pending[j] = (e_ps, d_ps)
+
+        def interpolate(j):
+            e_ps, d_ps = pending[j]
             e_part = ring.tile([P, PACK, P], F32, name="e_part")
             d_part = ring.tile([P, PACK, P], F32, name="d_part")
-            nc.vector.scalar_tensor_tensor(
-                e_part[:], gate[j][:], 1.0, e_ps[:].rearrange("j (p i) -> j i p", i=PACK),
-                ALU.subtract, ALU.mult,
-            )
+            if j in JOINED:
+                nc.scalar.activation(
+                    e_part[:], e_ps[:].rearrange("j (p i) -> j i p", i=PACK), ACT.Copy, scale=-2.0
+                )
+            else:
+                nc.vector.scalar_tensor_tensor(
+                    e_part[:], gate[j][:], 1.0, e_ps[:].rearrange("j (p i) -> j i p", i=PACK),
+                    ALU.subtract, ALU.mult,
+                )
             nc.vector.scalar_tensor_tensor(
                 d_part[:], gate[j][:], 1.0, d_ps[:].rearrange("j (p i) -> j i p", i=PACK),
                 ALU.add, ALU.mult,
@@ -260,24 +308,40 @@ def tile_list_sniff_correction_kernel(
                 y[:, i, cols], wg[:, cols], ALU.mult,
             )
 
-        hidden(0)
-        prepare_wd(0)
-        hidden(1)
-        prepare_wd(1)
+        LEAD = 3
+        units = [(j, 0) for j in range(LEAD)] + [(j, 1) for j in range(LEAD)]
+        units = units + [(j, b) for j in range(LEAD, JT) for b in range(HB)]
+
+        def advance(k):
+            hidden(*units[k])
+            if k + 2 < len(units):
+                first_products(*units[k + 2])
+
+        first_products(*units[0])
+        first_products(*units[1])
+        for k in range(len(units)):
+            advance(k)
+            if k == 2 * LEAD:
+                prepare_wd(0)
+            if k == 2 * LEAD + 2:
+                prepare_wd(1)
+            if k > 0 and units[k - 1][1] == HB - 1:
+                quantize_hidden(units[k - 1][0])
+        quantize_hidden(JT - 1)
+        pages.append(held([P, T2], F32, "page3", "h_bf%d" % (JT - 1)))
+        nc.gpsimd.memset(pages[3][:], 0.0)
         gate_of(0)
+        second_products(0)
         for j in range(JT):
-            if j + 2 < JT:
-                hidden(j + 2)
             if j + 1 < JT:
                 gate_of(j + 1)
-            responses(j)
+                second_products(j + 1)
+            interpolate(j)
             if j > 0:
-                for i in range(2):
+                for i in range(3):
                     put(pages[i], i, j - 1, j)
-        for i in range(2):
+        for i in range(3):
             put(pages[i], i, JT - 1, JT)
             nc.sync.dma_start(out=out_rows[:, i, :], in_=pages[i][:])
-        put(pages[2], 2, 0, JT)
-        nc.sync.dma_start(out=out_rows[:, 2, :], in_=pages[2][:])
-        put(pages[0], 3, 0, JT)
-        nc.sync.dma_start(out=out_rows[:, 3, :], in_=pages[0][:])
+        put(pages[3], 3, 0, JT)
+        nc.sync.dma_start(out=out_rows[:, 3, :], in_=pages[3][:])

@@ -23,7 +23,8 @@ KP = P * PACK
 HB = H // KP
 JT = S // P
 LIST_COLS = P // 16
-JOINED = (1, 3, 5)
+JOINED = (3, 5, 6)
+EARLY = 2
 
 
 def tile_list_sniff_correction_kernel(
@@ -49,8 +50,8 @@ def tile_list_sniff_correction_kernel(
         tab_s = held([P, T], U8, "tab_s", "slot_a")
         wb_s_raw = held([P, H], U8, "wb_s_raw", "slot_e")
         v_s = held([P, S], U8, "v_s")
-        warm = held([P, 8], F32, "warm")
-        warm_out = held([P, 8], F32, "warm_out")
+        warm = staged([P, 32], F32, "warm", 32768 - 64)
+        warm_out = held([P, 32], F32, "warm_out")
         pages = [held([P, T2], F32, "page%d" % i) for i in range(2)]
 
         nc.vector.memset(warm[:], 0.0)
@@ -76,28 +77,42 @@ def tile_list_sniff_correction_kernel(
             out=tab_s[:].bitcast(I32),
             in_=tab_scales[0].bitcast(I32).unsqueeze(1).to_broadcast([16, 8, T // 4]),
         )
+        load_scale_rows(nc.sync, wb_s_raw[:], wb_scales)
         nc.sync.dma_start(out=wa_raw0[:], in_=wa_rows[:, :, 0:KP])
         nc.sync.dma_start(out=wb_raw[:].bitcast(I32), in_=wb_words[0].bitcast(I32))
         nc.sync.dma_start(
             out=tab_w[:].bitcast(I32),
             in_=tab_words[0].rearrange("p t i -> p (t i)").bitcast(I32),
         )
-        load_scale_rows(nc.scalar, wb_s_raw[:], wb_scales)
-        wa_raw1 = held([P, PACK, KP], F32, "wa_raw1", "slot_g")
-        nc.sync.dma_start(out=wa_raw1[:], in_=wa_rows[:, :, KP : 2 * KP])
         nc.scalar.activation(warm_out[:], warm[:], ACT.Silu)
         nc.sync.dma_start(place[:], offs2)
 
         for page in pages:
-            nc.vector.memset(page[:], 0.0)
+            nc.vector.memset(page[:].bitcast(I32), 0)
+
+        pages.append(staged([P, T2], F32, "page2", 24576))
+        nc.gpsimd.memset(pages[2][:].bitcast(I32), 0)
+        late_s = staged([P, (1 + HB) * N], U8, "late_s", 32768)
+        nc.gpsimd.memset(late_s[:].bitcast(I32), 0)
+        wc_s = late_s[:, 0:N]
+        we_s = late_s[:, N : (1 + HB) * N]
+        for plane, rows in ((wc_s, wc_scales), (we_s, we_scales)):
+            dst = plane.bitcast(I32).rearrange("p (a w) -> p a w", a=rows.shape[0])
+            for q in range(4):
+                nc.gpsimd.dma_start(
+                    out=dst[32 * q : 32 * q + 4, :, :],
+                    in_=rows.bitcast(I32)[:, 4 * q : 4 * q + 4, :].rearrange("a r w -> r a w"),
+                )
 
         got_s = held([P, S], U8, "got_s", "slot_f")
         nc.vector.tensor_copy(got_s[:], tab_s[:].indirect(pick[:]))
         for r in range(4):
-            nc.scalar.dma_start(
+            nc.sync.dma_start(
                 out=v_s[:].bitcast(I32)[r:P:32, :],
                 in_=got_s[:].bitcast(I32)[8 * r : P : 32, :],
             )
+        wa_raw1 = held([P, PACK, KP], F32, "wa_raw1", "slot_a")
+        nc.sync.dma_start(out=wa_raw1[:], in_=wa_rows[:, :, KP : 2 * KP])
         wa_raw = [wa_raw0, wa_raw1]
 
         wb_w = held([P, 2 * H], U8, "wb_w")
@@ -121,9 +136,11 @@ def tile_list_sniff_correction_kernel(
         def prepare_wa(b, share):
             dst = wa_bf[b][:].rearrange("p (t m i) -> p m i t", t=PACK, i=PACK)
             src = wa_raw[b][:].rearrange("p i (m t) -> p m i t", t=PACK)
-            nc.scalar.copy(dst[:, 0:share], src[:, 0:share])
-            if share < P:
-                nc.vector.tensor_copy(dst[:, share:P], src[:, share:P])
+            cut = P if b not in (0, 1) else 64
+            for m0 in range(0, cut, min(share, cut)):
+                nc.scalar.copy(dst[:, m0 : m0 + min(share, cut)], src[:, m0 : m0 + min(share, cut)])
+            if cut < P:
+                nc.vector.tensor_copy(dst[:, cut:P], src[:, cut:P])
             nc.vector.quantize_mx(
                 out=wa_q[b][:].bitcast(FP8X4), scales=wa_s[b][:], in_=wa_bf[b][:]
             )
@@ -139,7 +156,6 @@ def tile_list_sniff_correction_kernel(
         gather_words(0)
         gather_words(1)
         gather_words(2)
-        prepare_wa(1, P)
 
         wc_w = staged([P, N], U32, "wc_w", 8192)
         we_w = staged([P, HB * 2 * N], U8, "we_w", 10240)
@@ -153,35 +169,27 @@ def tile_list_sniff_correction_kernel(
                 out=wd_raw[b][:],
                 in_=wd[b * KP : (b + 1) * KP, :].rearrange("(p i) n -> p i n", i=PACK),
             )
-        late_s = staged([P, (1 + HB) * N], U8, "late_s", 12288)
-        nc.gpsimd.memset(late_s[:].bitcast(I32), 0)
-        wc_s = late_s[:, 0:N]
-        we_s = late_s[:, N : (1 + HB) * N]
-        wg = held([P, S], F32, "wg", "slot_g")
-        for plane, rows in ((wc_s, wc_scales), (we_s, we_scales)):
-            dst = plane.bitcast(I32).rearrange("p (a w) -> p a w", a=rows.shape[0])
-            for q in range(4):
-                nc.sync.dma_start(
-                    out=dst[32 * q : 32 * q + 4, :, :],
-                    in_=rows.bitcast(I32)[:, 4 * q : 4 * q + 4, :].rearrange("a r w -> r a w"),
-                )
+        wg = held([P, S], F32, "wg", "slot_a")
         nc.sync.dma_start(
             out=we_w[:].bitcast(I32).rearrange("p (a w) -> p a w", a=HB),
             in_=we_words.bitcast(I32).rearrange("a p w -> p a w"),
         )
         nc.sync.dma_start(out=wg[:], in_=wgo)
-        pages.append(held([P, T2], F32, "page2", "wa_bf0"))
-        nc.vector.memset(pages[2][:], 0.0)
 
         def prepare_wd(b):
             dst = wd_bf[b][:].rearrange("p (c u i) -> p c i u", u=4, i=PACK)
             src = wd_raw[b][:].rearrange("p i (c u) -> p c i u", u=4)
-            if b == 0:
-                for part in range(2):
-                    cols = slice(64 * part, 64 * (part + 1))
-                    nc.scalar.activation(dst[:, cols], src[:, cols], ACT.Copy, scale=-1.0)
-            else:
+            who = "VA"[b]
+            if who == "V":
                 nc.vector.tensor_scalar(dst, src, -1.0, None, ALU.mult)
+            elif who == "A":
+                for c0 in range(0, P, 32):
+                    nc.scalar.activation(dst[:, c0 : c0 + 32], src[:, c0 : c0 + 32], ACT.Copy, scale=-1.0)
+            else:
+                gd = wd_bf[b][:].rearrange("p (c i) -> p c i", i=PACK)
+                gs = wd_raw[b][:].rearrange("p i c -> p c i")
+                for c0 in range(0, N, P):
+                    nc.gpsimd.tensor_scalar(gd[:, c0 : c0 + P], gs[:, c0 : c0 + P], -1.0, 0.0, ALU.mult, ALU.add)
             nc.vector.quantize_mx(
                 out=wd_q[b][:].bitcast(FP8X4), scales=wd_s[b][:], in_=wd_bf[b][:]
             )
@@ -193,7 +201,7 @@ def tile_list_sniff_correction_kernel(
         h_bf = [held([P, HB, P, PACK], BF16, "h_bf%d" % j) for j in range(JT)]
         h_q = [held([P, HB * P], U32, "h_q%d" % j) for j in range(JT)]
         h_s = [held([P, HB * P], U8, "h_s%d" % j) for j in range(JT)]
-        gate = [held([P, PACK, P], F32, "gate%d" % j) for j in range(JT)]
+        gate = {}
         pending = {}
 
         def v_cols(j):
@@ -237,6 +245,7 @@ def tile_list_sniff_correction_kernel(
         def gate_of(j):
             codes, scales = v_cols(j)
             c_ps = psum.tile([P, N], F32, name="c_ps")
+            gate[j] = ring.tile([P, PACK, P], F32, name="gate")
             nc.tensor.matmul_mx(
                 out=c_ps[:], lhsT=codes, lhsT_scale=scales,
                 rhs=wc_w[:].bitcast(FP8X4), rhs_scale=wc_s, start=True, stop=True,
@@ -246,7 +255,7 @@ def tile_list_sniff_correction_kernel(
             )
 
         def second_products(j):
-            if j % 3 == 0:
+            if j <= EARLY or (j - EARLY) % 3 == 0:
                 e_ps = psum.tile([P, N], F32, name="e_ps")
                 d_ps = psum.tile([P, N], F32, name="d_ps")
             else:
@@ -308,7 +317,7 @@ def tile_list_sniff_correction_kernel(
                 y[:, i, cols], wg[:, cols], ALU.mult,
             )
 
-        LEAD = 3
+        LEAD = 5
         units = [(j, 0) for j in range(LEAD)] + [(j, 1) for j in range(LEAD)]
         units = units + [(j, b) for j in range(LEAD, JT) for b in range(HB)]
 
@@ -317,30 +326,40 @@ def tile_list_sniff_correction_kernel(
             if k + 2 < len(units):
                 first_products(*units[k + 2])
 
-        first_products(*units[0])
-        first_products(*units[1])
-        for k in range(len(units)):
-            advance(k)
-            if k == 2 * LEAD:
-                prepare_wd(0)
-            if k == 2 * LEAD + 2:
-                prepare_wd(1)
-            if k > 0 and units[k - 1][1] == HB - 1:
-                quantize_hidden(units[k - 1][0])
-        quantize_hidden(JT - 1)
-        pages.append(held([P, T2], F32, "page3", "h_bf%d" % (JT - 1)))
-        nc.gpsimd.memset(pages[3][:], 0.0)
-        gate_of(0)
-        second_products(0)
-        for j in range(JT):
+        def second_stage(j):
             if j + 1 < JT:
                 gate_of(j + 1)
-                second_products(j + 1)
+                if j >= EARLY:
+                    second_products(j + 1)
             interpolate(j)
+            if j < EARLY:
+                second_products(j + 1)
             if j > 0:
-                for i in range(3):
+                for i in range(PACK - 1):
                     put(pages[i], i, j - 1, j)
-        for i in range(3):
+
+        first_products(*units[0])
+        first_products(*units[1])
+        prepare_wa(1, 32)
+        start = len(units) - 2 * EARLY
+        for k in range(len(units)):
+            advance(k)
+            if k == 6:
+                prepare_wd(0)
+            if k == 8:
+                prepare_wd(1)
+                gate_of(0)
+                second_products(0)
+            if k > 0 and units[k - 1][1] == HB - 1:
+                quantize_hidden(units[k - 1][0])
+            if k >= start and (k - start) % 2 == 1:
+                second_stage((k - start) // 2)
+        quantize_hidden(JT - 1)
+        pages.append(held([P, T2], F32, "page3", "h_bf%d" % (JT - 1)))
+        nc.gpsimd.memset(pages[3][:].bitcast(I32), 0)
+        for j in range(EARLY, JT):
+            second_stage(j)
+        for i in range(PACK - 1):
             put(pages[i], i, JT - 1, JT)
             nc.sync.dma_start(out=out_rows[:, i, :], in_=pages[i][:])
         put(pages[3], 3, 0, JT)

@@ -25,6 +25,7 @@ JT = S // P
 LIST_COLS = P // 16
 JOINED = (3, 5, 6)
 EARLY = 2
+SHIFT = 14
 
 
 def tile_list_sniff_correction_kernel(
@@ -46,74 +47,62 @@ def tile_list_sniff_correction_kernel(
 
         pick = held([P, S // 16], U16, "pick")
         place = held([P, S // 16], U16, "place")
-        tab_w = held([P, T], U32, "tab_w", "slot_b")
-        tab_s = held([P, T], U8, "tab_s", "slot_a")
-        wb_s_raw = held([P, H], U8, "wb_s_raw", "slot_e")
+        tab_w = staged([P, T], U32, "tab_w", 65536)
+        tab_s = staged([P, T], U8, "tab_s", 16384)
+        wb_s_raw = held([P, H], U8, "wb_s_raw")
+        wb_raw = held([P, 2 * H], U8, "wb_raw")
         v_s = held([P, S], U8, "v_s")
-        warm = staged([P, 32], F32, "warm", 32768 - 64)
+        got_s = held([P, S], U8, "got_s")
+        warm = held([P, 32], F32, "warm")
         warm_out = held([P, 32], F32, "warm_out")
         pages = [held([P, T2], F32, "page%d" % i) for i in range(2)]
 
-        nc.vector.memset(warm[:], 0.0)
-        nc.vector.memset(v_s[:].bitcast(I32), 0)
+        nc.gpsimd.memset(warm[:], 0.0)
+        nc.gpsimd.memset(v_s[:].bitcast(I32), 0)
 
-        def load_scale_rows(queue, plane, rows):
-            passes = rows.shape[0]
-            dst = plane.bitcast(I32).rearrange("p (a w) -> p a w", a=passes)
+        def load_scale_rows(plane, rows, shift):
+            dst = plane.bitcast(I32)
             src = rows.bitcast(I32)
-            for a in range(passes):
-                for r in range(4):
-                    queue.dma_start(
-                        out=dst[r:P:4, a, :],
-                        in_=src[a, r:16:4, :].unsqueeze(1).to_broadcast([4, 8, src.shape[2]]),
-                    )
+            for r in range(4):
+                nc.sync.dma_start(
+                    out=dst[(r + shift) % 4 : P : 4, :],
+                    in_=src[r:16:4, :].unsqueeze(1).to_broadcast([4, 8, src.shape[1]]),
+                )
 
         wa_rows = wa.rearrange("(p i) c -> p i c", i=PACK)
-        wa_raw0 = staged([P, PACK, KP], F32, "wa_raw0", 7680)
-        wb_raw = held([P, 2 * H], U8, "wb_raw", "slot_d")
+        HALF = KP // 2
+        wa_raw0 = [staged([P, PACK, HALF], F32, "wa_raw0%d" % u, 40960 + 4096 * u) for u in range(2)]
 
         nc.sync.dma_start(pick[:], offs)
-        nc.sync.dma_start(
-            out=tab_s[:].bitcast(I32),
-            in_=tab_scales[0].bitcast(I32).unsqueeze(1).to_broadcast([16, 8, T // 4]),
-        )
-        load_scale_rows(nc.sync, wb_s_raw[:], wb_scales)
-        nc.sync.dma_start(out=wa_raw0[:], in_=wa_rows[:, :, 0:KP])
+        load_scale_rows(tab_s[:], tab_scales[0], SHIFT)
+        for u in range(2):
+            nc.sync.dma_start(out=wa_raw0[u][:], in_=wa_rows[:, :, u * HALF : (u + 1) * HALF])
         nc.sync.dma_start(out=wb_raw[:].bitcast(I32), in_=wb_words[0].bitcast(I32))
+        load_scale_rows(wb_s_raw[:], wb_scales[0], 0)
         nc.sync.dma_start(
             out=tab_w[:].bitcast(I32),
             in_=tab_words[0].rearrange("p t i -> p (t i)").bitcast(I32),
         )
-        nc.scalar.activation(warm_out[:], warm[:], ACT.Silu)
         nc.sync.dma_start(place[:], offs2)
+        nc.scalar.activation(warm_out[:], warm[:], ACT.Silu)
 
         for page in pages:
             nc.vector.memset(page[:].bitcast(I32), 0)
 
-        pages.append(staged([P, T2], F32, "page2", 24576))
-        nc.gpsimd.memset(pages[2][:].bitcast(I32), 0)
-        late_s = staged([P, (1 + HB) * N], U8, "late_s", 32768)
-        nc.gpsimd.memset(late_s[:].bitcast(I32), 0)
-        wc_s = late_s[:, 0:N]
-        we_s = late_s[:, N : (1 + HB) * N]
-        for plane, rows in ((wc_s, wc_scales), (we_s, we_scales)):
-            dst = plane.bitcast(I32).rearrange("p (a w) -> p a w", a=rows.shape[0])
-            for q in range(4):
-                nc.gpsimd.dma_start(
-                    out=dst[32 * q : 32 * q + 4, :, :],
-                    in_=rows.bitcast(I32)[:, 4 * q : 4 * q + 4, :].rearrange("a r w -> r a w"),
-                )
-
-        got_s = held([P, S], U8, "got_s", "slot_f")
         nc.vector.tensor_copy(got_s[:], tab_s[:].indirect(pick[:]))
-        for r in range(4):
-            nc.sync.dma_start(
-                out=v_s[:].bitcast(I32)[r:P:32, :],
-                in_=got_s[:].bitcast(I32)[8 * r : P : 32, :],
-            )
-        wa_raw1 = held([P, PACK, KP], F32, "wa_raw1", "slot_a")
+        nc.sync.dma_start(
+            out=v_s[:].bitcast(I32)[0 : P - SHIFT, :], in_=got_s[:].bitcast(I32)[SHIFT:P, :]
+        )
+        wa_raw1 = staged([P, PACK, KP], F32, "wa_raw1", 8448)
         nc.sync.dma_start(out=wa_raw1[:], in_=wa_rows[:, :, KP : 2 * KP])
-        wa_raw = [wa_raw0, wa_raw1]
+        we_plane = staged([P, HB * N], U8, "we_plane", 16640)
+        we_s = we_plane[:]
+        nc.vector.memset(we_s.bitcast(I32), 0)
+        for q in range(4):
+            nc.sync.dma_start(
+                out=we_s.bitcast(I32).rearrange("p (a w) -> p a w", a=HB)[32 * q : 32 * q + 4, :, :],
+                in_=we_scales.bitcast(I32)[:, 4 * q : 4 * q + 4, :].rearrange("a r w -> r a w"),
+            )
 
         wb_w = held([P, 2 * H], U8, "wb_w")
         wb_s = held([P, H], U8, "wb_s")
@@ -133,14 +122,15 @@ def tile_list_sniff_correction_kernel(
         wd_q = [held([P, N], U32, "wd_q%d" % b) for b in range(HB)]
         wd_s = [held([P, N], U8, "wd_s%d" % b) for b in range(HB)]
 
-        def prepare_wa(b, share):
-            dst = wa_bf[b][:].rearrange("p (t m i) -> p m i t", t=PACK, i=PACK)
-            src = wa_raw[b][:].rearrange("p i (m t) -> p m i t", t=PACK)
-            cut = P if b not in (0, 1) else 64
-            for m0 in range(0, cut, min(share, cut)):
-                nc.scalar.copy(dst[:, m0 : m0 + min(share, cut)], src[:, m0 : m0 + min(share, cut)])
-            if cut < P:
-                nc.vector.tensor_copy(dst[:, cut:P], src[:, cut:P])
+        def round_wa(b, engine, raw, m0, m1):
+            dst = wa_bf[b][:].rearrange("p (t m i) -> p m i t", t=PACK, i=PACK)[:, m0:m1]
+            src = raw.rearrange("p i (m t) -> p m i t", t=PACK)
+            if engine == "A":
+                nc.scalar.copy(dst, src)
+            else:
+                nc.vector.tensor_copy(dst, src)
+
+        def quantize_wa(b):
             nc.vector.quantize_mx(
                 out=wa_q[b][:].bitcast(FP8X4), scales=wa_s[b][:], in_=wa_bf[b][:]
             )
@@ -152,50 +142,59 @@ def tile_list_sniff_correction_kernel(
             j0, j1 = spans[u]
             nc.vector.tensor_copy(v_w[u][:], tab_w[:].indirect(pick[:, j0 * LIST_COLS : j1 * LIST_COLS]))
 
-        prepare_wa(0, P)
+        for u in range(2):
+            round_wa(0, "A", wa_raw0[u][:], 64 * u, 64 * (u + 1))
         gather_words(0)
+        quantize_wa(0)
         gather_words(1)
         gather_words(2)
 
-        wc_w = staged([P, N], U32, "wc_w", 8192)
-        we_w = staged([P, HB * 2 * N], U8, "we_w", 10240)
-        nc.sync.dma_start(
-            out=wc_w[:].bitcast(I32),
-            in_=wc_words[0].rearrange("p c i -> p (c i)").bitcast(I32),
-        )
-        wd_raw = [staged([P, PACK, N], F32, "wd_raw%d" % b, (0, 15360)[b]) for b in range(HB)]
-        for b in range(HB):
+        wd_raw = [staged([P, PACK, N], F32, "wd_raw%d" % b, (33024, 48896)[b]) for b in range(HB)]
+        we_w = staged([P, HB * 2 * N], U8, "we_w", 43264)
+        wc_plane = staged([P, N], U8, "wc_plane", 46336)
+        wc_s = wc_plane[:]
+        wc_w = staged([P, N], U32, "wc_w", 46848)
+        wg = staged([P, S], F32, "wg", 8448)
+
+        def load_wd(b):
             nc.sync.dma_start(
                 out=wd_raw[b][:],
                 in_=wd[b * KP : (b + 1) * KP, :].rearrange("(p i) n -> p i n", i=PACK),
             )
-        wg = held([P, S], F32, "wg", "slot_a")
+
+        load_wd(0)
+        load_wd(1)
+        load_scale_rows(wc_s, wc_scales[0], 0)
+        nc.sync.dma_start(
+            out=wc_w[:].bitcast(I32),
+            in_=wc_words[0].rearrange("p c i -> p (c i)").bitcast(I32),
+        )
         nc.sync.dma_start(
             out=we_w[:].bitcast(I32).rearrange("p (a w) -> p a w", a=HB),
             in_=we_words.bitcast(I32).rearrange("a p w -> p a w"),
         )
-        nc.sync.dma_start(out=wg[:], in_=wgo)
+        ident = staged([P, P], F32, "ident", 33024)
+        pages.append(staged([P, T2], F32, "page2", 65536))
+        pages.append(staged([P, T2], F32, "page3", 49152))
+
+        def clear(page):
+            for c0 in range(0, T2, KP):
+                nc.gpsimd.memset(page[:, c0 : c0 + KP].bitcast(I32), 0)
 
         def prepare_wd(b):
-            dst = wd_bf[b][:].rearrange("p (c u i) -> p c i u", u=4, i=PACK)
-            src = wd_raw[b][:].rearrange("p i (c u) -> p c i u", u=4)
-            who = "VA"[b]
-            if who == "V":
-                nc.vector.tensor_scalar(dst, src, -1.0, None, ALU.mult)
-            elif who == "A":
+            if b == 0:
+                dst = wd_bf[b][:].rearrange("p (c i) -> p c i", i=PACK)
+                src = wd_raw[b][:].rearrange("p i c -> p c i")
+                for c0 in range(0, N, P):
+                    nc.gpsimd.tensor_scalar(dst[:, c0 : c0 + P], src[:, c0 : c0 + P], -1.0, 0.0, ALU.mult, ALU.add)
+            else:
+                dst = wd_bf[b][:].rearrange("p (c u i) -> p c i u", u=4, i=PACK)
+                src = wd_raw[b][:].rearrange("p i (c u) -> p c i u", u=4)
                 for c0 in range(0, P, 32):
                     nc.scalar.activation(dst[:, c0 : c0 + 32], src[:, c0 : c0 + 32], ACT.Copy, scale=-1.0)
-            else:
-                gd = wd_bf[b][:].rearrange("p (c i) -> p c i", i=PACK)
-                gs = wd_raw[b][:].rearrange("p i c -> p c i")
-                for c0 in range(0, N, P):
-                    nc.gpsimd.tensor_scalar(gd[:, c0 : c0 + P], gs[:, c0 : c0 + P], -1.0, 0.0, ALU.mult, ALU.add)
             nc.vector.quantize_mx(
                 out=wd_q[b][:].bitcast(FP8X4), scales=wd_s[b][:], in_=wd_bf[b][:]
             )
-
-        ident = held([P, P], F32, "ident")
-        make_identity(nc, ident[:])
 
         y = held([P, PACK, S], F32, "y")
         h_bf = [held([P, HB, P, PACK], BF16, "h_bf%d" % j) for j in range(JT)]
@@ -317,7 +316,7 @@ def tile_list_sniff_correction_kernel(
                 y[:, i, cols], wg[:, cols], ALU.mult,
             )
 
-        LEAD = 5
+        LEAD = 6
         units = [(j, 0) for j in range(LEAD)] + [(j, 1) for j in range(LEAD)]
         units = units + [(j, b) for j in range(LEAD, JT) for b in range(HB)]
 
@@ -340,7 +339,11 @@ def tile_list_sniff_correction_kernel(
 
         first_products(*units[0])
         first_products(*units[1])
-        prepare_wa(1, 32)
+        for m0 in range(0, 64, 32):
+            round_wa(1, "A", wa_raw1[:, :, 4 * m0 : 4 * (m0 + 32)], m0, m0 + 32)
+        round_wa(1, "V", wa_raw1[:, :, HALF:KP], 64, P)
+        quantize_wa(1)
+        nc.sync.dma_start(out=wg[:], in_=wgo)
         start = len(units) - 2 * EARLY
         for k in range(len(units)):
             advance(k)
@@ -348,6 +351,9 @@ def tile_list_sniff_correction_kernel(
                 prepare_wd(0)
             if k == 8:
                 prepare_wd(1)
+                make_identity(nc, ident[:])
+                clear(pages[2])
+                clear(pages[3])
                 gate_of(0)
                 second_products(0)
             if k > 0 and units[k - 1][1] == HB - 1:
@@ -355,8 +361,6 @@ def tile_list_sniff_correction_kernel(
             if k >= start and (k - start) % 2 == 1:
                 second_stage((k - start) // 2)
         quantize_hidden(JT - 1)
-        pages.append(held([P, T2], F32, "page3", "h_bf%d" % (JT - 1)))
-        nc.gpsimd.memset(pages[3][:].bitcast(I32), 0)
         for j in range(EARLY, JT):
             second_stage(j)
         for i in range(PACK - 1):

@@ -25,6 +25,9 @@ JT = S // P
 LIST_COLS = P // 16
 JOINED = (3, 5, 6)
 EARLY = 2
+WD_ON_VECTOR = (64, 0)
+WD_AT = (6, 8)
+SECOND_AT = 8
 SHIFT = 14
 
 
@@ -47,18 +50,16 @@ def tile_list_sniff_correction_kernel(
 
         pick = held([P, S // 16], U16, "pick")
         place = held([P, S // 16], U16, "place")
-        tab_w = staged([P, T], U32, "tab_w", 65536)
         tab_s = staged([P, T], U8, "tab_s", 16384)
         wb_s_raw = held([P, H], U8, "wb_s_raw")
         wb_raw = held([P, 2 * H], U8, "wb_raw")
         v_s = held([P, S], U8, "v_s")
         got_s = held([P, S], U8, "got_s")
-        warm = held([P, 32], F32, "warm")
         warm_out = held([P, 32], F32, "warm_out")
-        pages = [held([P, T2], F32, "page%d" % i) for i in range(2)]
+        pages = [held([P, T2], F32, "page%d" % i) for i in range(PACK)]
 
-        nc.gpsimd.memset(warm[:], 0.0)
-        nc.gpsimd.memset(v_s[:].bitcast(I32), 0)
+        ident = held([P, P], F32, "ident")
+        make_identity(nc, ident[:])
 
         def load_scale_rows(plane, rows, shift):
             dst = plane.bitcast(I32)
@@ -71,39 +72,36 @@ def tile_list_sniff_correction_kernel(
 
         wa_rows = wa.rearrange("(p i) c -> p i c", i=PACK)
         HALF = KP // 2
-        wa_raw0 = [staged([P, PACK, HALF], F32, "wa_raw0%d" % u, 40960 + 4096 * u) for u in range(2)]
+        wa_raw = [staged([P, PACK, HALF], F32, "wa_raw%d" % u, 36864 + 4096 * u) for u in range(1, 3)]
+        wa_raw = [held([P, PACK, HALF], F32, "wa_raw0")] + wa_raw
 
         nc.sync.dma_start(pick[:], offs)
         load_scale_rows(tab_s[:], tab_scales[0], SHIFT)
-        for u in range(2):
-            nc.sync.dma_start(out=wa_raw0[u][:], in_=wa_rows[:, :, u * HALF : (u + 1) * HALF])
+        def load_wa(u):
+            nc.sync.dma_start(out=wa_raw[u][:], in_=wa_rows[:, :, u * HALF : (u + 1) * HALF])
+
+        load_wa(0)
+        load_wa(1)
         nc.sync.dma_start(out=wb_raw[:].bitcast(I32), in_=wb_words[0].bitcast(I32))
         load_scale_rows(wb_s_raw[:], wb_scales[0], 0)
+        load_wa(2)
+        tab_w = held([P, T], U32, "tab_w")
         nc.sync.dma_start(
             out=tab_w[:].bitcast(I32),
             in_=tab_words[0].rearrange("p t i -> p (t i)").bitcast(I32),
         )
         nc.sync.dma_start(place[:], offs2)
-        nc.scalar.activation(warm_out[:], warm[:], ACT.Silu)
+        nc.scalar.activation(warm_out[:], ident[:, 0:32], ACT.Silu)
 
-        for page in pages:
+        for page in pages[0:2]:
             nc.vector.memset(page[:].bitcast(I32), 0)
 
         nc.vector.tensor_copy(got_s[:], tab_s[:].indirect(pick[:]))
         nc.sync.dma_start(
             out=v_s[:].bitcast(I32)[0 : P - SHIFT, :], in_=got_s[:].bitcast(I32)[SHIFT:P, :]
         )
-        wa_raw1 = staged([P, PACK, KP], F32, "wa_raw1", 8448)
-        nc.sync.dma_start(out=wa_raw1[:], in_=wa_rows[:, :, KP : 2 * KP])
-        we_plane = staged([P, HB * N], U8, "we_plane", 16640)
-        we_s = we_plane[:]
-        nc.vector.memset(we_s.bitcast(I32), 0)
-        for q in range(4):
-            nc.sync.dma_start(
-                out=we_s.bitcast(I32).rearrange("p (a w) -> p a w", a=HB)[32 * q : 32 * q + 4, :, :],
-                in_=we_scales.bitcast(I32)[:, 4 * q : 4 * q + 4, :].rearrange("a r w -> r a w"),
-            )
-
+        wa_raw.append(staged([P, PACK, HALF], F32, "wa_raw3", 12544))
+        load_wa(3)
         wb_w = held([P, 2 * H], U8, "wb_w")
         wb_s = held([P, H], U8, "wb_s")
         nc.vector.tensor_copy(
@@ -142,11 +140,15 @@ def tile_list_sniff_correction_kernel(
             j0, j1 = spans[u]
             nc.vector.tensor_copy(v_w[u][:], tab_w[:].indirect(pick[:, j0 * LIST_COLS : j1 * LIST_COLS]))
 
-        for u in range(2):
-            round_wa(0, "A", wa_raw0[u][:], 64 * u, 64 * (u + 1))
-        gather_words(0)
+        for u in range(3):
+            round_wa(u // 2, "A", wa_raw[u][:], 64 * (u % 2), 64 * (u % 2 + 1))
         quantize_wa(0)
+        gather_words(0)
+        round_wa(1, "A", wa_raw[3][:], 64, P)
+        quantize_wa(1)
         gather_words(1)
+        for page in pages[2:]:
+            nc.vector.memset(page[:].bitcast(I32), 0)
         gather_words(2)
 
         wd_raw = [staged([P, PACK, N], F32, "wd_raw%d" % b, (33024, 48896)[b]) for b in range(HB)]
@@ -154,7 +156,7 @@ def tile_list_sniff_correction_kernel(
         wc_plane = staged([P, N], U8, "wc_plane", 46336)
         wc_s = wc_plane[:]
         wc_w = staged([P, N], U32, "wc_w", 46848)
-        wg = staged([P, S], F32, "wg", 8448)
+        wg = staged([P, S], F32, "wg", 12544)
 
         def load_wd(b):
             nc.sync.dma_start(
@@ -163,6 +165,14 @@ def tile_list_sniff_correction_kernel(
             )
 
         load_wd(0)
+        we_plane = staged([P, HB * N], U8, "we_plane", 41216)
+        we_s = we_plane[:]
+        nc.vector.memset(we_s.bitcast(I32), 0)
+        for q in range(4):
+            nc.sync.dma_start(
+                out=we_s.bitcast(I32).rearrange("p (a w) -> p a w", a=HB)[32 * q : 32 * q + 4, :, :],
+                in_=we_scales.bitcast(I32)[:, 4 * q : 4 * q + 4, :].rearrange("a r w -> r a w"),
+            )
         load_wd(1)
         load_scale_rows(wc_s, wc_scales[0], 0)
         nc.sync.dma_start(
@@ -173,25 +183,15 @@ def tile_list_sniff_correction_kernel(
             out=we_w[:].bitcast(I32).rearrange("p (a w) -> p a w", a=HB),
             in_=we_words.bitcast(I32).rearrange("a p w -> p a w"),
         )
-        ident = staged([P, P], F32, "ident", 33024)
-        pages.append(staged([P, T2], F32, "page2", 65536))
-        pages.append(staged([P, T2], F32, "page3", 49152))
-
-        def clear(page):
-            for c0 in range(0, T2, KP):
-                nc.gpsimd.memset(page[:, c0 : c0 + KP].bitcast(I32), 0)
 
         def prepare_wd(b):
-            if b == 0:
-                dst = wd_bf[b][:].rearrange("p (c i) -> p c i", i=PACK)
-                src = wd_raw[b][:].rearrange("p i c -> p c i")
-                for c0 in range(0, N, P):
-                    nc.gpsimd.tensor_scalar(dst[:, c0 : c0 + P], src[:, c0 : c0 + P], -1.0, 0.0, ALU.mult, ALU.add)
-            else:
-                dst = wd_bf[b][:].rearrange("p (c u i) -> p c i u", u=4, i=PACK)
-                src = wd_raw[b][:].rearrange("p i (c u) -> p c i u", u=4)
-                for c0 in range(0, P, 32):
-                    nc.scalar.activation(dst[:, c0 : c0 + 32], src[:, c0 : c0 + 32], ACT.Copy, scale=-1.0)
+            dst = wd_bf[b][:].rearrange("p (c u i) -> p c i u", u=4, i=PACK)
+            src = wd_raw[b][:].rearrange("p i (c u) -> p c i u", u=4)
+            cut = P - WD_ON_VECTOR[b]
+            for c0 in range(0, cut, 32):
+                nc.scalar.activation(dst[:, c0 : c0 + 32], src[:, c0 : c0 + 32], ACT.Copy, scale=-1.0)
+            if cut < P:
+                nc.vector.tensor_scalar(dst[:, cut:P], src[:, cut:P], -1.0, None, ALU.mult)
             nc.vector.quantize_mx(
                 out=wd_q[b][:].bitcast(FP8X4), scales=wd_s[b][:], in_=wd_bf[b][:]
             )
@@ -316,7 +316,7 @@ def tile_list_sniff_correction_kernel(
                 y[:, i, cols], wg[:, cols], ALU.mult,
             )
 
-        LEAD = 6
+        LEAD = 5
         units = [(j, 0) for j in range(LEAD)] + [(j, 1) for j in range(LEAD)]
         units = units + [(j, b) for j in range(LEAD, JT) for b in range(HB)]
 
@@ -339,21 +339,15 @@ def tile_list_sniff_correction_kernel(
 
         first_products(*units[0])
         first_products(*units[1])
-        for m0 in range(0, 64, 32):
-            round_wa(1, "A", wa_raw1[:, :, 4 * m0 : 4 * (m0 + 32)], m0, m0 + 32)
-        round_wa(1, "V", wa_raw1[:, :, HALF:KP], 64, P)
-        quantize_wa(1)
         nc.sync.dma_start(out=wg[:], in_=wgo)
         start = len(units) - 2 * EARLY
         for k in range(len(units)):
             advance(k)
-            if k == 6:
+            if k == WD_AT[0]:
                 prepare_wd(0)
-            if k == 8:
+            if k == WD_AT[1]:
                 prepare_wd(1)
-                make_identity(nc, ident[:])
-                clear(pages[2])
-                clear(pages[3])
+            if k == SECOND_AT:
                 gate_of(0)
                 second_products(0)
             if k > 0 and units[k - 1][1] == HB - 1:

@@ -23,12 +23,16 @@ KP = P * PACK
 HB = H // KP
 JT = S // P
 LIST_COLS = P // 16
-JOINED = (3, 5, 6)
+JOINED = (2, 3, 4)
+TURNED = (5, 6, 7)
+PAIRS = ((6, 7), (0, 2), (1, 3))
 EARLY = 2
-WD_ON_VECTOR = (64, 0)
+LATE_TURN = 0
+PLANE = S + H + N + HB * N
+WA_ON_VECTOR = 64
+WD_ON_VECTOR = (0, 64)
 WD_AT = (6, 8)
 SECOND_AT = 8
-SHIFT = 14
 
 
 def tile_list_sniff_correction_kernel(
@@ -50,67 +54,75 @@ def tile_list_sniff_correction_kernel(
 
         pick = held([P, S // 16], U16, "pick")
         place = held([P, S // 16], U16, "place")
-        tab_s = staged([P, T], U8, "tab_s", 16384)
+        tab_w = held([P, T], U32, "tab_w")
+        tab_s = held([P, T], U8, "tab_s")
         wb_s_raw = held([P, H], U8, "wb_s_raw")
         wb_raw = held([P, 2 * H], U8, "wb_raw")
-        v_s = held([P, S], U8, "v_s")
         got_s = held([P, S], U8, "got_s")
+        rows = held([P, PLANE], U8, "rows")
+        planes = held([P, PLANE], U8, "planes")
+        v_s = planes[:, 0:S]
+        wb_s = planes[:, S : S + H]
+        wc_s = planes[:, S + H : S + H + N]
+        we_s = planes[:, S + H + N : PLANE]
         warm_out = held([P, 32], F32, "warm_out")
         pages = [held([P, T2], F32, "page%d" % i) for i in range(PACK)]
 
         ident = held([P, P], F32, "ident")
         make_identity(nc, ident[:])
 
-        def load_scale_rows(plane, rows, shift):
-            dst = plane.bitcast(I32)
-            src = rows.bitcast(I32)
-            for r in range(4):
-                nc.sync.dma_start(
-                    out=dst[(r + shift) % 4 : P : 4, :],
-                    in_=src[r:16:4, :].unsqueeze(1).to_broadcast([4, 8, src.shape[1]]),
-                )
-
         wa_rows = wa.rearrange("(p i) c -> p i c", i=PACK)
         HALF = KP // 2
-        wa_raw = [staged([P, PACK, HALF], F32, "wa_raw%d" % u, 36864 + 4096 * u) for u in range(1, 3)]
-        wa_raw = [held([P, PACK, HALF], F32, "wa_raw0")] + wa_raw
+        wa_raw = [staged([P, PACK, KP], F32, "wa_raw%d" % b, (40960, 0)[b]) for b in range(HB)]
+
+        def load_wa(b):
+            nc.sync.dma_start(out=wa_raw[b][:], in_=wa_rows[:, :, b * KP : (b + 1) * KP])
+
+        def load_repeated(tile, scales):
+            nc.sync.dma_start(
+                out=tile[:].bitcast(I32),
+                in_=scales.bitcast(I32).unsqueeze(1).to_broadcast([16, 8, scales.shape[1] // 4]),
+            )
 
         nc.sync.dma_start(pick[:], offs)
-        load_scale_rows(tab_s[:], tab_scales[0], SHIFT)
-        def load_wa(u):
-            nc.sync.dma_start(out=wa_raw[u][:], in_=wa_rows[:, :, u * HALF : (u + 1) * HALF])
-
+        load_repeated(tab_s, tab_scales[0])
+        load_repeated(wb_s_raw, wb_scales[0])
+        nc.sync.dma_start(
+            out=rows[0:P:8, S + H : S + H + N].bitcast(I32), in_=wc_scales[0].bitcast(I32)
+        )
+        nc.sync.dma_start(
+            out=rows[0:P:8, S + H + N : PLANE].bitcast(I32).rearrange("q (a w) -> q a w", a=HB),
+            in_=we_scales.bitcast(I32).rearrange("a q w -> q a w"),
+        )
         load_wa(0)
-        load_wa(1)
         nc.sync.dma_start(out=wb_raw[:].bitcast(I32), in_=wb_words[0].bitcast(I32))
-        load_scale_rows(wb_s_raw[:], wb_scales[0], 0)
-        load_wa(2)
-        tab_w = held([P, T], U32, "tab_w")
         nc.sync.dma_start(
             out=tab_w[:].bitcast(I32),
             in_=tab_words[0].rearrange("p t i -> p (t i)").bitcast(I32),
         )
         nc.sync.dma_start(place[:], offs2)
+        load_wa(1)
         nc.scalar.activation(warm_out[:], ident[:, 0:32], ACT.Silu)
 
         for page in pages[0:2]:
             nc.vector.memset(page[:].bitcast(I32), 0)
 
         nc.vector.tensor_copy(got_s[:], tab_s[:].indirect(pick[:]))
-        nc.sync.dma_start(
-            out=v_s[:].bitcast(I32)[0 : P - SHIFT, :], in_=got_s[:].bitcast(I32)[SHIFT:P, :]
+        nc.vector.tensor_copy(rows[:, 0:S].bitcast(I32), got_s[:].bitcast(I32))
+        nc.vector.tensor_copy(
+            rows[:, S : S + H].rearrange("p (b t m) -> p b t m", b=HB, t=PACK),
+            wb_s_raw[:].rearrange("p (b m t) -> p b t m", b=HB, t=PACK),
         )
-        wa_raw.append(staged([P, PACK, HALF], F32, "wa_raw3", 12544))
-        load_wa(3)
+        for r in range(4):
+            nc.scalar.dma_start(
+                out=planes[:].bitcast(I32)[r:P:32, :], in_=rows[:].bitcast(I32)[8 * r : P : 32, :]
+            )
+        for page in pages[2:]:
+            nc.vector.memset(page[:].bitcast(I32), 0)
         wb_w = held([P, 2 * H], U8, "wb_w")
-        wb_s = held([P, H], U8, "wb_s")
         nc.vector.tensor_copy(
             wb_w[:].bitcast(U16).rearrange("p (b t m) -> p b t m", b=HB, t=PACK),
             wb_raw[:].bitcast(U16).rearrange("p (b m t) -> p b t m", b=HB, t=PACK),
-        )
-        nc.vector.tensor_copy(
-            wb_s[:].rearrange("p (b t m) -> p b t m", b=HB, t=PACK),
-            wb_s_raw[:].rearrange("p (b m t) -> p b t m", b=HB, t=PACK),
         )
 
         wa_bf = [held([P, KP * PACK], BF16, "wa_bf%d" % b) for b in range(HB)]
@@ -140,23 +152,17 @@ def tile_list_sniff_correction_kernel(
             j0, j1 = spans[u]
             nc.vector.tensor_copy(v_w[u][:], tab_w[:].indirect(pick[:, j0 * LIST_COLS : j1 * LIST_COLS]))
 
-        for u in range(3):
-            round_wa(u // 2, "A", wa_raw[u][:], 64 * (u % 2), 64 * (u % 2 + 1))
+        for u in range(2):
+            round_wa(0, "A", wa_raw[0][:, :, u * HALF : (u + 1) * HALF], 64 * u, 64 * (u + 1))
         quantize_wa(0)
         gather_words(0)
-        round_wa(1, "A", wa_raw[3][:], 64, P)
-        quantize_wa(1)
         gather_words(1)
-        for page in pages[2:]:
-            nc.vector.memset(page[:].bitcast(I32), 0)
         gather_words(2)
 
         wd_raw = [staged([P, PACK, N], F32, "wd_raw%d" % b, (33024, 48896)[b]) for b in range(HB)]
         we_w = staged([P, HB * 2 * N], U8, "we_w", 43264)
-        wc_plane = staged([P, N], U8, "wc_plane", 46336)
-        wc_s = wc_plane[:]
         wc_w = staged([P, N], U32, "wc_w", 46848)
-        wg = staged([P, S], F32, "wg", 12544)
+        wg = staged([P, S], F32, "wg", 0)
 
         def load_wd(b):
             nc.sync.dma_start(
@@ -165,16 +171,7 @@ def tile_list_sniff_correction_kernel(
             )
 
         load_wd(0)
-        we_plane = staged([P, HB * N], U8, "we_plane", 41216)
-        we_s = we_plane[:]
-        nc.vector.memset(we_s.bitcast(I32), 0)
-        for q in range(4):
-            nc.sync.dma_start(
-                out=we_s.bitcast(I32).rearrange("p (a w) -> p a w", a=HB)[32 * q : 32 * q + 4, :, :],
-                in_=we_scales.bitcast(I32)[:, 4 * q : 4 * q + 4, :].rearrange("a r w -> r a w"),
-            )
         load_wd(1)
-        load_scale_rows(wc_s, wc_scales[0], 0)
         nc.sync.dma_start(
             out=wc_w[:].bitcast(I32),
             in_=wc_words[0].rearrange("p c i -> p (c i)").bitcast(I32),
@@ -208,10 +205,14 @@ def tile_list_sniff_correction_kernel(
             c = (j - spans[u][0]) * P
             return v_w[u][:, c : c + P].bitcast(FP8X4), v_s[:, j * P : (j + 1) * P]
 
+        def bank(number, shape):
+            return psum.tile(shape, F32, name="bank%d" % number)
+
         def first_products(j, b):
             codes, scales = v_cols(j)
-            a_ps = psum.tile([P, PACK, P], F32, name="a_ps", bufs=2)
-            b_ps = psum.tile([P, PACK, P], F32, name="b_ps", bufs=2)
+            turn_of = units.index((j, b)) % 2
+            a_ps = bank(turn_of, [P, PACK, P])
+            b_ps = bank(2 + turn_of, [P, PACK, P])
             for t in range(PACK):
                 m = slice(t * P, (t + 1) * P)
                 nc.tensor.matmul_mx(
@@ -243,8 +244,8 @@ def tile_list_sniff_correction_kernel(
 
         def gate_of(j):
             codes, scales = v_cols(j)
-            c_ps = psum.tile([P, N], F32, name="c_ps")
-            gate[j] = ring.tile([P, PACK, P], F32, name="gate")
+            c_ps = bank(4, [P, N])
+            gate[j] = ring.tile([P, PACK, P], F32, name="gate", bufs=3)
             nc.tensor.matmul_mx(
                 out=c_ps[:], lhsT=codes, lhsT_scale=scales,
                 rhs=wc_w[:].bitcast(FP8X4), rhs_scale=wc_s, start=True, stop=True,
@@ -253,13 +254,55 @@ def tile_list_sniff_correction_kernel(
                 gate[j][:], c_ps[:].rearrange("j (p i) -> j i p", i=PACK), ACT.Tanh, scale=0.5
             )
 
+        def turned_products(j):
+            e_rows = bank(PAIRS[2][0], [P, PACK, P])
+            d_rows = bank(PAIRS[2][1], [P, PACK, P])
+            for q in range(PACK):
+                for b in range(HB):
+                    c0 = b * N + q * P
+                    m = slice(b * P, (b + 1) * P)
+                    nc.tensor.matmul_mx(
+                        out=e_rows[:, q, :], lhsT=we_w[:, 2 * c0 : 2 * (c0 + P)].bitcast(FP4X4),
+                        lhsT_scale=we_s[:, c0 : c0 + P],
+                        rhs=h_q[j][:, m].bitcast(FP8X4), rhs_scale=h_s[j][:, m],
+                        start=(b == 0), stop=(b == HB - 1),
+                    )
+            for q in range(PACK):
+                for b in range(HB):
+                    n = slice(q * P, (q + 1) * P)
+                    m = slice(b * P, (b + 1) * P)
+                    nc.tensor.matmul_mx(
+                        out=d_rows[:, q, :], lhsT=wd_q[b][:, n].bitcast(FP8X4), lhsT_scale=wd_s[b][:, n],
+                        rhs=h_q[j][:, m].bitcast(FP8X4), rhs_scale=h_s[j][:, m],
+                        start=(b == 0), stop=(b == HB - 1),
+                    )
+            e_sb = ring.tile([P, PACK, P], F32, name="e_sb")
+            d_sb = ring.tile([P, PACK, P], F32, name="d_sb")
+            nc.scalar.copy(e_sb[:], e_rows[:])
+            nc.scalar.copy(d_sb[:], d_rows[:])
+            pending[j] = (e_sb, d_sb)
+
+        def turn_back(j):
+            e_sb, d_sb = pending[j]
+            pair = PAIRS[0 if j <= EARLY else (j - EARLY) % 2]
+            e_ps = bank(pair[0], [P, N])
+            d_ps = bank(pair[1], [P, N])
+            for q in range(PACK):
+                n = slice(q * P, (q + 1) * P)
+                nc.tensor.matmul(e_ps[:, n], e_sb[:, q, :], ident[:], start=True, stop=True, is_transpose=True)
+            for q in range(PACK):
+                n = slice(q * P, (q + 1) * P)
+                nc.tensor.matmul(d_ps[:, n], e_sb[:, q, :], ident[:], start=True, stop=False, is_transpose=True)
+                nc.tensor.matmul(d_ps[:, n], d_sb[:, q, :], ident[:], start=False, stop=True, is_transpose=True)
+            pending[j] = (e_ps, d_ps)
+
         def second_products(j):
-            if j <= EARLY or (j - EARLY) % 3 == 0:
-                e_ps = psum.tile([P, N], F32, name="e_ps")
-                d_ps = psum.tile([P, N], F32, name="d_ps")
-            else:
-                e_ps = psum.tile([P, N], F32, name="e_late", tag="a_ps", bufs=2)
-                d_ps = psum.tile([P, N], F32, name="d_late", tag="b_ps", bufs=2)
+            pair = PAIRS[0 if j <= EARLY else (j - EARLY) % 2]
+            if j in TURNED:
+                turn_back(j)
+                return
+            e_ps = bank(pair[0], [P, N])
+            d_ps = bank(pair[1], [P, N])
 
             def e_passes(bank, first, last):
                 for b in range(HB):
@@ -286,9 +329,9 @@ def tile_list_sniff_correction_kernel(
 
         def interpolate(j):
             e_ps, d_ps = pending[j]
-            e_part = ring.tile([P, PACK, P], F32, name="e_part")
-            d_part = ring.tile([P, PACK, P], F32, name="d_part")
-            if j in JOINED:
+            e_part = ring.tile([P, PACK, P], F32, name="e_part", bufs=3)
+            d_part = ring.tile([P, PACK, P], F32, name="d_part", bufs=3)
+            if j in JOINED + TURNED:
                 nc.scalar.activation(
                     e_part[:], e_ps[:].rearrange("j (p i) -> j i p", i=PACK), ACT.Copy, scale=-2.0
                 )
@@ -301,7 +344,11 @@ def tile_list_sniff_correction_kernel(
                 d_part[:], gate[j][:], 1.0, d_ps[:].rearrange("j (p i) -> j i p", i=PACK),
                 ALU.add, ALU.mult,
             )
-            y_ps = psum.tile([P, PACK, P], F32, name="y_ps")
+            pending[j] = (e_part, d_part)
+
+        def turn(j):
+            e_part, d_part = pending[j]
+            y_ps = bank(5, [P, PACK, P])
             for i in range(PACK):
                 nc.tensor.matmul(y_ps[:, i, :], e_part[:, i, :], ident[:], start=True, stop=False, is_transpose=True)
                 nc.tensor.matmul(y_ps[:, i, :], d_part[:, i, :], ident[:], start=False, stop=True, is_transpose=True)
@@ -316,7 +363,7 @@ def tile_list_sniff_correction_kernel(
                 y[:, i, cols], wg[:, cols], ALU.mult,
             )
 
-        LEAD = 5
+        LEAD = 4
         units = [(j, 0) for j in range(LEAD)] + [(j, 1) for j in range(LEAD)]
         units = units + [(j, b) for j in range(LEAD, JT) for b in range(HB)]
 
@@ -326,6 +373,11 @@ def tile_list_sniff_correction_kernel(
                 first_products(*units[k + 2])
 
         def second_stage(j):
+            if LATE_TURN == 0 and j > 0:
+                turn(j - 1)
+                place_tiles(j)
+            if j + 2 in TURNED:
+                turned_products(j + 2)
             if j + 1 < JT:
                 gate_of(j + 1)
                 if j >= EARLY:
@@ -333,12 +385,21 @@ def tile_list_sniff_correction_kernel(
             interpolate(j)
             if j < EARLY:
                 second_products(j + 1)
-            if j > 0:
-                for i in range(PACK - 1):
-                    put(pages[i], i, j - 1, j)
+            if LATE_TURN == 1 and j > 0:
+                turn(j - 1)
+                place_tiles(j)
+
+        def place_tiles(j):
+            for i in range(PACK - 1):
+                put(pages[i], i, j - 1, j)
 
         first_products(*units[0])
         first_products(*units[1])
+        for m0 in range(0, P - WA_ON_VECTOR, 32):
+            round_wa(1, "A", wa_raw[1][:, :, 4 * m0 : 4 * (m0 + 32)], m0, m0 + 32)
+        if WA_ON_VECTOR:
+            round_wa(1, "V", wa_raw[1][:, :, 4 * (P - WA_ON_VECTOR) : KP], P - WA_ON_VECTOR, P)
+        quantize_wa(1)
         nc.sync.dma_start(out=wg[:], in_=wgo)
         start = len(units) - 2 * EARLY
         for k in range(len(units)):
@@ -357,6 +418,7 @@ def tile_list_sniff_correction_kernel(
         quantize_hidden(JT - 1)
         for j in range(EARLY, JT):
             second_stage(j)
+        turn(JT - 1)
         for i in range(PACK - 1):
             put(pages[i], i, JT - 1, JT)
             nc.sync.dma_start(out=out_rows[:, i, :], in_=pages[i][:])

@@ -27,12 +27,15 @@ JOINED = (2, 3, 4)
 TURNED = (5, 6, 7)
 PAIRS = ((6, 7), (0, 2), (1, 3))
 EARLY = 2
+ACT_AT = 86016
+WIDE_RING = (2, 3, 4, 6, 7)
+WIDE_UNITS = 10
 LATE_TURN = 0
 PLANE = S + H + N + HB * N
 WA_ON_VECTOR = 64
-WD_ON_VECTOR = (0, 64)
-WD_AT = (6, 8)
-SECOND_AT = 8
+WD_ON_VECTOR = (64, 0)
+WD_AT = (1, 4)
+SECOND_AT = 9
 
 
 def tile_list_sniff_correction_kernel(
@@ -54,11 +57,11 @@ def tile_list_sniff_correction_kernel(
 
         pick = held([P, S // 16], U16, "pick")
         place = held([P, S // 16], U16, "place")
-        tab_w = held([P, T], U32, "tab_w")
+        tab_w = staged([P, T], U32, "tab_w", 57344)
         tab_s = held([P, T], U8, "tab_s")
         wb_s_raw = held([P, H], U8, "wb_s_raw")
-        wb_raw = held([P, 2 * H], U8, "wb_raw")
-        got_s = held([P, S], U8, "got_s")
+        wb_raw = staged([P, 2 * H], U8, "wb_raw", 8128)
+        got_s = staged([P, S], U8, "got_s", 20480)
         rows = held([P, PLANE], U8, "rows")
         planes = held([P, PLANE], U8, "planes")
         v_s = planes[:, 0:S]
@@ -66,14 +69,16 @@ def tile_list_sniff_correction_kernel(
         wc_s = planes[:, S + H : S + H + N]
         we_s = planes[:, S + H + N : PLANE]
         warm_out = held([P, 32], F32, "warm_out")
-        pages = [held([P, T2], F32, "page%d" % i) for i in range(PACK)]
+        pages = [held([P, T2], F32, "page%d" % i) for i in range(2)]
 
+        warm = held([P, 32], F32, "warm")
+        nc.vector.memset(warm[:], 0.0)
         ident = held([P, P], F32, "ident")
         make_identity(nc, ident[:])
 
         wa_rows = wa.rearrange("(p i) c -> p i c", i=PACK)
         HALF = KP // 2
-        wa_raw = [staged([P, PACK, KP], F32, "wa_raw%d" % b, (40960, 0)[b]) for b in range(HB)]
+        wa_raw = [staged([P, PACK, KP], F32, "wa_raw0", 40960)]
 
         def load_wa(b):
             nc.sync.dma_start(out=wa_raw[b][:], in_=wa_rows[:, :, b * KP : (b + 1) * KP])
@@ -85,8 +90,8 @@ def tile_list_sniff_correction_kernel(
             )
 
         nc.sync.dma_start(pick[:], offs)
-        load_repeated(tab_s, tab_scales[0])
         load_repeated(wb_s_raw, wb_scales[0])
+        load_repeated(tab_s, tab_scales[0])
         nc.sync.dma_start(
             out=rows[0:P:8, S + H : S + H + N].bitcast(I32), in_=wc_scales[0].bitcast(I32)
         )
@@ -94,15 +99,14 @@ def tile_list_sniff_correction_kernel(
             out=rows[0:P:8, S + H + N : PLANE].bitcast(I32).rearrange("q (a w) -> q a w", a=HB),
             in_=we_scales.bitcast(I32).rearrange("a q w -> q a w"),
         )
-        load_wa(0)
         nc.sync.dma_start(out=wb_raw[:].bitcast(I32), in_=wb_words[0].bitcast(I32))
+        load_wa(0)
         nc.sync.dma_start(
             out=tab_w[:].bitcast(I32),
             in_=tab_words[0].rearrange("p t i -> p (t i)").bitcast(I32),
         )
         nc.sync.dma_start(place[:], offs2)
-        load_wa(1)
-        nc.scalar.activation(warm_out[:], ident[:, 0:32], ACT.Silu)
+        nc.scalar.activation(warm_out[:], warm[:], ACT.Silu)
 
         for page in pages[0:2]:
             nc.vector.memset(page[:].bitcast(I32), 0)
@@ -114,21 +118,25 @@ def tile_list_sniff_correction_kernel(
             wb_s_raw[:].rearrange("p (b m t) -> p b t m", b=HB, t=PACK),
         )
         for r in range(4):
-            nc.scalar.dma_start(
+            nc.sync.dma_start(
                 out=planes[:].bitcast(I32)[r:P:32, :], in_=rows[:].bitcast(I32)[8 * r : P : 32, :]
             )
-        for page in pages[2:]:
-            nc.vector.memset(page[:].bitcast(I32), 0)
-        wb_w = held([P, 2 * H], U8, "wb_w")
+        wb_w = staged([P, 2 * H], U8, "wb_w", 18496)
         nc.vector.tensor_copy(
             wb_w[:].bitcast(U16).rearrange("p (b t m) -> p b t m", b=HB, t=PACK),
             wb_raw[:].bitcast(U16).rearrange("p (b m t) -> p b t m", b=HB, t=PACK),
         )
 
-        wa_bf = [held([P, KP * PACK], BF16, "wa_bf%d" % b) for b in range(HB)]
+        wa_raw.append(staged([P, PACK, KP], F32, "wa_raw1", 0))
+        load_wa(1)
+        pages.extend(staged([P, T2], F32, "page%d" % i, (10112, 21440)[i - 2]) for i in range(2, PACK))
+        for page in pages[2:]:
+            nc.vector.memset(page[:].bitcast(I32), 0)
+
+        wa_bf = [staged([P, KP * PACK], BF16, "wa_bf%d" % b, (77824, 57344)[b]) for b in range(HB)]
         wa_q = [held([P, KP], U32, "wa_q%d" % b) for b in range(HB)]
         wa_s = [held([P, KP], U8, "wa_s%d" % b) for b in range(HB)]
-        wd_bf = [held([P, N * PACK], BF16, "wd_bf%d" % b) for b in range(HB)]
+        wd_bf = {}
         wd_q = [held([P, N], U32, "wd_q%d" % b) for b in range(HB)]
         wd_s = [held([P, N], U8, "wd_s%d" % b) for b in range(HB)]
 
@@ -146,16 +154,17 @@ def tile_list_sniff_correction_kernel(
             )
 
         spans = [(0, 2), (2, 4), (4, 8)]
-        v_w = [held([P, (j1 - j0) * P], U32, "v_w%d" % j0) for j0, j1 in spans]
+        v_w = {}
 
         def gather_words(u):
             j0, j1 = spans[u]
+            v_w[u] = staged([P, (j1 - j0) * P], U32, "v_w%d" % j0, (8192, 77824, 78848)[u])
             nc.vector.tensor_copy(v_w[u][:], tab_w[:].indirect(pick[:, j0 * LIST_COLS : j1 * LIST_COLS]))
 
         for u in range(2):
             round_wa(0, "A", wa_raw[0][:, :, u * HALF : (u + 1) * HALF], 64 * u, 64 * (u + 1))
-        quantize_wa(0)
         gather_words(0)
+        quantize_wa(0)
         gather_words(1)
         gather_words(2)
 
@@ -182,6 +191,7 @@ def tile_list_sniff_correction_kernel(
         )
 
         def prepare_wd(b):
+            wd_bf[b] = staged([P, N * PACK], BF16, "wd_bf%d" % b, ACT_AT + 2048 * WD_AT[b])
             dst = wd_bf[b][:].rearrange("p (c u i) -> p c i u", u=4, i=PACK)
             src = wd_raw[b][:].rearrange("p i (c u) -> p c i u", u=4)
             cut = P - WD_ON_VECTOR[b]
@@ -210,9 +220,9 @@ def tile_list_sniff_correction_kernel(
 
         def first_products(j, b):
             codes, scales = v_cols(j)
-            turn_of = units.index((j, b)) % 2
-            a_ps = bank(turn_of, [P, PACK, P])
-            b_ps = bank(2 + turn_of, [P, PACK, P])
+            k = units.index((j, b))
+            a_ps = bank(k % 2, [P, PACK, P])
+            b_ps = bank(WIDE_RING[k % 5] if k < WIDE_UNITS else 2 + k % 2, [P, PACK, P])
             for t in range(PACK):
                 m = slice(t * P, (t + 1) * P)
                 nc.tensor.matmul_mx(
@@ -226,7 +236,7 @@ def tile_list_sniff_correction_kernel(
                     lhsT_scale=wb_s[:, c0 : c0 + P],
                     rhs=codes, rhs_scale=scales, start=True, stop=True,
                 )
-            act = ring.tile([P, P, PACK], F32, name="act", bufs=3)
+            act = staged([P, P, PACK], F32, "act%d" % k, ACT_AT + 2048 * k)
             nc.scalar.activation(act[:], a_ps[:].rearrange("p t j -> p j t"), ACT.Silu)
             pending[j, b] = (b_ps, act)
 
@@ -363,14 +373,15 @@ def tile_list_sniff_correction_kernel(
                 y[:, i, cols], wg[:, cols], ALU.mult,
             )
 
-        LEAD = 4
+        LEAD = 5
         units = [(j, 0) for j in range(LEAD)] + [(j, 1) for j in range(LEAD)]
         units = units + [(j, b) for j in range(LEAD, JT) for b in range(HB)]
 
         def advance(k):
             hidden(*units[k])
-            if k + 2 < len(units):
-                first_products(*units[k + 2])
+            ahead = k + 5 if k + 5 < WIDE_UNITS else k + 2 if k + 2 >= WIDE_UNITS else None
+            if ahead is not None and ahead < len(units):
+                first_products(*units[ahead])
 
         def second_stage(j):
             if LATE_TURN == 0 and j > 0:
@@ -395,11 +406,14 @@ def tile_list_sniff_correction_kernel(
 
         first_products(*units[0])
         first_products(*units[1])
+        first_products(*units[2])
         for m0 in range(0, P - WA_ON_VECTOR, 32):
             round_wa(1, "A", wa_raw[1][:, :, 4 * m0 : 4 * (m0 + 32)], m0, m0 + 32)
         if WA_ON_VECTOR:
             round_wa(1, "V", wa_raw[1][:, :, 4 * (P - WA_ON_VECTOR) : KP], P - WA_ON_VECTOR, P)
         quantize_wa(1)
+        first_products(*units[3])
+        first_products(*units[4])
         nc.sync.dma_start(out=wg[:], in_=wgo)
         start = len(units) - 2 * EARLY
         for k in range(len(units)):

@@ -23,19 +23,48 @@ KP = P * PACK
 HB = H // KP
 JT = S // P
 LIST_COLS = P // 16
+LATE = N + HB * N
+ROUND_ROWS = 32
+
+LEAD = 5
+UNITS = [(j, b) for b in range(HB) for j in range(LEAD)] + [(j, b) for j in range(LEAD, JT) for b in range(HB)]
+WIDE_RING = (2, 3, 4, 6, 7)
+WIDE_UNITS = HB * LEAD
+GATE_BANK, Y_BANK = 4, 5
+PAIRS = ((6, 7), (0, 2))
+ROWS_PAIR = (1, 3)
+EARLY = 2
 JOINED = (2, 3, 4)
 TURNED = (5, 6, 7)
-PAIRS = ((6, 7), (0, 2), (1, 3))
-EARLY = 2
-ACT_AT = 86016
-WIDE_RING = (2, 3, 4, 6, 7)
-WIDE_UNITS = 10
-LATE_TURN = 0
-PLANE = S + H + N + HB * N
-WA_ON_VECTOR = 64
-WD_ON_VECTOR = (64, 0)
-WD_AT = (1, 4)
-SECOND_AT = 9
+WD_AT = (1, LEAD - 1)
+SPLIT = 2
+SPANS = ((0, 2), (2, 4), (4, 8))
+
+AT = {
+    "wa_raw1": 0,
+    "wg": 0,
+    "wd_bf0": 4096,
+    "wb_raw": 8128,
+    "v_w0": 8192,
+    "wb_w": 18496,
+    "got_s": 20480,
+    "page2": 21440,
+    "wd_raw0": 33024,
+    "late_rows": 41216,
+    "we_w": 43264,
+    "wc_w": 46848,
+    "wd_raw1": 48896,
+    "wa_raw0": 40960,
+    "page1": 57088,
+    "wa_bf1": 65280,
+    "page3": 73344,
+    "tab_w": 65216,
+    "act": 86016,
+    "wd_bf1": 86016 + 2048 * WD_AT[1],
+    "wa_bf0": 118784,
+    "v_w2": 118784,
+    "v_w4": 119808,
+}
 
 
 def tile_list_sniff_correction_kernel(
@@ -49,36 +78,41 @@ def tile_list_sniff_correction_kernel(
         ring = ctx.enter_context(tc.tile_pool(name="ring", bufs=2))
         psum = ctx.enter_context(tc.psum_pool(name="psum", bufs=1))
 
-        def held(shape, dtype, name, tag=None):
-            return keep.tile(shape, dtype, name=name, tag=tag or name, align_bytes=64)
+        def held(shape, dtype, name):
+            return keep.tile(shape, dtype, name=name, tag=name, align_bytes=64)
 
-        def staged(shape, dtype, name, offset):
-            return stage.tile(shape, dtype, name=name, align_bytes=64, offset=offset)
+        def staged(shape, dtype, name):
+            return stage.tile(shape, dtype, name=name, align_bytes=64, offset=AT[name])
+
+        def bank(number, shape):
+            return psum.tile(shape, F32, name="bank%d" % number)
+
+        def clear_page(i, tile):
+            pages[i] = tile
+            nc.vector.memset(tile[:].bitcast(I32), 0)
 
         pick = held([P, S // 16], U16, "pick")
         place = held([P, S // 16], U16, "place")
-        tab_w = staged([P, T], U32, "tab_w", 57344)
+        tab_w = staged([P, T], U32, "tab_w")
         tab_s = held([P, T], U8, "tab_s")
         wb_s_raw = held([P, H], U8, "wb_s_raw")
-        wb_raw = staged([P, 2 * H], U8, "wb_raw", 8128)
-        got_s = staged([P, S], U8, "got_s", 20480)
-        rows = held([P, PLANE], U8, "rows")
-        planes = held([P, PLANE], U8, "planes")
+        wb_raw = staged([P, 2 * H], U8, "wb_raw")
+        got_s = staged([P, S], U8, "got_s")
+        rows = held([P, S + H], U8, "rows")
+        planes = held([P, S + H], U8, "planes")
+        late_planes = held([P, LATE], U8, "late_planes")
         v_s = planes[:, 0:S]
         wb_s = planes[:, S : S + H]
-        wc_s = planes[:, S + H : S + H + N]
-        we_s = planes[:, S + H + N : PLANE]
-        warm_out = held([P, 32], F32, "warm_out")
-        pages = [held([P, T2], F32, "page%d" % i) for i in range(2)]
+        wc_s = late_planes[:, 0:N]
+        we_s = late_planes[:, N:LATE]
+        page0 = held([P, T2], F32, "page0")
+        pages = {}
 
-        warm = held([P, 32], F32, "warm")
-        nc.vector.memset(warm[:], 0.0)
         ident = held([P, P], F32, "ident")
         make_identity(nc, ident[:])
 
         wa_rows = wa.rearrange("(p i) c -> p i c", i=PACK)
-        HALF = KP // 2
-        wa_raw = [staged([P, PACK, KP], F32, "wa_raw0", 40960)]
+        wa_raw = [staged([P, PACK, KP], F32, "wa_raw0")]
 
         def load_wa(b):
             nc.sync.dma_start(out=wa_raw[b][:], in_=wa_rows[:, :, b * KP : (b + 1) * KP])
@@ -89,16 +123,15 @@ def tile_list_sniff_correction_kernel(
                 in_=scales.bitcast(I32).unsqueeze(1).to_broadcast([16, 8, scales.shape[1] // 4]),
             )
 
+        def move_rows(dst, src):
+            for r in range(4):
+                nc.sync.dma_start(
+                    out=dst[:].bitcast(I32)[r:P:32, :], in_=src[:].bitcast(I32)[8 * r : P : 32, :]
+                )
+
         nc.sync.dma_start(pick[:], offs)
         load_repeated(wb_s_raw, wb_scales[0])
         load_repeated(tab_s, tab_scales[0])
-        nc.sync.dma_start(
-            out=rows[0:P:8, S + H : S + H + N].bitcast(I32), in_=wc_scales[0].bitcast(I32)
-        )
-        nc.sync.dma_start(
-            out=rows[0:P:8, S + H + N : PLANE].bitcast(I32).rearrange("q (a w) -> q a w", a=HB),
-            in_=we_scales.bitcast(I32).rearrange("a q w -> q a w"),
-        )
         nc.sync.dma_start(out=wb_raw[:].bitcast(I32), in_=wb_words[0].bitcast(I32))
         load_wa(0)
         nc.sync.dma_start(
@@ -106,10 +139,8 @@ def tile_list_sniff_correction_kernel(
             in_=tab_words[0].rearrange("p t i -> p (t i)").bitcast(I32),
         )
         nc.sync.dma_start(place[:], offs2)
-        nc.scalar.activation(warm_out[:], warm[:], ACT.Silu)
 
-        for page in pages[0:2]:
-            nc.vector.memset(page[:].bitcast(I32), 0)
+        clear_page(0, page0)
 
         nc.vector.tensor_copy(got_s[:], tab_s[:].indirect(pick[:]))
         nc.vector.tensor_copy(rows[:, 0:S].bitcast(I32), got_s[:].bitcast(I32))
@@ -117,61 +148,53 @@ def tile_list_sniff_correction_kernel(
             rows[:, S : S + H].rearrange("p (b t m) -> p b t m", b=HB, t=PACK),
             wb_s_raw[:].rearrange("p (b m t) -> p b t m", b=HB, t=PACK),
         )
-        for r in range(4):
-            nc.sync.dma_start(
-                out=planes[:].bitcast(I32)[r:P:32, :], in_=rows[:].bitcast(I32)[8 * r : P : 32, :]
-            )
-        wb_w = staged([P, 2 * H], U8, "wb_w", 18496)
+        move_rows(planes, rows)
+        wb_w = staged([P, 2 * H], U8, "wb_w")
         nc.vector.tensor_copy(
             wb_w[:].bitcast(U16).rearrange("p (b t m) -> p b t m", b=HB, t=PACK),
             wb_raw[:].bitcast(U16).rearrange("p (b m t) -> p b t m", b=HB, t=PACK),
         )
 
-        wa_raw.append(staged([P, PACK, KP], F32, "wa_raw1", 0))
+        wa_raw.append(staged([P, PACK, KP], F32, "wa_raw1"))
         load_wa(1)
-        pages.extend(staged([P, T2], F32, "page%d" % i, (10112, 21440)[i - 2]) for i in range(2, PACK))
-        for page in pages[2:]:
-            nc.vector.memset(page[:].bitcast(I32), 0)
+        clear_page(2, staged([P, T2], F32, "page2"))
 
-        wa_bf = [staged([P, KP * PACK], BF16, "wa_bf%d" % b, (77824, 57344)[b]) for b in range(HB)]
+        wa_bf = [staged([P, KP * PACK], BF16, "wa_bf%d" % b) for b in range(HB)]
         wa_q = [held([P, KP], U32, "wa_q%d" % b) for b in range(HB)]
         wa_s = [held([P, KP], U8, "wa_s%d" % b) for b in range(HB)]
-        wd_bf = {}
         wd_q = [held([P, N], U32, "wd_q%d" % b) for b in range(HB)]
         wd_s = [held([P, N], U8, "wd_s%d" % b) for b in range(HB)]
 
-        def round_wa(b, engine, raw, m0, m1):
+        def round_wa(copy, b, m0, m1):
             dst = wa_bf[b][:].rearrange("p (t m i) -> p m i t", t=PACK, i=PACK)[:, m0:m1]
-            src = raw.rearrange("p i (m t) -> p m i t", t=PACK)
-            if engine == "A":
-                nc.scalar.copy(dst, src)
-            else:
-                nc.vector.tensor_copy(dst, src)
+            src = wa_raw[b][:, :, PACK * m0 : PACK * m1].rearrange("p i (m t) -> p m i t", t=PACK)
+            copy(dst, src)
 
         def quantize_wa(b):
             nc.vector.quantize_mx(
                 out=wa_q[b][:].bitcast(FP8X4), scales=wa_s[b][:], in_=wa_bf[b][:]
             )
 
-        spans = [(0, 2), (2, 4), (4, 8)]
-        v_w = {}
+        v_w = []
 
-        def gather_words(u):
-            j0, j1 = spans[u]
-            v_w[u] = staged([P, (j1 - j0) * P], U32, "v_w%d" % j0, (8192, 77824, 78848)[u])
-            nc.vector.tensor_copy(v_w[u][:], tab_w[:].indirect(pick[:, j0 * LIST_COLS : j1 * LIST_COLS]))
+        def gather_words(j0, j1):
+            words = staged([P, (j1 - j0) * P], U32, "v_w%d" % j0)
+            nc.vector.tensor_copy(words[:], tab_w[:].indirect(pick[:, j0 * LIST_COLS : j1 * LIST_COLS]))
+            v_w.extend(words[:, c : c + P] for c in range(0, (j1 - j0) * P, P))
 
-        for u in range(2):
-            round_wa(0, "A", wa_raw[0][:, :, u * HALF : (u + 1) * HALF], 64 * u, 64 * (u + 1))
-        gather_words(0)
+        round_wa(nc.scalar.copy, 0, 0, P // 2)
+        round_wa(nc.scalar.copy, 0, P // 2, P)
+        gather_words(*SPANS[0])
         quantize_wa(0)
-        gather_words(1)
-        gather_words(2)
+        gather_words(*SPANS[1])
+        gather_words(*SPANS[2])
+        for i in (1, 3):
+            clear_page(i, staged([P, T2], F32, "page%d" % i))
 
-        wd_raw = [staged([P, PACK, N], F32, "wd_raw%d" % b, (33024, 48896)[b]) for b in range(HB)]
-        we_w = staged([P, HB * 2 * N], U8, "we_w", 43264)
-        wc_w = staged([P, N], U32, "wc_w", 46848)
-        wg = staged([P, S], F32, "wg", 0)
+        wd_raw = [staged([P, PACK, N], F32, "wd_raw%d" % b) for b in range(HB)]
+        we_w = staged([P, HB * 2 * N], U8, "we_w")
+        wc_w = staged([P, N], U32, "wc_w")
+        wg = staged([P, S], F32, "wg")
 
         def load_wd(b):
             nc.sync.dma_start(
@@ -180,6 +203,12 @@ def tile_list_sniff_correction_kernel(
             )
 
         load_wd(0)
+        late_rows = staged([P, LATE], U8, "late_rows")
+        nc.sync.dma_start(out=late_rows[0:P:8, 0:N].bitcast(I32), in_=wc_scales[0].bitcast(I32))
+        nc.sync.dma_start(
+            out=late_rows[0:P:8, N:LATE].bitcast(I32).rearrange("q (a w) -> q a w", a=HB),
+            in_=we_scales.bitcast(I32).rearrange("a q w -> q a w"),
+        )
         load_wd(1)
         nc.sync.dma_start(
             out=wc_w[:].bitcast(I32),
@@ -189,40 +218,35 @@ def tile_list_sniff_correction_kernel(
             out=we_w[:].bitcast(I32).rearrange("p (a w) -> p a w", a=HB),
             in_=we_words.bitcast(I32).rearrange("a p w -> p a w"),
         )
+        move_rows(late_planes, late_rows)
 
         def prepare_wd(b):
-            wd_bf[b] = staged([P, N * PACK], BF16, "wd_bf%d" % b, ACT_AT + 2048 * WD_AT[b])
-            dst = wd_bf[b][:].rearrange("p (c u i) -> p c i u", u=4, i=PACK)
+            wd_bf = staged([P, N * PACK], BF16, "wd_bf%d" % b)
+            dst = wd_bf[:].rearrange("p (c u i) -> p c i u", u=4, i=PACK)
             src = wd_raw[b][:].rearrange("p i (c u) -> p c i u", u=4)
-            cut = P - WD_ON_VECTOR[b]
-            for c0 in range(0, cut, 32):
-                nc.scalar.activation(dst[:, c0 : c0 + 32], src[:, c0 : c0 + 32], ACT.Copy, scale=-1.0)
-            if cut < P:
-                nc.vector.tensor_scalar(dst[:, cut:P], src[:, cut:P], -1.0, None, ALU.mult)
-            nc.vector.quantize_mx(
-                out=wd_q[b][:].bitcast(FP8X4), scales=wd_s[b][:], in_=wd_bf[b][:]
-            )
+            for c0 in range(0, N // 4, ROUND_ROWS):
+                c1 = c0 + ROUND_ROWS
+                nc.scalar.activation(dst[:, c0:c1], src[:, c0:c1], ACT.Copy, scale=-1.0)
+            nc.vector.quantize_mx(out=wd_q[b][:].bitcast(FP8X4), scales=wd_s[b][:], in_=wd_bf[:])
 
         y = held([P, PACK, S], F32, "y")
         h_bf = [held([P, HB, P, PACK], BF16, "h_bf%d" % j) for j in range(JT)]
         h_q = [held([P, HB * P], U32, "h_q%d" % j) for j in range(JT)]
         h_s = [held([P, HB * P], U8, "h_s%d" % j) for j in range(JT)]
-        gate = {}
-        pending = {}
+        unit_parts, gate, copied, sums, terms = {}, {}, {}, {}, {}
 
-        def v_cols(j):
-            u = [k for k, (j0, j1) in enumerate(spans) if j0 <= j < j1][0]
-            c = (j - spans[u][0]) * P
-            return v_w[u][:, c : c + P].bitcast(FP8X4), v_s[:, j * P : (j + 1) * P]
+        def table_tile(j):
+            return v_w[j].bitcast(FP8X4), v_s[:, j * P : (j + 1) * P]
 
-        def bank(number, shape):
-            return psum.tile(shape, F32, name="bank%d" % number)
+        def h_pass(j, b):
+            m = slice(b * P, (b + 1) * P)
+            return h_q[j][:, m].bitcast(FP8X4), h_s[j][:, m]
 
-        def first_products(j, b):
-            codes, scales = v_cols(j)
-            k = units.index((j, b))
+        def first_products(k):
+            j, b = UNITS[k]
+            codes, scales = table_tile(j)
             a_ps = bank(k % 2, [P, PACK, P])
-            b_ps = bank(WIDE_RING[k % 5] if k < WIDE_UNITS else 2 + k % 2, [P, PACK, P])
+            b_ps = bank(WIDE_RING[k % LEAD] if k < WIDE_UNITS else 2 + k % 2, [P, PACK, P])
             for t in range(PACK):
                 m = slice(t * P, (t + 1) * P)
                 nc.tensor.matmul_mx(
@@ -236,12 +260,13 @@ def tile_list_sniff_correction_kernel(
                     lhsT_scale=wb_s[:, c0 : c0 + P],
                     rhs=codes, rhs_scale=scales, start=True, stop=True,
                 )
-            act = staged([P, P, PACK], F32, "act%d" % k, ACT_AT + 2048 * k)
+            act = stage.tile([P, P, PACK], F32, name="act%d" % k, align_bytes=64, offset=AT["act"] + 2048 * k)
             nc.scalar.activation(act[:], a_ps[:].rearrange("p t j -> p j t"), ACT.Silu)
-            pending[j, b] = (b_ps, act)
+            unit_parts[k] = (b_ps, act)
 
-        def hidden(j, b):
-            b_ps, act = pending[j, b]
+        def hidden(k):
+            j, b = UNITS[k]
+            b_ps, act = unit_parts[k]
             nc.vector.tensor_tensor(
                 h_bf[j][:, b], b_ps[:].rearrange("p t j -> p j t"), act[:], ALU.mult
             )
@@ -253,8 +278,8 @@ def tile_list_sniff_correction_kernel(
             )
 
         def gate_of(j):
-            codes, scales = v_cols(j)
-            c_ps = bank(4, [P, N])
+            codes, scales = table_tile(j)
+            c_ps = bank(GATE_BANK, [P, N])
             gate[j] = ring.tile([P, PACK, P], F32, name="gate", bufs=3)
             nc.tensor.matmul_mx(
                 out=c_ps[:], lhsT=codes, lhsT_scale=scales,
@@ -265,80 +290,70 @@ def tile_list_sniff_correction_kernel(
             )
 
         def turned_products(j):
-            e_rows = bank(PAIRS[2][0], [P, PACK, P])
-            d_rows = bank(PAIRS[2][1], [P, PACK, P])
-            for q in range(PACK):
+            e_rows = bank(ROWS_PAIR[0], [P, PACK, P])
+            d_rows = bank(ROWS_PAIR[1], [P, PACK, P])
+            for q in range(N // P):
                 for b in range(HB):
                     c0 = b * N + q * P
-                    m = slice(b * P, (b + 1) * P)
+                    codes, scales = h_pass(j, b)
                     nc.tensor.matmul_mx(
                         out=e_rows[:, q, :], lhsT=we_w[:, 2 * c0 : 2 * (c0 + P)].bitcast(FP4X4),
-                        lhsT_scale=we_s[:, c0 : c0 + P],
-                        rhs=h_q[j][:, m].bitcast(FP8X4), rhs_scale=h_s[j][:, m],
+                        lhsT_scale=we_s[:, c0 : c0 + P], rhs=codes, rhs_scale=scales,
                         start=(b == 0), stop=(b == HB - 1),
                     )
-            for q in range(PACK):
+            for q in range(N // P):
                 for b in range(HB):
                     n = slice(q * P, (q + 1) * P)
-                    m = slice(b * P, (b + 1) * P)
+                    codes, scales = h_pass(j, b)
                     nc.tensor.matmul_mx(
                         out=d_rows[:, q, :], lhsT=wd_q[b][:, n].bitcast(FP8X4), lhsT_scale=wd_s[b][:, n],
-                        rhs=h_q[j][:, m].bitcast(FP8X4), rhs_scale=h_s[j][:, m],
-                        start=(b == 0), stop=(b == HB - 1),
+                        rhs=codes, rhs_scale=scales, start=(b == 0), stop=(b == HB - 1),
                     )
             e_sb = ring.tile([P, PACK, P], F32, name="e_sb")
             d_sb = ring.tile([P, PACK, P], F32, name="d_sb")
             nc.scalar.copy(e_sb[:], e_rows[:])
             nc.scalar.copy(d_sb[:], d_rows[:])
-            pending[j] = (e_sb, d_sb)
+            copied[j] = (e_sb, d_sb)
 
-        def turn_back(j):
-            e_sb, d_sb = pending[j]
-            pair = PAIRS[0 if j <= EARLY else (j - EARLY) % 2]
-            e_ps = bank(pair[0], [P, N])
-            d_ps = bank(pair[1], [P, N])
-            for q in range(PACK):
-                n = slice(q * P, (q + 1) * P)
-                nc.tensor.matmul(e_ps[:, n], e_sb[:, q, :], ident[:], start=True, stop=True, is_transpose=True)
-            for q in range(PACK):
-                n = slice(q * P, (q + 1) * P)
-                nc.tensor.matmul(d_ps[:, n], e_sb[:, q, :], ident[:], start=True, stop=False, is_transpose=True)
-                nc.tensor.matmul(d_ps[:, n], d_sb[:, q, :], ident[:], start=False, stop=True, is_transpose=True)
-            pending[j] = (e_ps, d_ps)
+        def transpose(dst, src, first, last):
+            nc.tensor.matmul(dst, src, ident[:], start=first, stop=last, is_transpose=True)
+
+        def we_passes(j, dst, first):
+            for b in range(HB):
+                codes, scales = h_pass(j, b)
+                nc.tensor.matmul_mx(
+                    out=dst[:], lhsT=codes, lhsT_scale=scales,
+                    rhs=we_w[:, 2 * b * N : 2 * (b + 1) * N].bitcast(FP4X4),
+                    rhs_scale=we_s[:, b * N : (b + 1) * N],
+                    start=(first and b == 0), stop=(b == HB - 1),
+                )
 
         def second_products(j):
             pair = PAIRS[0 if j <= EARLY else (j - EARLY) % 2]
-            if j in TURNED:
-                turn_back(j)
-                return
             e_ps = bank(pair[0], [P, N])
             d_ps = bank(pair[1], [P, N])
-
-            def e_passes(bank, first, last):
-                for b in range(HB):
-                    m = slice(b * P, (b + 1) * P)
-                    nc.tensor.matmul_mx(
-                        out=bank[:], lhsT=h_q[j][:, m].bitcast(FP8X4), lhsT_scale=h_s[j][:, m],
-                        rhs=we_w[:, 2 * b * N : 2 * (b + 1) * N].bitcast(FP4X4),
-                        rhs_scale=we_s[:, b * N : (b + 1) * N],
-                        start=(first and b == 0), stop=(last and b == HB - 1),
-                    )
-
-            joined = j in JOINED
-            e_passes(e_ps, True, True)
+            sums[j] = (e_ps, d_ps)
+            if j in TURNED:
+                e_sb, d_sb = copied[j]
+                for q in range(N // P):
+                    transpose(e_ps[:, q * P : (q + 1) * P], e_sb[:, q, :], True, True)
+                for q in range(N // P):
+                    transpose(d_ps[:, q * P : (q + 1) * P], e_sb[:, q, :], True, False)
+                    transpose(d_ps[:, q * P : (q + 1) * P], d_sb[:, q, :], False, True)
+                return
+            we_passes(j, e_ps, True)
             for b in range(HB):
-                m = slice(b * P, (b + 1) * P)
+                codes, scales = h_pass(j, b)
                 nc.tensor.matmul_mx(
-                    out=d_ps[:], lhsT=h_q[j][:, m].bitcast(FP8X4), lhsT_scale=h_s[j][:, m],
+                    out=d_ps[:], lhsT=codes, lhsT_scale=scales,
                     rhs=wd_q[b][:].bitcast(FP8X4), rhs_scale=wd_s[b][:],
-                    start=(b == 0), stop=(b == HB - 1 and not joined),
+                    start=(b == 0), stop=(b == HB - 1 and j not in JOINED),
                 )
-            if joined:
-                e_passes(d_ps, False, True)
-            pending[j] = (e_ps, d_ps)
+            if j in JOINED:
+                we_passes(j, d_ps, False)
 
         def interpolate(j):
-            e_ps, d_ps = pending[j]
+            e_ps, d_ps = sums[j]
             e_part = ring.tile([P, PACK, P], F32, name="e_part", bufs=3)
             d_part = ring.tile([P, PACK, P], F32, name="d_part", bufs=3)
             if j in JOINED + TURNED:
@@ -354,39 +369,30 @@ def tile_list_sniff_correction_kernel(
                 d_part[:], gate[j][:], 1.0, d_ps[:].rearrange("j (p i) -> j i p", i=PACK),
                 ALU.add, ALU.mult,
             )
-            pending[j] = (e_part, d_part)
+            terms[j] = (e_part, d_part)
 
-        def turn(j):
-            e_part, d_part = pending[j]
-            y_ps = bank(5, [P, PACK, P])
+        def add_terms(j):
+            e_part, d_part = terms[j]
+            y_ps = bank(Y_BANK, [P, PACK, P])
             for i in range(PACK):
-                nc.tensor.matmul(y_ps[:, i, :], e_part[:, i, :], ident[:], start=True, stop=False, is_transpose=True)
-                nc.tensor.matmul(y_ps[:, i, :], d_part[:, i, :], ident[:], start=False, stop=True, is_transpose=True)
+                transpose(y_ps[:, i, :], e_part[:, i, :], True, False)
+                transpose(y_ps[:, i, :], d_part[:, i, :], False, True)
             nc.scalar.activation(y[:, :, j * P : (j + 1) * P], y_ps[:], ACT.Copy, scale=-0.5)
 
-        out_rows = out.rearrange("(p i) t -> p i t", i=PACK)
-
-        def put(page, i, j0, j1):
+        def put(i, j0, j1):
             cols = slice(j0 * P, j1 * P)
             nc.vector.tensor_tensor(
-                page[:].indirect(place[:, j0 * LIST_COLS : j1 * LIST_COLS]),
+                pages[i][:].indirect(place[:, j0 * LIST_COLS : j1 * LIST_COLS]),
                 y[:, i, cols], wg[:, cols], ALU.mult,
             )
 
-        LEAD = 5
-        units = [(j, 0) for j in range(LEAD)] + [(j, 1) for j in range(LEAD)]
-        units = units + [(j, b) for j in range(LEAD, JT) for b in range(HB)]
-
-        def advance(k):
-            hidden(*units[k])
-            ahead = k + 5 if k + 5 < WIDE_UNITS else k + 2 if k + 2 >= WIDE_UNITS else None
-            if ahead is not None and ahead < len(units):
-                first_products(*units[ahead])
-
         def second_stage(j):
-            if LATE_TURN == 0 and j > 0:
-                turn(j - 1)
-                place_tiles(j)
+            if j > 0:
+                add_terms(j - 1)
+                for i in range(PACK - 1):
+                    put(i, j - 1, j)
+            if j == SPLIT:
+                put(PACK - 1, 0, SPLIT)
             if j + 2 in TURNED:
                 turned_products(j + 2)
             if j + 1 < JT:
@@ -396,45 +402,39 @@ def tile_list_sniff_correction_kernel(
             interpolate(j)
             if j < EARLY:
                 second_products(j + 1)
-            if LATE_TURN == 1 and j > 0:
-                turn(j - 1)
-                place_tiles(j)
 
-        def place_tiles(j):
-            for i in range(PACK - 1):
-                put(pages[i], i, j - 1, j)
-
-        first_products(*units[0])
-        first_products(*units[1])
-        first_products(*units[2])
-        for m0 in range(0, P - WA_ON_VECTOR, 32):
-            round_wa(1, "A", wa_raw[1][:, :, 4 * m0 : 4 * (m0 + 32)], m0, m0 + 32)
-        if WA_ON_VECTOR:
-            round_wa(1, "V", wa_raw[1][:, :, 4 * (P - WA_ON_VECTOR) : KP], P - WA_ON_VECTOR, P)
+        for k in range(LEAD - 2):
+            first_products(k)
+        for m0 in range(0, P // 2, ROUND_ROWS):
+            round_wa(nc.scalar.copy, 1, m0, m0 + ROUND_ROWS)
+        round_wa(nc.vector.tensor_copy, 1, P // 2, P)
         quantize_wa(1)
-        first_products(*units[3])
-        first_products(*units[4])
+        for k in range(LEAD - 2, LEAD):
+            first_products(k)
         nc.sync.dma_start(out=wg[:], in_=wgo)
-        start = len(units) - 2 * EARLY
-        for k in range(len(units)):
-            advance(k)
-            if k == WD_AT[0]:
-                prepare_wd(0)
-            if k == WD_AT[1]:
-                prepare_wd(1)
-            if k == SECOND_AT:
+
+        overlap_from = len(UNITS) - HB * EARLY
+        for k in range(len(UNITS)):
+            hidden(k)
+            if k + LEAD < WIDE_UNITS:
+                first_products(k + LEAD)
+            if WIDE_UNITS <= k + 2 < len(UNITS):
+                first_products(k + 2)
+            if k in WD_AT:
+                prepare_wd(WD_AT.index(k))
+            if k == WIDE_UNITS - 1:
                 gate_of(0)
                 second_products(0)
-            if k > 0 and units[k - 1][1] == HB - 1:
-                quantize_hidden(units[k - 1][0])
-            if k >= start and (k - start) % 2 == 1:
-                second_stage((k - start) // 2)
+            if k > 0 and UNITS[k - 1][1] == HB - 1:
+                quantize_hidden(UNITS[k - 1][0])
+            if k >= overlap_from and (k - overlap_from) % HB == HB - 1:
+                second_stage((k - overlap_from) // HB)
         quantize_hidden(JT - 1)
         for j in range(EARLY, JT):
             second_stage(j)
-        turn(JT - 1)
-        for i in range(PACK - 1):
-            put(pages[i], i, JT - 1, JT)
+
+        out_rows = out.rearrange("(p i) t -> p i t", i=PACK)
+        add_terms(JT - 1)
+        for i in range(PACK):
+            put(i, SPLIT if i == PACK - 1 else JT - 1, JT)
             nc.sync.dma_start(out=out_rows[:, i, :], in_=pages[i][:])
-        put(pages[3], 3, 0, JT)
-        nc.sync.dma_start(out=out_rows[:, 3, :], in_=pages[3][:])

@@ -26,44 +26,49 @@ LIST_COLS = P // 16
 LATE = N + HB * N
 ROUND_ROWS = 32
 
-LEAD = 5
+LEAD = 8
 UNITS = [(j, b) for b in range(HB) for j in range(LEAD)] + [(j, b) for j in range(LEAD, JT) for b in range(HB)]
-WIDE_RING = (2, 3, 4, 6, 7)
-WIDE_UNITS = HB * LEAD
+WIDE_A, WIDE_B = (0, 1, 4, 5), (2, 3, 6, 7)
+WIDE_UNITS = 10
 GATE_BANK, Y_BANK = 4, 5
 PAIRS = ((6, 7), (0, 2))
 ROWS_PAIR = (1, 3)
 EARLY = 2
 JOINED = (2, 3, 4)
 TURNED = (5, 6, 7)
-WD_AT = (1, LEAD - 1)
+WA1_AT = 1
+WA1_ON = 0
+PIECES = {3: ((0, 0), (0, 1)), 7: ((1, 0),), 8: ((1, 1),), 9: ((1, 2),), 10: ((1, 3),), 11: ((2, 0),), 12: ((2, 1),)}
+WD1_AT = 9
+WDQ_AT = (9, 11)
+SECOND_AT = 11
+STEP = 1
+
 SPLIT = 2
+SPLIT_AT = 3
 SPANS = ((0, 2), (2, 4), (4, 8))
 
 AT = {
     "wa_raw1": 0,
     "wg": 0,
-    "wd_bf0": 4096,
-    "wb_raw": 8128,
-    "v_w0": 8192,
-    "wb_w": 18496,
-    "got_s": 20480,
-    "page2": 21440,
+    "got_s": 8128,
+    "tab_s": 9216,
+    "page2": 11200,
     "wd_raw0": 33024,
     "late_rows": 41216,
-    "we_w": 43264,
+    "wb_w": 42752,
+    "we_w": 44800,
     "wc_w": 46848,
     "wd_raw1": 48896,
     "wa_raw0": 40960,
-    "page1": 57088,
-    "wa_bf1": 65280,
-    "page3": 73344,
-    "tab_w": 65216,
-    "act": 86016,
-    "wd_bf1": 86016 + 2048 * WD_AT[1],
-    "wa_bf0": 118784,
-    "v_w2": 118784,
-    "v_w4": 119808,
+    "h_last": 57344,
+    "page3": 57344,
+    "act": 65536,
+    "wa_bf1": 65536 + 2048 * WA1_ON - 4032,
+    "wa_bf0": 100352,
+    "v_w0": 98304,
+    "v_w2": 100352,
+    "v_w4": 101376,
 }
 
 
@@ -93,19 +98,15 @@ def tile_list_sniff_correction_kernel(
 
         pick = held([P, S // 16], U16, "pick")
         place = held([P, S // 16], U16, "place")
-        tab_w = staged([P, T], U32, "tab_w")
-        tab_s = held([P, T], U8, "tab_s")
+        tab_w = held([P, T], U32, "tab_w")
+        tab_s = staged([P, T], U8, "tab_s")
         wb_s_raw = held([P, H], U8, "wb_s_raw")
-        wb_raw = staged([P, 2 * H], U8, "wb_raw")
+        wb_raw = held([P, 2 * H], U8, "wb_raw")
         got_s = staged([P, S], U8, "got_s")
         rows = held([P, S + H], U8, "rows")
         planes = held([P, S + H], U8, "planes")
-        late_planes = held([P, LATE], U8, "late_planes")
         v_s = planes[:, 0:S]
         wb_s = planes[:, S : S + H]
-        wc_s = late_planes[:, 0:N]
-        we_s = late_planes[:, N:LATE]
-        page0 = held([P, T2], F32, "page0")
         pages = {}
 
         ident = held([P, P], F32, "ident")
@@ -130,36 +131,33 @@ def tile_list_sniff_correction_kernel(
                 )
 
         nc.sync.dma_start(pick[:], offs)
-        load_repeated(wb_s_raw, wb_scales[0])
         load_repeated(tab_s, tab_scales[0])
-        nc.sync.dma_start(out=wb_raw[:].bitcast(I32), in_=wb_words[0].bitcast(I32))
+        load_repeated(wb_s_raw, wb_scales[0])
         load_wa(0)
         nc.sync.dma_start(
             out=tab_w[:].bitcast(I32),
             in_=tab_words[0].rearrange("p t i -> p (t i)").bitcast(I32),
         )
+        nc.sync.dma_start(out=wb_raw[:].bitcast(I32), in_=wb_words[0].bitcast(I32))
         nc.sync.dma_start(place[:], offs2)
 
-        clear_page(0, page0)
+
+        for i in range(2):
+            clear_page(i, held([P, T2], F32, "page%d" % i))
 
         nc.vector.tensor_copy(got_s[:], tab_s[:].indirect(pick[:]))
-        nc.vector.tensor_copy(rows[:, 0:S].bitcast(I32), got_s[:].bitcast(I32))
         nc.vector.tensor_copy(
             rows[:, S : S + H].rearrange("p (b t m) -> p b t m", b=HB, t=PACK),
             wb_s_raw[:].rearrange("p (b m t) -> p b t m", b=HB, t=PACK),
         )
+        nc.vector.tensor_copy(rows[:, 0:S].bitcast(I32), got_s[:].bitcast(I32))
         move_rows(planes, rows)
-        wb_w = staged([P, 2 * H], U8, "wb_w")
-        nc.vector.tensor_copy(
-            wb_w[:].bitcast(U16).rearrange("p (b t m) -> p b t m", b=HB, t=PACK),
-            wb_raw[:].bitcast(U16).rearrange("p (b m t) -> p b t m", b=HB, t=PACK),
-        )
 
         wa_raw.append(staged([P, PACK, KP], F32, "wa_raw1"))
         load_wa(1)
         clear_page(2, staged([P, T2], F32, "page2"))
 
-        wa_bf = [staged([P, KP * PACK], BF16, "wa_bf%d" % b) for b in range(HB)]
+        wa_bf = [staged([P, KP * PACK], BF16, "wa_bf0")]
         wa_q = [held([P, KP], U32, "wa_q%d" % b) for b in range(HB)]
         wa_s = [held([P, KP], U8, "wa_s%d" % b) for b in range(HB)]
         wd_q = [held([P, N], U32, "wd_q%d" % b) for b in range(HB)]
@@ -186,10 +184,13 @@ def tile_list_sniff_correction_kernel(
         round_wa(nc.scalar.copy, 0, P // 2, P)
         gather_words(*SPANS[0])
         quantize_wa(0)
-        gather_words(*SPANS[1])
-        gather_words(*SPANS[2])
-        for i in (1, 3):
-            clear_page(i, staged([P, T2], F32, "page%d" % i))
+        wb_w = staged([P, 2 * H], U8, "wb_w")
+        nc.vector.tensor_copy(
+            wb_w[:].bitcast(U16).rearrange("p (b t m) -> p b t m", b=HB, t=PACK),
+            wb_raw[:].bitcast(U16).rearrange("p (b m t) -> p b t m", b=HB, t=PACK),
+        )
+        for span in SPANS[1:]:
+            gather_words(*span)
 
         wd_raw = [staged([P, PACK, N], F32, "wd_raw%d" % b) for b in range(HB)]
         we_w = staged([P, HB * 2 * N], U8, "we_w")
@@ -202,13 +203,13 @@ def tile_list_sniff_correction_kernel(
                 in_=wd[b * KP : (b + 1) * KP, :].rearrange("(p i) n -> p i n", i=PACK),
             )
 
-        load_wd(0)
         late_rows = staged([P, LATE], U8, "late_rows")
         nc.sync.dma_start(out=late_rows[0:P:8, 0:N].bitcast(I32), in_=wc_scales[0].bitcast(I32))
         nc.sync.dma_start(
             out=late_rows[0:P:8, N:LATE].bitcast(I32).rearrange("q (a w) -> q a w", a=HB),
             in_=we_scales.bitcast(I32).rearrange("a q w -> q a w"),
         )
+        load_wd(0)
         load_wd(1)
         nc.sync.dma_start(
             out=wc_w[:].bitcast(I32),
@@ -218,19 +219,27 @@ def tile_list_sniff_correction_kernel(
             out=we_w[:].bitcast(I32).rearrange("p (a w) -> p a w", a=HB),
             in_=we_words.bitcast(I32).rearrange("a p w -> p a w"),
         )
+        late_planes = held([P, LATE], U8, "late_planes")
+        wc_s = late_planes[:, 0:N]
+        we_s = late_planes[:, N:LATE]
         move_rows(late_planes, late_rows)
 
-        def prepare_wd(b):
-            wd_bf = staged([P, N * PACK], BF16, "wd_bf%d" % b)
-            dst = wd_bf[:].rearrange("p (c u i) -> p c i u", u=4, i=PACK)
-            src = wd_raw[b][:].rearrange("p i (c u) -> p c i u", u=4)
-            for c0 in range(0, N // 4, ROUND_ROWS):
-                c1 = c0 + ROUND_ROWS
-                nc.scalar.activation(dst[:, c0:c1], src[:, c0:c1], ACT.Copy, scale=-1.0)
-            nc.vector.quantize_mx(out=wd_q[b][:].bitcast(FP8X4), scales=wd_s[b][:], in_=wd_bf[:])
+        wd_bf = [held([P, N * PACK], BF16, "wd_bf%d" % b) for b in range(HB)]
+
+        def round_wd(b, c0, c1, on_vector):
+            dst = wd_bf[b][:].rearrange("p (c u i) -> p c i u", u=4, i=PACK)[:, c0:c1]
+            src = wd_raw[b][:].rearrange("p i (c u) -> p c i u", u=4)[:, c0:c1]
+            if on_vector:
+                nc.vector.tensor_scalar(dst, src, -1.0, None, ALU.mult)
+            else:
+                nc.scalar.activation(dst, src, ACT.Copy, scale=-1.0)
+
+        def quantize_wd(b):
+            nc.vector.quantize_mx(out=wd_q[b][:].bitcast(FP8X4), scales=wd_s[b][:], in_=wd_bf[b][:])
 
         y = held([P, PACK, S], F32, "y")
-        h_bf = [held([P, HB, P, PACK], BF16, "h_bf%d" % j) for j in range(JT)]
+        h_bf = [held([P, HB, P, PACK], BF16, "h_bf%d" % j) for j in range(JT - 1)]
+        h_bf.append(staged([P, HB, P, PACK], BF16, "h_last"))
         h_q = [held([P, HB * P], U32, "h_q%d" % j) for j in range(JT)]
         h_s = [held([P, HB * P], U8, "h_s%d" % j) for j in range(JT)]
         unit_parts, gate, copied, sums, terms = {}, {}, {}, {}, {}
@@ -245,8 +254,8 @@ def tile_list_sniff_correction_kernel(
         def first_products(k):
             j, b = UNITS[k]
             codes, scales = table_tile(j)
-            a_ps = bank(k % 2, [P, PACK, P])
-            b_ps = bank(WIDE_RING[k % LEAD] if k < WIDE_UNITS else 2 + k % 2, [P, PACK, P])
+            a_ps = bank(WIDE_A[k % 4] if k < WIDE_UNITS else k % 2, [P, PACK, P])
+            b_ps = bank(WIDE_B[k % 4] if k < WIDE_UNITS else 2 + k % 2, [P, PACK, P])
             for t in range(PACK):
                 m = slice(t * P, (t + 1) * P)
                 nc.tensor.matmul_mx(
@@ -375,8 +384,8 @@ def tile_list_sniff_correction_kernel(
             e_part, d_part = terms[j]
             y_ps = bank(Y_BANK, [P, PACK, P])
             for i in range(PACK):
-                transpose(y_ps[:, i, :], e_part[:, i, :], True, False)
-                transpose(y_ps[:, i, :], d_part[:, i, :], False, True)
+                transpose(y_ps[:, i, :], d_part[:, i, :], True, False)
+                transpose(y_ps[:, i, :], e_part[:, i, :], False, True)
             nc.scalar.activation(y[:, :, j * P : (j + 1) * P], y_ps[:], ACT.Copy, scale=-0.5)
 
         def put(i, j0, j1):
@@ -391,7 +400,7 @@ def tile_list_sniff_correction_kernel(
                 add_terms(j - 1)
                 for i in range(PACK - 1):
                     put(i, j - 1, j)
-            if j == SPLIT:
+            if j == SPLIT_AT:
                 put(PACK - 1, 0, SPLIT)
             if j + 2 in TURNED:
                 turned_products(j + 2)
@@ -403,33 +412,40 @@ def tile_list_sniff_correction_kernel(
             if j < EARLY:
                 second_products(j + 1)
 
-        for k in range(LEAD - 2):
-            first_products(k)
-        for m0 in range(0, P // 2, ROUND_ROWS):
-            round_wa(nc.scalar.copy, 1, m0, m0 + ROUND_ROWS)
-        round_wa(nc.vector.tensor_copy, 1, P // 2, P)
-        quantize_wa(1)
-        for k in range(LEAD - 2, LEAD):
-            first_products(k)
-        nc.sync.dma_start(out=wg[:], in_=wgo)
-
-        overlap_from = len(UNITS) - HB * EARLY
-        for k in range(len(UNITS)):
-            hidden(k)
-            if k + LEAD < WIDE_UNITS:
-                first_products(k + LEAD)
-            if WIDE_UNITS <= k + 2 < len(UNITS):
+        for k in range(-2, len(UNITS)):
+            if k >= 0:
+                hidden(k)
+            if k + 2 < len(UNITS):
                 first_products(k + 2)
-            if k in WD_AT:
-                prepare_wd(WD_AT.index(k))
-            if k == WIDE_UNITS - 1:
+            if k + 2 == min(PIECES):
+                wa_bf.append(staged([P, KP * PACK], BF16, "wa_bf1"))
+            for block, piece in PIECES.get(k + 2, ()):
+                c0 = piece * ROUND_ROWS
+                if block == 0:
+                    round_wa(nc.scalar.copy, 1, c0, c0 + ROUND_ROWS)
+                else:
+                    round_wd(block - 1, c0, c0 + ROUND_ROWS, False)
+            if k == WA1_AT:
+                round_wa(nc.vector.tensor_copy, 1, P // 2, P)
+            if k == WA1_AT + 1:
+                quantize_wa(1)
+                nc.sync.dma_start(out=wg[:], in_=wgo)
+            if k == WD1_AT:
+                round_wd(1, P // 2, P, True)
+            if k in WDQ_AT:
+                quantize_wd(WDQ_AT.index(k))
+            if k == SECOND_AT:
                 gate_of(0)
-                second_products(0)
             if k > 0 and UNITS[k - 1][1] == HB - 1:
                 quantize_hidden(UNITS[k - 1][0])
-            if k >= overlap_from and (k - overlap_from) % HB == HB - 1:
-                second_stage((k - overlap_from) // HB)
+            if k == SECOND_AT:
+                second_products(0)
+            for j in range(EARLY):
+                if k == SECOND_AT + STEP * (j + 1):
+                    second_stage(j)
         quantize_hidden(JT - 1)
+        pages[PACK - 1] = staged([P, T2], F32, "page3")
+        nc.gpsimd.memset(pages[PACK - 1][:].bitcast(I32), 0)
         for j in range(EARLY, JT):
             second_stage(j)
 

@@ -29,19 +29,18 @@ ROUND_ROWS = 32
 LEAD = 8
 UNITS = [(j, b) for b in range(HB) for j in range(LEAD)] + [(j, b) for j in range(LEAD, JT) for b in range(HB)]
 WIDE_A, WIDE_B = (0, 1, 4, 5), (2, 3, 6, 7)
-WIDE_UNITS = 10
+WIDE_UNITS = 12
 GATE_BANK, Y_BANK = 4, 5
 PAIRS = ((6, 7), (0, 2))
 ROWS_PAIR = (1, 3)
 EARLY = 2
 JOINED = (2, 3, 4)
 TURNED = (5, 6, 7)
-WA1_AT = 1
-WA1_ON = 0
-PIECES = {3: ((0, 0), (0, 1)), 7: ((1, 0),), 8: ((1, 1),), 9: ((1, 2),), 10: ((1, 3),), 11: ((2, 0),), 12: ((2, 1),)}
-WD1_AT = 9
-WDQ_AT = (9, 11)
-SECOND_AT = 11
+WA1_AT = 2
+WD_COLS = 256
+HELD_Q = 3
+QN = 3
+SECOND_AT = 12
 STEP = 1
 
 SPLIT = 2
@@ -49,24 +48,26 @@ SPLIT_AT = 3
 SPANS = ((0, 2), (2, 4), (4, 8))
 
 AT = {
-    "wa_raw1": 0,
+    "wa_raw11": 0,
     "wg": 0,
-    "got_s": 8128,
+    "got_s": 4032,
+    "wa_raw10": 4992,
+    "act2": 5056,
     "tab_s": 9216,
     "page2": 11200,
-    "wd_raw0": 33024,
-    "late_rows": 41216,
-    "wb_w": 42752,
-    "we_w": 44800,
-    "wc_w": 46848,
-    "wd_raw1": 48896,
-    "wa_raw0": 40960,
+    "wd_raw0": 24640,
+    "wa_raw00": 32768,
+    "late_rows": 32832,
+    "wb_w": 34368,
+    "we_w": 36416,
+    "wc_w": 38464,
+    "wd_raw1": 40896,
+    "wd_q0": 40896 + 64,
     "h_last": 57344,
     "page3": 57344,
     "act": 65536,
-    "wa_bf1": 65536 + 2048 * WA1_ON - 4032,
-    "wa_bf0": 100352,
     "v_w0": 98304,
+    "wa_bf0": 100352,
     "v_w2": 100352,
     "v_w4": 101376,
 }
@@ -104,19 +105,19 @@ def tile_list_sniff_correction_kernel(
         wb_raw = held([P, 2 * H], U8, "wb_raw")
         got_s = staged([P, S], U8, "got_s")
         rows = held([P, S + H], U8, "rows")
-        planes = held([P, S + H], U8, "planes")
-        v_s = planes[:, 0:S]
-        wb_s = planes[:, S : S + H]
         pages = {}
 
-        ident = held([P, P], F32, "ident")
-        make_identity(nc, ident[:])
 
         wa_rows = wa.rearrange("(p i) c -> p i c", i=PACK)
-        wa_raw = [staged([P, PACK, KP], F32, "wa_raw0")]
+        wa_raw = {}
 
-        def load_wa(b):
-            nc.sync.dma_start(out=wa_raw[b][:], in_=wa_rows[:, :, b * KP : (b + 1) * KP])
+        def load_wa(b, half, halves):
+            cols = halves * KP // 2
+            raw = staged([P, PACK, cols], F32, "wa_raw%d%d" % (b, half))
+            c0 = b * KP + half * KP // 2
+            nc.sync.dma_start(out=raw[:], in_=wa_rows[:, :, c0 : c0 + cols])
+            for h in range(halves):
+                wa_raw[b, half + h] = raw[:, :, h * KP // 2 : (h + 1) * KP // 2]
 
         def load_repeated(tile, scales):
             nc.sync.dma_start(
@@ -133,7 +134,7 @@ def tile_list_sniff_correction_kernel(
         nc.sync.dma_start(pick[:], offs)
         load_repeated(tab_s, tab_scales[0])
         load_repeated(wb_s_raw, wb_scales[0])
-        load_wa(0)
+        load_wa(0, 0, 2)
         nc.sync.dma_start(
             out=tab_w[:].bitcast(I32),
             in_=tab_words[0].rearrange("p t i -> p (t i)").bitcast(I32),
@@ -151,21 +152,23 @@ def tile_list_sniff_correction_kernel(
             wb_s_raw[:].rearrange("p (b m t) -> p b t m", b=HB, t=PACK),
         )
         nc.vector.tensor_copy(rows[:, 0:S].bitcast(I32), got_s[:].bitcast(I32))
+        planes = held([P, S + H], U8, "planes")
+        v_s = planes[:, 0:S]
+        wb_s = planes[:, S : S + H]
         move_rows(planes, rows)
+        load_wa(1, 0, 1)
+        load_wa(1, 1, 1)
 
-        wa_raw.append(staged([P, PACK, KP], F32, "wa_raw1"))
-        load_wa(1)
         clear_page(2, staged([P, T2], F32, "page2"))
 
         wa_bf = [staged([P, KP * PACK], BF16, "wa_bf0")]
         wa_q = [held([P, KP], U32, "wa_q%d" % b) for b in range(HB)]
         wa_s = [held([P, KP], U8, "wa_s%d" % b) for b in range(HB)]
-        wd_q = [held([P, N], U32, "wd_q%d" % b) for b in range(HB)]
         wd_s = [held([P, N], U8, "wd_s%d" % b) for b in range(HB)]
 
-        def round_wa(copy, b, m0, m1):
-            dst = wa_bf[b][:].rearrange("p (t m i) -> p m i t", t=PACK, i=PACK)[:, m0:m1]
-            src = wa_raw[b][:, :, PACK * m0 : PACK * m1].rearrange("p i (m t) -> p m i t", t=PACK)
+        def round_wa(copy, b, half):
+            dst = wa_bf[b][:].rearrange("p (t m i) -> p m i t", t=PACK, i=PACK)[:, half * P // 2 : (half + 1) * P // 2]
+            src = wa_raw[b, half].rearrange("p i (m t) -> p m i t", t=PACK)
             copy(dst, src)
 
         def quantize_wa(b):
@@ -180,8 +183,8 @@ def tile_list_sniff_correction_kernel(
             nc.vector.tensor_copy(words[:], tab_w[:].indirect(pick[:, j0 * LIST_COLS : j1 * LIST_COLS]))
             v_w.extend(words[:, c : c + P] for c in range(0, (j1 - j0) * P, P))
 
-        round_wa(nc.scalar.copy, 0, 0, P // 2)
-        round_wa(nc.scalar.copy, 0, P // 2, P)
+        round_wa(nc.scalar.copy, 0, 0)
+        round_wa(nc.scalar.copy, 0, 1)
         gather_words(*SPANS[0])
         quantize_wa(0)
         wb_w = staged([P, 2 * H], U8, "wb_w")
@@ -191,6 +194,7 @@ def tile_list_sniff_correction_kernel(
         )
         for span in SPANS[1:]:
             gather_words(*span)
+        wa_bf.append(held([P, KP * PACK], BF16, "wa_bf1"))
 
         wd_raw = [staged([P, PACK, N], F32, "wd_raw%d" % b) for b in range(HB)]
         we_w = staged([P, HB * 2 * N], U8, "we_w")
@@ -203,14 +207,14 @@ def tile_list_sniff_correction_kernel(
                 in_=wd[b * KP : (b + 1) * KP, :].rearrange("(p i) n -> p i n", i=PACK),
             )
 
+        load_wd(0)
+        load_wd(1)
         late_rows = staged([P, LATE], U8, "late_rows")
         nc.sync.dma_start(out=late_rows[0:P:8, 0:N].bitcast(I32), in_=wc_scales[0].bitcast(I32))
         nc.sync.dma_start(
             out=late_rows[0:P:8, N:LATE].bitcast(I32).rearrange("q (a w) -> q a w", a=HB),
             in_=we_scales.bitcast(I32).rearrange("a q w -> q a w"),
         )
-        load_wd(0)
-        load_wd(1)
         nc.sync.dma_start(
             out=wc_w[:].bitcast(I32),
             in_=wc_words[0].rearrange("p c i -> p (c i)").bitcast(I32),
@@ -224,23 +228,28 @@ def tile_list_sniff_correction_kernel(
         we_s = late_planes[:, N:LATE]
         move_rows(late_planes, late_rows)
 
-        wd_bf = [held([P, N * PACK], BF16, "wd_bf%d" % b) for b in range(HB)]
+        ident = held([P, P], F32, "ident")
+        make_identity(nc, ident[:])
+        wd_bf = [held([P, N, PACK], BF16, "wd_bf%d" % b) for b in range(HB)]
+        for b in range(HB):
+            for c0 in range(0, N, WD_COLS):
+                nc.gpsimd.tensor_scalar(
+                    wd_bf[b][:, c0 : c0 + WD_COLS],
+                    wd_raw[b][:].rearrange("p i n -> p n i")[:, c0 : c0 + WD_COLS], -1.0, 0.0, ALU.mult, ALU.add,
+                )
 
-        def round_wd(b, c0, c1, on_vector):
-            dst = wd_bf[b][:].rearrange("p (c u i) -> p c i u", u=4, i=PACK)[:, c0:c1]
-            src = wd_raw[b][:].rearrange("p i (c u) -> p c i u", u=4)[:, c0:c1]
-            if on_vector:
-                nc.vector.tensor_scalar(dst, src, -1.0, None, ALU.mult)
-            else:
-                nc.scalar.activation(dst, src, ACT.Copy, scale=-1.0)
+        wd_q = [staged([P, N], U32, "wd_q0"), held([P, N], U32, "wd_q1")]
 
         def quantize_wd(b):
-            nc.vector.quantize_mx(out=wd_q[b][:].bitcast(FP8X4), scales=wd_s[b][:], in_=wd_bf[b][:])
+            nc.vector.quantize_mx(out=wd_q[b][:].bitcast(FP8X4), scales=wd_s[b][:], in_=wd_bf[b][:].rearrange("p n i -> p (n i)"))
 
         y = held([P, PACK, S], F32, "y")
         h_bf = [held([P, HB, P, PACK], BF16, "h_bf%d" % j) for j in range(JT - 1)]
         h_bf.append(staged([P, HB, P, PACK], BF16, "h_last"))
-        h_q = [held([P, HB * P], U32, "h_q%d" % j) for j in range(JT)]
+        h_q = [
+            stage.tile([P, HB * P], U32, name="h_q%d" % j, align_bytes=64, offset=AT["wd_raw1"] + 2112 + 1024 * j)
+            if j < HELD_Q else held([P, HB * P], U32, "h_q%d" % j) for j in range(JT)
+        ]
         h_s = [held([P, HB * P], U8, "h_s%d" % j) for j in range(JT)]
         unit_parts, gate, copied, sums, terms = {}, {}, {}, {}, {}
 
@@ -269,7 +278,7 @@ def tile_list_sniff_correction_kernel(
                     lhsT_scale=wb_s[:, c0 : c0 + P],
                     rhs=codes, rhs_scale=scales, start=True, stop=True,
                 )
-            act = stage.tile([P, P, PACK], F32, name="act%d" % k, align_bytes=64, offset=AT["act"] + 2048 * k)
+            act = stage.tile([P, P, PACK], F32, name="act%d" % k, align_bytes=64, offset=AT["act2"] if k == 2 else AT["act"] + 2048 * k)
             nc.scalar.activation(act[:], a_ps[:].rearrange("p t j -> p j t"), ACT.Silu)
             unit_parts[k] = (b_ps, act)
 
@@ -417,33 +426,29 @@ def tile_list_sniff_correction_kernel(
                 hidden(k)
             if k + 2 < len(UNITS):
                 first_products(k + 2)
-            if k + 2 == min(PIECES):
-                wa_bf.append(staged([P, KP * PACK], BF16, "wa_bf1"))
-            for block, piece in PIECES.get(k + 2, ()):
-                c0 = piece * ROUND_ROWS
-                if block == 0:
-                    round_wa(nc.scalar.copy, 1, c0, c0 + ROUND_ROWS)
-                else:
-                    round_wd(block - 1, c0, c0 + ROUND_ROWS, False)
+            if k == -1:
+                round_wa(nc.scalar.copy, 1, 0)
+            if k == WA1_AT - 1:
+                round_wa(nc.vector.tensor_copy, 1, 1)
             if k == WA1_AT:
-                round_wa(nc.vector.tensor_copy, 1, P // 2, P)
-            if k == WA1_AT + 1:
                 quantize_wa(1)
                 nc.sync.dma_start(out=wg[:], in_=wgo)
-            if k == WD1_AT:
-                round_wd(1, P // 2, P, True)
-            if k in WDQ_AT:
-                quantize_wd(WDQ_AT.index(k))
             if k == SECOND_AT:
                 gate_of(0)
-            if k > 0 and UNITS[k - 1][1] == HB - 1:
-                quantize_hidden(UNITS[k - 1][0])
-            if k == SECOND_AT:
+                quantize_hidden(0)
+                quantize_wd(0)
+                quantize_wd(1)
                 second_products(0)
+                for j in range(1, QN):
+                    quantize_hidden(j)
             for j in range(EARLY):
                 if k == SECOND_AT + STEP * (j + 1):
                     second_stage(j)
-        quantize_hidden(JT - 1)
+        for j in range(QN, JT):
+            quantize_hidden(j)
+        for j in range(EARLY):
+            if len(UNITS) <= SECOND_AT + STEP * (j + 1):
+                second_stage(j)
         pages[PACK - 1] = staged([P, T2], F32, "page3")
         nc.gpsimd.memset(pages[PACK - 1][:].bitcast(I32), 0)
         for j in range(EARLY, JT):

@@ -29,22 +29,24 @@ ROUND_ROWS = 32
 LEAD = 8
 UNITS = [(j, b) for b in range(HB) for j in range(LEAD)] + [(j, b) for j in range(LEAD, JT) for b in range(HB)]
 WIDE_A, WIDE_B = (0, 1, 4, 5), (2, 3, 6, 7)
-WIDE_UNITS = 12
+WIDE_UNITS = 10
 GATE_BANK, Y_BANK = 4, 5
 PAIRS = ((6, 7), (0, 2))
 ROWS_PAIR = (1, 3)
 EARLY = 2
 JOINED = (2, 3, 4)
-TURNED = (5, 6, 7)
+TURNED = (6, 7)
 WA1_AT = 2
 WD_COLS = 256
+WD1_FROM = 8
+WD1_ON = 4
+WD1_V = 1
+WD1_V_AT = 8
 HELD_Q = 3
-QN = 3
-SECOND_AT = 12
-STEP = 1
+Q_AT = 9
+SECOND_AT = 9
+STEP = 2
 
-SPLIT = 2
-SPLIT_AT = 3
 SPANS = ((0, 2), (2, 4), (4, 8))
 
 AT = {
@@ -53,8 +55,6 @@ AT = {
     "got_s": 4032,
     "wa_raw10": 4992,
     "act2": 5056,
-    "tab_s": 9216,
-    "page2": 11200,
     "wd_raw0": 24640,
     "wa_raw00": 32768,
     "late_rows": 32832,
@@ -62,11 +62,13 @@ AT = {
     "we_w": 36416,
     "wc_w": 38464,
     "wd_raw1": 40896,
-    "wd_q0": 40896 + 64,
+    "wd_q0": 24640,
+    "wd_bf1": 65600 + 2048 * WD1_ON,
     "h_last": 57344,
-    "page3": 57344,
-    "act": 65536,
-    "v_w0": 98304,
+    "page2": 57344 + 64 - 8192,
+    "page3": 57344 + 64,
+    "act": 65536 + 64,
+    "v_w0": 98368,
     "wa_bf0": 100352,
     "v_w2": 100352,
     "v_w4": 101376,
@@ -100,7 +102,7 @@ def tile_list_sniff_correction_kernel(
         pick = held([P, S // 16], U16, "pick")
         place = held([P, S // 16], U16, "place")
         tab_w = held([P, T], U32, "tab_w")
-        tab_s = staged([P, T], U8, "tab_s")
+        tab_s = held([P, T], U8, "tab_s")
         wb_s_raw = held([P, H], U8, "wb_s_raw")
         wb_raw = held([P, 2 * H], U8, "wb_raw")
         got_s = staged([P, S], U8, "got_s")
@@ -159,7 +161,6 @@ def tile_list_sniff_correction_kernel(
         load_wa(1, 0, 1)
         load_wa(1, 1, 1)
 
-        clear_page(2, staged([P, T2], F32, "page2"))
 
         wa_bf = [staged([P, KP * PACK], BF16, "wa_bf0")]
         wa_q = [held([P, KP], U32, "wa_q%d" % b) for b in range(HB)]
@@ -207,14 +208,14 @@ def tile_list_sniff_correction_kernel(
                 in_=wd[b * KP : (b + 1) * KP, :].rearrange("(p i) n -> p i n", i=PACK),
             )
 
-        load_wd(0)
-        load_wd(1)
         late_rows = staged([P, LATE], U8, "late_rows")
         nc.sync.dma_start(out=late_rows[0:P:8, 0:N].bitcast(I32), in_=wc_scales[0].bitcast(I32))
         nc.sync.dma_start(
             out=late_rows[0:P:8, N:LATE].bitcast(I32).rearrange("q (a w) -> q a w", a=HB),
             in_=we_scales.bitcast(I32).rearrange("a q w -> q a w"),
         )
+        load_wd(0)
+        load_wd(1)
         nc.sync.dma_start(
             out=wc_w[:].bitcast(I32),
             in_=wc_words[0].rearrange("p c i -> p (c i)").bitcast(I32),
@@ -230,13 +231,21 @@ def tile_list_sniff_correction_kernel(
 
         ident = held([P, P], F32, "ident")
         make_identity(nc, ident[:])
-        wd_bf = [held([P, N, PACK], BF16, "wd_bf%d" % b) for b in range(HB)]
-        for b in range(HB):
+        wd_bf = [held([P, N, PACK], BF16, "wd_bf0")]
+        for b in range(1):
             for c0 in range(0, N, WD_COLS):
                 nc.gpsimd.tensor_scalar(
                     wd_bf[b][:, c0 : c0 + WD_COLS],
                     wd_raw[b][:].rearrange("p i n -> p n i")[:, c0 : c0 + WD_COLS], -1.0, 0.0, ALU.mult, ALU.add,
                 )
+
+        def round_wd(b, c0, c1, on_vector=False):
+            dst = wd_bf[b][:].rearrange("p (c u) i -> p c i u", u=4)[:, c0:c1]
+            src = wd_raw[b][:].rearrange("p i (c u) -> p c i u", u=4)[:, c0:c1]
+            if on_vector:
+                nc.vector.tensor_scalar(dst, src, -1.0, None, ALU.mult)
+            else:
+                nc.scalar.activation(dst, src, ACT.Copy, scale=-1.0)
 
         wd_q = [staged([P, N], U32, "wd_q0"), held([P, N], U32, "wd_q1")]
 
@@ -247,7 +256,7 @@ def tile_list_sniff_correction_kernel(
         h_bf = [held([P, HB, P, PACK], BF16, "h_bf%d" % j) for j in range(JT - 1)]
         h_bf.append(staged([P, HB, P, PACK], BF16, "h_last"))
         h_q = [
-            stage.tile([P, HB * P], U32, name="h_q%d" % j, align_bytes=64, offset=AT["wd_raw1"] + 2112 + 1024 * j)
+            stage.tile([P, HB * P], U32, name="h_q%d" % j, align_bytes=64, offset=AT["wd_raw0"] + 2048 + 1024 * j)
             if j < HELD_Q else held([P, HB * P], U32, "h_q%d" % j) for j in range(JT)
         ]
         h_s = [held([P, HB * P], U8, "h_s%d" % j) for j in range(JT)]
@@ -407,10 +416,15 @@ def tile_list_sniff_correction_kernel(
         def second_stage(j):
             if j > 0:
                 add_terms(j - 1)
+                if j - 1 == EARLY:
+                    put(2, 0, EARLY)
                 for i in range(PACK - 1):
-                    put(i, j - 1, j)
-            if j == SPLIT_AT:
-                put(PACK - 1, 0, SPLIT)
+                    if i < 2 or j > EARLY:
+                        put(i, j - 1, j)
+                if j - 1 == EARLY + 1:
+                    put(3, 0, 1)
+                if j == JT - 1:
+                    put(3, j - 1, j)
             if j + 2 in TURNED:
                 turned_products(j + 2)
             if j + 1 < JT:
@@ -421,11 +435,19 @@ def tile_list_sniff_correction_kernel(
             if j < EARLY:
                 second_products(j + 1)
 
+        done = []
         for k in range(-2, len(UNITS)):
             if k >= 0:
                 hidden(k)
             if k + 2 < len(UNITS):
                 first_products(k + 2)
+            if k + 2 == WD1_FROM:
+                wd_bf.append(staged([P, N, PACK], BF16, "wd_bf1"))
+            if WD1_FROM <= k + 2 < WD1_FROM + 4 - WD1_V:
+                c0 = (k + 2 - WD1_FROM) * ROUND_ROWS
+                round_wd(1, c0, c0 + ROUND_ROWS)
+            if k == WD1_V_AT and WD1_V:
+                round_wd(1, (4 - WD1_V) * ROUND_ROWS, P, True)
             if k == -1:
                 round_wa(nc.scalar.copy, 1, 0)
             if k == WA1_AT - 1:
@@ -433,29 +455,39 @@ def tile_list_sniff_correction_kernel(
             if k == WA1_AT:
                 quantize_wa(1)
                 nc.sync.dma_start(out=wg[:], in_=wgo)
-            if k == SECOND_AT:
-                gate_of(0)
+            if k == Q_AT:
                 quantize_hidden(0)
+                done.append(0)
                 quantize_wd(0)
                 quantize_wd(1)
+            if k == SECOND_AT:
+                gate_of(0)
                 second_products(0)
-                for j in range(1, QN):
-                    quantize_hidden(j)
+            if k >= Q_AT:
+                for j in range(JT - 1):
+                    if j not in done and LEAD + j < k:
+                        quantize_hidden(j)
+                        done.append(j)
             for j in range(EARLY):
                 if k == SECOND_AT + STEP * (j + 1):
                     second_stage(j)
-        for j in range(QN, JT):
-            quantize_hidden(j)
+        for j in range(JT):
+            if j not in done:
+                quantize_hidden(j)
+        for i in (2, 3):
+            pages[i] = staged([P, T2], F32, "page%d" % i)
+            nc.gpsimd.memset(pages[i][:].bitcast(I32), 0)
         for j in range(EARLY):
             if len(UNITS) <= SECOND_AT + STEP * (j + 1):
                 second_stage(j)
-        pages[PACK - 1] = staged([P, T2], F32, "page3")
-        nc.gpsimd.memset(pages[PACK - 1][:].bitcast(I32), 0)
         for j in range(EARLY, JT):
             second_stage(j)
 
         out_rows = out.rearrange("(p i) t -> p i t", i=PACK)
         add_terms(JT - 1)
-        for i in range(PACK):
-            put(i, SPLIT if i == PACK - 1 else JT - 1, JT)
-            nc.sync.dma_start(out=out_rows[:, i, :], in_=pages[i][:])
+        for i in (0, 1, 3, 2):
+            put(i, JT - 1, JT)
+            if i < 3:
+                nc.sync.dma_start(out=out_rows[:, i, :], in_=pages[i][:])
+        put(3, 1, JT - 2)
+        nc.sync.dma_start(out=out_rows[:, 3, :], in_=pages[3][:])

@@ -29,7 +29,7 @@ ROUND_ROWS = 32
 LEAD = 8
 UNITS = [(j, b) for b in range(HB) for j in range(LEAD)] + [(j, b) for j in range(LEAD, JT) for b in range(HB)]
 WIDE_A, WIDE_B = (0, 1, 4, 5), (2, 3, 6, 7)
-WIDE_UNITS = 10
+WIDE_UNITS = 12
 GATE_BANK, Y_BANK = 4, 5
 PAIRS = ((6, 7), (0, 2))
 ROWS_PAIR = (1, 3)
@@ -37,14 +37,12 @@ EARLY = 2
 JOINED = (2, 3, 4)
 TURNED = (6, 7)
 WA1_AT = 2
-WD_COLS = 256
-WD1_FROM = 8
-WD1_ON = 4
-WD1_V = 1
+WD_FROM = 6
+WD_ON = (2, 5)
+WD1_V = 2
 WD1_V_AT = 8
-HELD_Q = 3
-Q_AT = 9
-SECOND_AT = 9
+Q_AT = 10
+SECOND_AT = 11
 STEP = 2
 
 SPANS = ((0, 2), (2, 4), (4, 8))
@@ -62,16 +60,16 @@ AT = {
     "we_w": 36416,
     "wc_w": 38464,
     "wd_raw1": 40896,
-    "wd_q0": 24640,
-    "wd_bf1": 65600 + 2048 * WD1_ON,
-    "h_last": 57344,
-    "page2": 57344 + 64 - 8192,
-    "page3": 57344 + 64,
-    "act": 65536 + 64,
-    "v_w0": 98368,
-    "wa_bf0": 100352,
-    "v_w2": 100352,
-    "v_w4": 101376,
+    "wd_bf0": 67584 + 2048 * WD_ON[0],
+    "wd_bf1": 67584 + 2048 * WD_ON[1],
+    "page2": 49152,
+    "tab_s": 49152 + 8192 - 64,
+    "page3": 49152 + 8192 + 2048 - 128,
+    "act": 67584,
+    "v_w0": 100352,
+    "wa_bf0": 101376,
+    "v_w2": 101376,
+    "v_w4": 102400,
 }
 
 
@@ -102,7 +100,7 @@ def tile_list_sniff_correction_kernel(
         pick = held([P, S // 16], U16, "pick")
         place = held([P, S // 16], U16, "place")
         tab_w = held([P, T], U32, "tab_w")
-        tab_s = held([P, T], U8, "tab_s")
+        tab_s = staged([P, T], U8, "tab_s")
         wb_s_raw = held([P, H], U8, "wb_s_raw")
         wb_raw = held([P, 2 * H], U8, "wb_raw")
         got_s = staged([P, S], U8, "got_s")
@@ -160,6 +158,8 @@ def tile_list_sniff_correction_kernel(
         move_rows(planes, rows)
         load_wa(1, 0, 1)
         load_wa(1, 1, 1)
+        for i in (2, 3):
+            clear_page(i, staged([P, T2], F32, "page%d" % i))
 
 
         wa_bf = [staged([P, KP * PACK], BF16, "wa_bf0")]
@@ -231,15 +231,11 @@ def tile_list_sniff_correction_kernel(
 
         ident = held([P, P], F32, "ident")
         make_identity(nc, ident[:])
-        wd_bf = [held([P, N, PACK], BF16, "wd_bf0")]
-        for b in range(1):
-            for c0 in range(0, N, WD_COLS):
-                nc.gpsimd.tensor_scalar(
-                    wd_bf[b][:, c0 : c0 + WD_COLS],
-                    wd_raw[b][:].rearrange("p i n -> p n i")[:, c0 : c0 + WD_COLS], -1.0, 0.0, ALU.mult, ALU.add,
-                )
+        wd_bf = {}
 
         def round_wd(b, c0, c1, on_vector=False):
+            if b not in wd_bf:
+                wd_bf[b] = staged([P, N, PACK], BF16, "wd_bf%d" % b)
             dst = wd_bf[b][:].rearrange("p (c u) i -> p c i u", u=4)[:, c0:c1]
             src = wd_raw[b][:].rearrange("p i (c u) -> p c i u", u=4)[:, c0:c1]
             if on_vector:
@@ -247,18 +243,14 @@ def tile_list_sniff_correction_kernel(
             else:
                 nc.scalar.activation(dst, src, ACT.Copy, scale=-1.0)
 
-        wd_q = [staged([P, N], U32, "wd_q0"), held([P, N], U32, "wd_q1")]
+        wd_q = [held([P, N], U32, "wd_q%d" % b) for b in range(HB)]
 
         def quantize_wd(b):
             nc.vector.quantize_mx(out=wd_q[b][:].bitcast(FP8X4), scales=wd_s[b][:], in_=wd_bf[b][:].rearrange("p n i -> p (n i)"))
 
         y = held([P, PACK, S], F32, "y")
-        h_bf = [held([P, HB, P, PACK], BF16, "h_bf%d" % j) for j in range(JT - 1)]
-        h_bf.append(staged([P, HB, P, PACK], BF16, "h_last"))
-        h_q = [
-            stage.tile([P, HB * P], U32, name="h_q%d" % j, align_bytes=64, offset=AT["wd_raw0"] + 2048 + 1024 * j)
-            if j < HELD_Q else held([P, HB * P], U32, "h_q%d" % j) for j in range(JT)
-        ]
+        h_bf = [held([P, HB, P, PACK], BF16, "h_bf%d" % j) for j in range(JT)]
+        h_q = [held([P, HB * P], U32, "h_q%d" % j) for j in range(JT)]
         h_s = [held([P, HB * P], U8, "h_s%d" % j) for j in range(JT)]
         unit_parts, gate, copied, sums, terms = {}, {}, {}, {}, {}
 
@@ -416,12 +408,9 @@ def tile_list_sniff_correction_kernel(
         def second_stage(j):
             if j > 0:
                 add_terms(j - 1)
-                if j - 1 == EARLY:
-                    put(2, 0, EARLY)
                 for i in range(PACK - 1):
-                    if i < 2 or j > EARLY:
-                        put(i, j - 1, j)
-                if j - 1 == EARLY + 1:
+                    put(i, j - 1, j)
+                if j == 1:
                     put(3, 0, 1)
                 if j == JT - 1:
                     put(3, j - 1, j)
@@ -435,17 +424,14 @@ def tile_list_sniff_correction_kernel(
             if j < EARLY:
                 second_products(j + 1)
 
-        done = []
         for k in range(-2, len(UNITS)):
             if k >= 0:
                 hidden(k)
             if k + 2 < len(UNITS):
                 first_products(k + 2)
-            if k + 2 == WD1_FROM:
-                wd_bf.append(staged([P, N, PACK], BF16, "wd_bf1"))
-            if WD1_FROM <= k + 2 < WD1_FROM + 4 - WD1_V:
-                c0 = (k + 2 - WD1_FROM) * ROUND_ROWS
-                round_wd(1, c0, c0 + ROUND_ROWS)
+            if WD_FROM <= k + 2 < WD_FROM + 8 - WD1_V:
+                b, piece = divmod(k + 2 - WD_FROM, 4)
+                round_wd(b, piece * ROUND_ROWS, (piece + 1) * ROUND_ROWS)
             if k == WD1_V_AT and WD1_V:
                 round_wd(1, (4 - WD1_V) * ROUND_ROWS, P, True)
             if k == -1:
@@ -455,31 +441,19 @@ def tile_list_sniff_correction_kernel(
             if k == WA1_AT:
                 quantize_wa(1)
                 nc.sync.dma_start(out=wg[:], in_=wgo)
-            if k == Q_AT:
-                quantize_hidden(0)
-                done.append(0)
+            if k == WD_FROM + 2:
                 quantize_wd(0)
+            if k == Q_AT:
                 quantize_wd(1)
+            if k > LEAD:
+                quantize_hidden(k - 1 - LEAD)
             if k == SECOND_AT:
                 gate_of(0)
                 second_products(0)
-            if k >= Q_AT:
-                for j in range(JT - 1):
-                    if j not in done and LEAD + j < k:
-                        quantize_hidden(j)
-                        done.append(j)
             for j in range(EARLY):
                 if k == SECOND_AT + STEP * (j + 1):
                     second_stage(j)
-        for j in range(JT):
-            if j not in done:
-                quantize_hidden(j)
-        for i in (2, 3):
-            pages[i] = staged([P, T2], F32, "page%d" % i)
-            nc.gpsimd.memset(pages[i][:].bitcast(I32), 0)
-        for j in range(EARLY):
-            if len(UNITS) <= SECOND_AT + STEP * (j + 1):
-                second_stage(j)
+        quantize_hidden(JT - 1)
         for j in range(EARLY, JT):
             second_stage(j)
 

@@ -29,21 +29,23 @@ ROUND_ROWS = 32
 LEAD = 8
 UNITS = [(j, b) for b in range(HB) for j in range(LEAD)] + [(j, b) for j in range(LEAD, JT) for b in range(HB)]
 WIDE_A, WIDE_B = (0, 1, 4, 5), (2, 3, 6, 7)
-WIDE_UNITS = 12
+WIDE_UNITS = 10
 GATE_BANK, Y_BANK = 4, 5
 PAIRS = ((6, 7), (0, 2))
 ROWS_PAIR = (1, 3)
 EARLY = 2
 JOINED = (2, 3, 4)
-TURNED = (6, 7)
+TURNED = (5, 6, 7)
 WA1_AT = 2
 WD_FROM = 6
 WD_ON = (2, 5)
 WD1_V = 2
 WD1_V_AT = 8
 Q_AT = 10
-SECOND_AT = 11
+SECOND_AT = 10
 STEP = 2
+PAGES = 4
+P2 = 4
 
 SPANS = ((0, 2), (2, 4), (4, 8))
 
@@ -62,8 +64,10 @@ AT = {
     "wd_raw1": 40896,
     "wd_bf0": 67584 + 2048 * WD_ON[0],
     "wd_bf1": 67584 + 2048 * WD_ON[1],
+    "tab_s": 10240,
+    "page1": 10240 + 2048 - 64,
     "page2": 49152,
-    "tab_s": 49152 + 8192 - 64,
+    "h_last": 49152 + 8192 - 64,
     "page3": 49152 + 8192 + 2048 - 128,
     "act": 67584,
     "v_w0": 100352,
@@ -143,8 +147,7 @@ def tile_list_sniff_correction_kernel(
         nc.sync.dma_start(place[:], offs2)
 
 
-        for i in range(2):
-            clear_page(i, held([P, T2], F32, "page%d" % i))
+        clear_page(0, held([P, T2], F32, "page0"))
 
         nc.vector.tensor_copy(got_s[:], tab_s[:].indirect(pick[:]))
         nc.vector.tensor_copy(
@@ -158,8 +161,7 @@ def tile_list_sniff_correction_kernel(
         move_rows(planes, rows)
         load_wa(1, 0, 1)
         load_wa(1, 1, 1)
-        for i in (2, 3):
-            clear_page(i, staged([P, T2], F32, "page%d" % i))
+        clear_page(1, staged([P, T2], F32, "page1"))
 
 
         wa_bf = [staged([P, KP * PACK], BF16, "wa_bf0")]
@@ -249,7 +251,8 @@ def tile_list_sniff_correction_kernel(
             nc.vector.quantize_mx(out=wd_q[b][:].bitcast(FP8X4), scales=wd_s[b][:], in_=wd_bf[b][:].rearrange("p n i -> p (n i)"))
 
         y = held([P, PACK, S], F32, "y")
-        h_bf = [held([P, HB, P, PACK], BF16, "h_bf%d" % j) for j in range(JT)]
+        h_bf = [held([P, HB, P, PACK], BF16, "h_bf%d" % j) for j in range(JT - 1)]
+        h_bf.append(staged([P, HB, P, PACK], BF16, "h_last"))
         h_q = [held([P, HB * P], U32, "h_q%d" % j) for j in range(JT)]
         h_s = [held([P, HB * P], U8, "h_s%d" % j) for j in range(JT)]
         unit_parts, gate, copied, sums, terms = {}, {}, {}, {}, {}
@@ -408,12 +411,17 @@ def tile_list_sniff_correction_kernel(
         def second_stage(j):
             if j > 0:
                 add_terms(j - 1)
+                if j - 1 == EARLY and PAGES == 4:
+                    put(2, 0, EARLY)
                 for i in range(PACK - 1):
-                    put(i, j - 1, j)
-                if j == 1:
+                    if i < 2 or (j > EARLY and PAGES == 4):
+                        put(i, j - 1, j)
+                if PAGES == 4 and j - 1 == EARLY + 1:
                     put(3, 0, 1)
-                if j == JT - 1:
+                if PAGES == 4 and j == JT - 1:
                     put(3, j - 1, j)
+                if PAGES == 3 and EARLY <= j - 1 < EARLY + P2:
+                    put(2, j - 1 - EARLY, j - EARLY)
             if j + 2 in TURNED:
                 turned_products(j + 2)
             if j + 1 < JT:
@@ -454,14 +462,24 @@ def tile_list_sniff_correction_kernel(
                 if k == SECOND_AT + STEP * (j + 1):
                     second_stage(j)
         quantize_hidden(JT - 1)
+        for i in range(2, PAGES):
+            pages[i] = staged([P, T2], F32, "page%d" % i)
+            nc.gpsimd.memset(pages[i][:].bitcast(I32), 0)
         for j in range(EARLY, JT):
             second_stage(j)
 
         out_rows = out.rearrange("(p i) t -> p i t", i=PACK)
         add_terms(JT - 1)
-        for i in (0, 1, 3, 2):
-            put(i, JT - 1, JT)
-            if i < 3:
+        if PAGES == 4:
+            for i in (0, 1, 3, 2):
+                put(i, JT - 1, JT)
+                if i < 3:
+                    nc.sync.dma_start(out=out_rows[:, i, :], in_=pages[i][:])
+            put(3, 1, JT - 2)
+        else:
+            for i in range(3):
+                put(i, JT - 1 if i < 2 else P2, JT)
                 nc.sync.dma_start(out=out_rows[:, i, :], in_=pages[i][:])
-        put(3, 1, JT - 2)
+            pages[3] = pages[0]
+            put(3, 0, JT)
         nc.sync.dma_start(out=out_rows[:, 3, :], in_=pages[3][:])

@@ -68,7 +68,7 @@ AT = {
     "page1": 10240 + 2048 - 64,
     "page2": 49152,
     "h_last": 49152 + 8192 - 64,
-    "page3": 49152 + 8192 + 2048 - 128,
+    "page3": 105472,
     "act": 67584,
     "v_w0": 100352,
     "wa_bf0": 101376,
@@ -147,7 +147,13 @@ def tile_list_sniff_correction_kernel(
         nc.sync.dma_start(place[:], offs2)
 
 
-        clear_page(0, held([P, T2], F32, "page0"))
+        pages[0] = held([P, T2], F32, "page0")
+        nc.vector.memset(pages[0][:, 0 : T2 // 2 - 1].bitcast(I32), 0)
+        nc.vector.memset(pages[0][:, T2 // 2 - 1 : T2].bitcast(I32), 0)
+        ident = held([P, P], F32, "ident")
+        make_identity(nc, ident[:])
+        pages[3] = staged([P, T2], F32, "page3")
+        nc.gpsimd.memset(pages[3][:].bitcast(I32), 0)
 
         nc.vector.tensor_copy(got_s[:], tab_s[:].indirect(pick[:]))
         nc.vector.tensor_copy(
@@ -231,8 +237,6 @@ def tile_list_sniff_correction_kernel(
         we_s = late_planes[:, N:LATE]
         move_rows(late_planes, late_rows)
 
-        ident = held([P, P], F32, "ident")
-        make_identity(nc, ident[:])
         wd_bf = {}
 
         def round_wd(b, c0, c1, on_vector=False):
@@ -462,7 +466,7 @@ def tile_list_sniff_correction_kernel(
                 if k == SECOND_AT + STEP * (j + 1):
                     second_stage(j)
         quantize_hidden(JT - 1)
-        for i in range(2, PAGES):
+        for i in range(2, PAGES - 1):
             pages[i] = staged([P, T2], F32, "page%d" % i)
             nc.gpsimd.memset(pages[i][:].bitcast(I32), 0)
         for j in range(EARLY, JT):

@@ -39,7 +39,7 @@ TURNED = (5, 6, 7)
 WA1_AT = 2
 WD_FROM = 6
 WD_ON = (2, 5)
-WD1_V = 2
+WD1_V = 1
 WD1_V_AT = 8
 Q_AT = 10
 SECOND_AT = 10
@@ -66,7 +66,7 @@ AT = {
     "wd_bf1": 67584 + 2048 * WD_ON[1],
     "tab_s": 10240,
     "page1": 10240 + 2048 - 64,
-    "page2": 49152,
+    "page2": 105472 + 8192,
     "h_last": 49152 + 8192 - 64,
     "page3": 105472,
     "act": 67584,
@@ -154,6 +154,9 @@ def tile_list_sniff_correction_kernel(
         make_identity(nc, ident[:])
         pages[3] = staged([P, T2], F32, "page3")
         nc.gpsimd.memset(pages[3][:].bitcast(I32), 0)
+        pages[2] = staged([P, T2], F32, "page2")
+        for c in range(0, T2, T2 // 4):
+            nc.gpsimd.memset(pages[2][:, c : c + T2 // 4].bitcast(I32), 0)
 
         nc.vector.tensor_copy(got_s[:], tab_s[:].indirect(pick[:]))
         nc.vector.tensor_copy(
@@ -466,9 +469,6 @@ def tile_list_sniff_correction_kernel(
                 if k == SECOND_AT + STEP * (j + 1):
                     second_stage(j)
         quantize_hidden(JT - 1)
-        for i in range(2, PAGES - 1):
-            pages[i] = staged([P, T2], F32, "page%d" % i)
-            nc.gpsimd.memset(pages[i][:].bitcast(I32), 0)
         for j in range(EARLY, JT):
             second_stage(j)
 

@@ -37,6 +37,9 @@ EARLY = 2
 JOINED = (2, 3, 4)
 TURNED = (5, 6, 7)
 WA1_AT = 2
+HELD_ACT = 1
+WA0_S = 54
+P2_V = 352
 WD_FROM = 6
 WD_ON = (2, 5)
 WD1_V = 1
@@ -58,22 +61,22 @@ AT = {
     "wd_raw0": 24640,
     "wa_raw00": 32768,
     "late_rows": 32832,
-    "wb_w": 34368,
+    "wb_w": 121856,
     "we_w": 36416,
     "wc_w": 38464,
     "wd_raw1": 40896,
     "wd_bf0": 67584 + 2048 * WD_ON[0],
     "wd_bf1": 67584 + 2048 * WD_ON[1],
-    "tab_s": 10240,
+    "wb_raw": 10240,
     "page1": 10240 + 2048 - 64,
     "page2": 105472 + 8192,
     "h_last": 49152 + 8192 - 64,
     "page3": 105472,
     "act": 67584,
-    "v_w0": 100352,
-    "wa_bf0": 101376,
-    "v_w2": 101376,
-    "v_w4": 102400,
+    "v_w0": 123904,
+    "wa_bf0": 123840,
+    "v_w2": 124928,
+    "v_w4": 125952,
 }
 
 
@@ -104,9 +107,9 @@ def tile_list_sniff_correction_kernel(
         pick = held([P, S // 16], U16, "pick")
         place = held([P, S // 16], U16, "place")
         tab_w = held([P, T], U32, "tab_w")
-        tab_s = staged([P, T], U8, "tab_s")
+        tab_s = held([P, T], U8, "tab_s")
         wb_s_raw = held([P, H], U8, "wb_s_raw")
-        wb_raw = held([P, 2 * H], U8, "wb_raw")
+        wb_raw = staged([P, 2 * H], U8, "wb_raw")
         got_s = staged([P, S], U8, "got_s")
         rows = held([P, S + H], U8, "rows")
         pages = {}
@@ -122,6 +125,7 @@ def tile_list_sniff_correction_kernel(
             nc.sync.dma_start(out=raw[:], in_=wa_rows[:, :, c0 : c0 + cols])
             for h in range(halves):
                 wa_raw[b, half + h] = raw[:, :, h * KP // 2 : (h + 1) * KP // 2]
+            return raw
 
         def load_repeated(tile, scales):
             nc.sync.dma_start(
@@ -138,7 +142,7 @@ def tile_list_sniff_correction_kernel(
         nc.sync.dma_start(pick[:], offs)
         load_repeated(tab_s, tab_scales[0])
         load_repeated(wb_s_raw, wb_scales[0])
-        load_wa(0, 0, 2)
+        wa0 = load_wa(0, 0, 2)
         nc.sync.dma_start(
             out=tab_w[:].bitcast(I32),
             in_=tab_words[0].rearrange("p t i -> p (t i)").bitcast(I32),
@@ -155,8 +159,9 @@ def tile_list_sniff_correction_kernel(
         pages[3] = staged([P, T2], F32, "page3")
         nc.gpsimd.memset(pages[3][:].bitcast(I32), 0)
         pages[2] = staged([P, T2], F32, "page2")
-        for c in range(0, T2, T2 // 4):
-            nc.gpsimd.memset(pages[2][:, c : c + T2 // 4].bitcast(I32), 0)
+        nc.vector.memset(pages[2][:, 0 : P2_V // 2 - 1].bitcast(I32), 0)
+        nc.vector.memset(pages[2][:, P2_V // 2 - 1 : P2_V].bitcast(I32), 0)
+        nc.gpsimd.memset(pages[2][:, P2_V:T2].bitcast(I32), 0)
 
         nc.vector.tensor_copy(got_s[:], tab_s[:].indirect(pick[:]))
         nc.vector.tensor_copy(
@@ -170,7 +175,6 @@ def tile_list_sniff_correction_kernel(
         move_rows(planes, rows)
         load_wa(1, 0, 1)
         load_wa(1, 1, 1)
-        clear_page(1, staged([P, T2], F32, "page1"))
 
 
         wa_bf = [staged([P, KP * PACK], BF16, "wa_bf0")]
@@ -195,15 +199,19 @@ def tile_list_sniff_correction_kernel(
             nc.vector.tensor_copy(words[:], tab_w[:].indirect(pick[:, j0 * LIST_COLS : j1 * LIST_COLS]))
             v_w.extend(words[:, c : c + P] for c in range(0, (j1 - j0) * P, P))
 
-        round_wa(nc.scalar.copy, 0, 0)
-        round_wa(nc.scalar.copy, 0, 1)
-        gather_words(*SPANS[0])
+        wa0_dst = wa_bf[0][:].rearrange("p (t m i) -> p m i t", t=PACK, i=PACK)
+        wa0_src = wa0[:].rearrange("p i (m t) -> p m i t", t=PACK)
+        nc.scalar.copy(wa0_dst[:, 0:WA0_S], wa0_src[:, 0:WA0_S])
+        nc.vector.tensor_copy(wa0_dst[:, WA0_S:P], wa0_src[:, WA0_S:P])
         quantize_wa(0)
+        gather_words(*SPANS[0])
         wb_w = staged([P, 2 * H], U8, "wb_w")
         nc.vector.tensor_copy(
             wb_w[:].bitcast(U16).rearrange("p (b t m) -> p b t m", b=HB, t=PACK),
             wb_raw[:].bitcast(U16).rearrange("p (b m t) -> p b t m", b=HB, t=PACK),
         )
+        pages[1] = staged([P, T2], F32, "page1")
+        nc.gpsimd.memset(pages[1][:].bitcast(I32), 0)
         for span in SPANS[1:]:
             gather_words(*span)
         wa_bf.append(held([P, KP * PACK], BF16, "wa_bf1"))
@@ -289,7 +297,7 @@ def tile_list_sniff_correction_kernel(
                     lhsT_scale=wb_s[:, c0 : c0 + P],
                     rhs=codes, rhs_scale=scales, start=True, stop=True,
                 )
-            act = stage.tile([P, P, PACK], F32, name="act%d" % k, align_bytes=64, offset=AT["act2"] if k == 2 else AT["act"] + 2048 * k)
+            act = stage.tile([P, P, PACK], F32, name="act%d" % k, align_bytes=64, offset=AT["act2"] if k == HELD_ACT else AT["act"] + 2048 * k)
             nc.scalar.activation(act[:], a_ps[:].rearrange("p t j -> p j t"), ACT.Silu)
             unit_parts[k] = (b_ps, act)
 

@@ -47,8 +47,12 @@ WD1_V_AT = 8
 Q_AT = 10
 SECOND_AT = 10
 STEP = 2
-PAGES = 4
-P2 = 4
+RUNS = (
+    ((0, 1), (1, 2), (2, 3), (3, 4), (4, 6), (6, 7), (7, 8)),
+    ((0, 1), (1, 2), (2, 4), (4, 7), (7, 8)),
+    ((0, 2), (2, 5), (5, 6), (6, 8)),
+    ((0, 1), (1, 3), (3, 8)),
+)
 
 SPANS = ((0, 2), (2, 4), (4, 8))
 
@@ -423,20 +427,20 @@ def tile_list_sniff_correction_kernel(
                 y[:, i, cols], wg[:, cols], ALU.mult,
             )
 
+        def place_ready(j):
+            for i in range(PACK):
+                for j0, j1 in RUNS[i]:
+                    if j1 - 1 == j:
+                        put(i, j0, j1)
+                if j == JT - 1:
+                    nc.sync.dma_start(out=out_rows[:, i, :], in_=pages[i][:])
+
+        out_rows = out.rearrange("(p i) t -> p i t", i=PACK)
+
         def second_stage(j):
             if j > 0:
                 add_terms(j - 1)
-                if j - 1 == EARLY and PAGES == 4:
-                    put(2, 0, EARLY)
-                for i in range(PACK - 1):
-                    if i < 2 or (j > EARLY and PAGES == 4):
-                        put(i, j - 1, j)
-                if PAGES == 4 and j - 1 == EARLY + 1:
-                    put(3, 0, 1)
-                if PAGES == 4 and j == JT - 1:
-                    put(3, j - 1, j)
-                if PAGES == 3 and EARLY <= j - 1 < EARLY + P2:
-                    put(2, j - 1 - EARLY, j - EARLY)
+                place_ready(j - 1)
             if j + 2 in TURNED:
                 turned_products(j + 2)
             if j + 1 < JT:
@@ -480,18 +484,5 @@ def tile_list_sniff_correction_kernel(
         for j in range(EARLY, JT):
             second_stage(j)
 
-        out_rows = out.rearrange("(p i) t -> p i t", i=PACK)
         add_terms(JT - 1)
-        if PAGES == 4:
-            for i in (0, 1, 3, 2):
-                put(i, JT - 1, JT)
-                if i < 3:
-                    nc.sync.dma_start(out=out_rows[:, i, :], in_=pages[i][:])
-            put(3, 1, JT - 2)
-        else:
-            for i in range(3):
-                put(i, JT - 1 if i < 2 else P2, JT)
-                nc.sync.dma_start(out=out_rows[:, i, :], in_=pages[i][:])
-            pages[3] = pages[0]
-            put(3, 0, JT)
-        nc.sync.dma_start(out=out_rows[:, 3, :], in_=pages[3][:])
+        place_ready(JT - 1)

@@ -40,10 +40,9 @@ WA1_AT = 2
 HELD_ACT = 1
 WA0_S = 54
 P2_V = 352
-WD_FROM = 6
+WD_FROM = 8
+Q0_AT = 8
 WD_ON = (2, 5)
-WD1_V = 1
-WD1_V_AT = 8
 Q_AT = 10
 SECOND_AT = 10
 STEP = 2
@@ -69,7 +68,8 @@ AT = {
     "we_w": 36416,
     "wc_w": 38464,
     "wd_raw1": 40896,
-    "wd_bf0": 67584 + 2048 * WD_ON[0],
+    "wd_bf0": 59392,
+    "wa_bf1": 59392,
     "wd_bf1": 67584 + 2048 * WD_ON[1],
     "wb_raw": 10240,
     "page1": 10240 + 2048 - 64,
@@ -218,7 +218,7 @@ def tile_list_sniff_correction_kernel(
         nc.gpsimd.memset(pages[1][:].bitcast(I32), 0)
         for span in SPANS[1:]:
             gather_words(*span)
-        wa_bf.append(held([P, KP * PACK], BF16, "wa_bf1"))
+        wa_bf.append(staged([P, KP * PACK], BF16, "wa_bf1"))
 
         wd_raw = [staged([P, PACK, N], F32, "wd_raw%d" % b) for b in range(HB)]
         we_w = staged([P, HB * 2 * N], U8, "we_w")
@@ -456,19 +456,21 @@ def tile_list_sniff_correction_kernel(
                 hidden(k)
             if k + 2 < len(UNITS):
                 first_products(k + 2)
-            if WD_FROM <= k + 2 < WD_FROM + 8 - WD1_V:
-                b, piece = divmod(k + 2 - WD_FROM, 4)
-                round_wd(b, piece * ROUND_ROWS, (piece + 1) * ROUND_ROWS)
-            if k == WD1_V_AT and WD1_V:
-                round_wd(1, (4 - WD1_V) * ROUND_ROWS, P, True)
+            if WD_FROM <= k + 2 < WD_FROM + 4:
+                piece = k + 2 - WD_FROM
+                round_wd(1, piece * ROUND_ROWS, (piece + 1) * ROUND_ROWS)
             if k == -1:
                 round_wa(nc.scalar.copy, 1, 0)
             if k == WA1_AT - 1:
                 round_wa(nc.vector.tensor_copy, 1, 1)
             if k == WA1_AT:
                 quantize_wa(1)
+                wd_bf[0] = staged([P, N, PACK], BF16, "wd_bf0")
+                nc.gpsimd.tensor_scalar(
+                    wd_bf[0][:], wd_raw[0][:].rearrange("p i n -> p n i"), -1.0, 0.0, ALU.mult, ALU.add
+                )
                 nc.sync.dma_start(out=wg[:], in_=wgo)
-            if k == WD_FROM + 2:
+            if k == Q0_AT:
                 quantize_wd(0)
             if k == Q_AT:
                 quantize_wd(1)

@@ -27,31 +27,35 @@ LATE = N + HB * N
 ROUND_ROWS = 32
 
 LEAD = 8
+RIDE = 0
+PRE = ("wc_s",)
+FRONT = ("wb", "we_s")
+MID = ("wa10", "wa11")
+BACK = ("wd0", "wd1", "moves", "wc", "we", "place")
 UNITS = [(j, b) for b in range(HB) for j in range(LEAD)] + [(j, b) for j in range(LEAD, JT) for b in range(HB)]
 WIDE_A, WIDE_B = (0, 1, 4, 5), (2, 3, 6, 7)
 WIDE_UNITS = 10
 GATE_BANK, Y_BANK = 4, 5
+LAST_BANKS = (1, 3, 4, 6)
 PAIRS = ((6, 7), (0, 2))
 ROWS_PAIR = (1, 3)
 EARLY = 2
-JOINED = (2, 3, 4)
-TURNED = (5, 6, 7)
+JOINED = (1, 2, 3)
+TURNED = (4, 5, 6, 7)
 WA1_AT = 2
 HELD_ACT = 1
 WA0_S = 54
 P2_V = 352
-WD_FROM = 8
+G_COLS = (256, 256)
+WD_STEPS = (8, 9, 9, 10)
+WD_PIECES = [(b, piece) for b in range(HB) for piece in range((N - G_COLS[b]) // (4 * ROUND_ROWS))]
 Q0_AT = 8
-WD_ON = (2, 5)
-Q_AT = 10
-SECOND_AT = 10
+ACT1 = 0
+Q_AT = 9
+SECOND_AT = 9
 STEP = 2
-RUNS = (
-    ((0, 1), (1, 2), (2, 3), (3, 4), (4, 6), (6, 7), (7, 8)),
-    ((0, 1), (1, 2), (2, 4), (4, 7), (7, 8)),
-    ((0, 2), (2, 5), (5, 6), (6, 8)),
-    ((0, 1), (1, 3), (3, 8)),
-)
+FIRST_T = 0
+RUNS = (((0, 1), (1, 2), (2, 3), (3, 4), (4, 5), (5, 6), (6, 7), (7, 8)), ((0, 1), (1, 2), (2, 3), (3, 4), (4, 5), (5, 6), (6, 8)), ((0, 2), (2, 3), (3, 4), (4, 5), (5, 7), (7, 8)), ((0, 1), (1, 2), (2, 3), (3, 8)))
 
 SPANS = ((0, 2), (2, 4), (4, 8))
 
@@ -70,7 +74,7 @@ AT = {
     "wd_raw1": 40896,
     "wd_bf0": 59392,
     "wa_bf1": 59392,
-    "wd_bf1": 67584 + 2048 * WD_ON[1],
+    "wd_bf1": 49152,
     "wb_raw": 10240,
     "page1": 10240 + 2048 - 64,
     "page2": 105472 + 8192,
@@ -115,7 +119,7 @@ def tile_list_sniff_correction_kernel(
         wb_s_raw = held([P, H], U8, "wb_s_raw")
         wb_raw = staged([P, 2 * H], U8, "wb_raw")
         got_s = staged([P, S], U8, "got_s")
-        rows = held([P, S + H], U8, "rows")
+        rows = held([P, S + H + N * RIDE], U8, "rows")
         pages = {}
 
 
@@ -140,19 +144,65 @@ def tile_list_sniff_correction_kernel(
         def move_rows(dst, src):
             for r in range(4):
                 nc.sync.dma_start(
-                    out=dst[:].bitcast(I32)[r:P:32, :], in_=src[:].bitcast(I32)[8 * r : P : 32, :]
+                    out=dst.bitcast(I32)[r:P:32, :], in_=src.bitcast(I32)[8 * r : P : 32, :]
                 )
 
         nc.sync.dma_start(pick[:], offs)
         load_repeated(tab_s, tab_scales[0])
         load_repeated(wb_s_raw, wb_scales[0])
+        late_rows = staged([P, LATE], U8, "late_rows") if "we_s" in BACK and "wc_s" in BACK else held([P, LATE], U8, "late_rows")
+        extra = N * RIDE
+
+        def load_named(name):
+            if name == "place":
+                nc.sync.dma_start(place[:], offs2)
+            elif name == "wc_s" and RIDE:
+                nc.sync.dma_start(out=rows[0:P:8, S + H : S + H + N].bitcast(I32), in_=wc_scales[0].bitcast(I32))
+            elif name == "wc_s":
+                nc.sync.dma_start(out=late_rows[0:P:8, 0:N].bitcast(I32), in_=wc_scales[0].bitcast(I32))
+            elif name == "we_s" and RIDE == 3:
+                nc.sync.dma_start(
+                    out=rows[0:P:8, S + H + N : S + H + LATE].bitcast(I32).rearrange("q (a w) -> q a w", a=HB),
+                    in_=we_scales.bitcast(I32).rearrange("a q w -> q a w"),
+                )
+            elif name == "we_s":
+                nc.sync.dma_start(
+                    out=late_rows[0:P:8, N:LATE].bitcast(I32).rearrange("q (a w) -> q a w", a=HB),
+                    in_=we_scales.bitcast(I32).rearrange("a q w -> q a w"),
+                )
+            elif name == "wb":
+                nc.sync.dma_start(out=wb_raw[:].bitcast(I32), in_=wb_words[0].bitcast(I32))
+            elif name == "wa10":
+                load_wa(1, 0, 1)
+            elif name == "wa11":
+                load_wa(1, 1, 1)
+            elif name == "wd0":
+                load_wd(0)
+            elif name == "wd1":
+                load_wd(1)
+            elif name == "wc":
+                nc.sync.dma_start(
+                    out=wc_w[:].bitcast(I32),
+                    in_=wc_words[0].rearrange("p c i -> p (c i)").bitcast(I32),
+                )
+            elif name == "we":
+                nc.sync.dma_start(
+                    out=we_w[:].bitcast(I32).rearrange("p (a w) -> p a w", a=HB),
+                    in_=we_words.bitcast(I32).rearrange("a p w -> p a w"),
+                )
+            elif name == "moves":
+                c0 = N * RIDE
+                move_rows(late_planes[:, c0:LATE], late_rows[:, c0:LATE])
+
+        for name in PRE:
+            load_named(name)
         wa0 = load_wa(0, 0, 2)
         nc.sync.dma_start(
             out=tab_w[:].bitcast(I32),
             in_=tab_words[0].rearrange("p t i -> p (t i)").bitcast(I32),
         )
-        nc.sync.dma_start(out=wb_raw[:].bitcast(I32), in_=wb_words[0].bitcast(I32))
-        nc.sync.dma_start(place[:], offs2)
+        for name in FRONT:
+            load_named(name)
 
 
         pages[0] = held([P, T2], F32, "page0")
@@ -173,12 +223,12 @@ def tile_list_sniff_correction_kernel(
             wb_s_raw[:].rearrange("p (b m t) -> p b t m", b=HB, t=PACK),
         )
         nc.vector.tensor_copy(rows[:, 0:S].bitcast(I32), got_s[:].bitcast(I32))
-        planes = held([P, S + H], U8, "planes")
+        planes = held([P, S + H + extra], U8, "planes")
         v_s = planes[:, 0:S]
         wb_s = planes[:, S : S + H]
-        move_rows(planes, rows)
-        load_wa(1, 0, 1)
-        load_wa(1, 1, 1)
+        move_rows(planes[:], rows[:])
+        for name in MID:
+            load_named(name)
 
 
         wa_bf = [staged([P, KP * PACK], BF16, "wa_bf0")]
@@ -231,26 +281,11 @@ def tile_list_sniff_correction_kernel(
                 in_=wd[b * KP : (b + 1) * KP, :].rearrange("(p i) n -> p i n", i=PACK),
             )
 
-        late_rows = staged([P, LATE], U8, "late_rows")
-        nc.sync.dma_start(out=late_rows[0:P:8, 0:N].bitcast(I32), in_=wc_scales[0].bitcast(I32))
-        nc.sync.dma_start(
-            out=late_rows[0:P:8, N:LATE].bitcast(I32).rearrange("q (a w) -> q a w", a=HB),
-            in_=we_scales.bitcast(I32).rearrange("a q w -> q a w"),
-        )
-        load_wd(0)
-        load_wd(1)
-        nc.sync.dma_start(
-            out=wc_w[:].bitcast(I32),
-            in_=wc_words[0].rearrange("p c i -> p (c i)").bitcast(I32),
-        )
-        nc.sync.dma_start(
-            out=we_w[:].bitcast(I32).rearrange("p (a w) -> p a w", a=HB),
-            in_=we_words.bitcast(I32).rearrange("a p w -> p a w"),
-        )
         late_planes = held([P, LATE], U8, "late_planes")
-        wc_s = late_planes[:, 0:N]
-        we_s = late_planes[:, N:LATE]
-        move_rows(late_planes, late_rows)
+        wc_s = planes[:, S + H : S + H + N] if RIDE else late_planes[:, 0:N]
+        we_s = planes[:, S + H + N : S + H + LATE] if RIDE == 3 else late_planes[:, N:LATE]
+        for name in BACK:
+            load_named(name)
 
         wd_bf = {}
 
@@ -301,7 +336,7 @@ def tile_list_sniff_correction_kernel(
                     lhsT_scale=wb_s[:, c0 : c0 + P],
                     rhs=codes, rhs_scale=scales, start=True, stop=True,
                 )
-            act = stage.tile([P, P, PACK], F32, name="act%d" % k, align_bytes=64, offset=AT["act2"] if k == HELD_ACT else AT["act"] + 2048 * k)
+            act = stage.tile([P, P, PACK], F32, name="act%d" % k, align_bytes=64, offset=(AT["act"] if ACT1 else AT["act2"]) if k == HELD_ACT else AT["act"] + 2048 * k)
             nc.scalar.activation(act[:], a_ps[:].rearrange("p t j -> p j t"), ACT.Silu)
             unit_parts[k] = (b_ps, act)
 
@@ -309,7 +344,7 @@ def tile_list_sniff_correction_kernel(
             j, b = UNITS[k]
             b_ps, act = unit_parts[k]
             nc.vector.tensor_tensor(
-                h_bf[j][:, b], b_ps[:].rearrange("p t j -> p j t"), act[:], ALU.mult
+                h_bf[j][:, b], act[:], b_ps[:].rearrange("p t j -> p j t"), ALU.mult
             )
 
         def quantize_hidden(j):
@@ -414,6 +449,13 @@ def tile_list_sniff_correction_kernel(
 
         def add_terms(j):
             e_part, d_part = terms[j]
+            if j == JT - 1:
+                for i in range(PACK):
+                    y_ps = bank(LAST_BANKS[i], [P, P])
+                    transpose(y_ps[:], d_part[:, i, :], True, False)
+                    transpose(y_ps[:], e_part[:, i, :], False, True)
+                    nc.scalar.activation(y[:, i, j * P : (j + 1) * P], y_ps[:], ACT.Copy, scale=-0.5)
+                return
             y_ps = bank(Y_BANK, [P, PACK, P])
             for i in range(PACK):
                 transpose(y_ps[:, i, :], d_part[:, i, :], True, False)
@@ -439,7 +481,8 @@ def tile_list_sniff_correction_kernel(
 
         def second_stage(j):
             if j > 0:
-                add_terms(j - 1)
+                if j > FIRST_T:
+                    add_terms(j - 1)
                 place_ready(j - 1)
             if j + 2 in TURNED:
                 turned_products(j + 2)
@@ -448,6 +491,8 @@ def tile_list_sniff_correction_kernel(
                 if j >= EARLY:
                     second_products(j + 1)
             interpolate(j)
+            if j < FIRST_T:
+                add_terms(j)
             if j < EARLY:
                 second_products(j + 1)
 
@@ -456,9 +501,9 @@ def tile_list_sniff_correction_kernel(
                 hidden(k)
             if k + 2 < len(UNITS):
                 first_products(k + 2)
-            if WD_FROM <= k + 2 < WD_FROM + 4:
-                piece = k + 2 - WD_FROM
-                round_wd(1, piece * ROUND_ROWS, (piece + 1) * ROUND_ROWS)
+            for at, (b, piece) in zip(WD_STEPS, WD_PIECES):
+                if k + 2 == at:
+                    round_wd(b, piece * ROUND_ROWS, (piece + 1) * ROUND_ROWS)
             if k == -1:
                 round_wa(nc.scalar.copy, 1, 0)
             if k == WA1_AT - 1:
@@ -466,9 +511,13 @@ def tile_list_sniff_correction_kernel(
             if k == WA1_AT:
                 quantize_wa(1)
                 wd_bf[0] = staged([P, N, PACK], BF16, "wd_bf0")
-                nc.gpsimd.tensor_scalar(
-                    wd_bf[0][:], wd_raw[0][:].rearrange("p i n -> p n i"), -1.0, 0.0, ALU.mult, ALU.add
-                )
+                wd_bf[1] = staged([P, N, PACK], BF16, "wd_bf1")
+                for b in range(HB):
+                    cols = slice(N - G_COLS[b], N)
+                    nc.gpsimd.tensor_scalar(
+                        wd_bf[b][:, cols], wd_raw[b][:, :, cols].rearrange("p i n -> p n i"),
+                        -1.0, 0.0, ALU.mult, ALU.add,
+                    )
                 nc.sync.dma_start(out=wg[:], in_=wgo)
             if k == Q0_AT:
                 quantize_wd(0)

@@ -24,65 +24,59 @@ HB = H // KP
 JT = S // P
 LIST_COLS = P // 16
 LATE = N + HB * N
-ROUND_ROWS = 32
+ACT_BYTES = 4 * KP
 
-LEAD = 8
-RIDE = 0
-PRE = ("wc_s",)
-FRONT = ("wb", "we_s")
-MID = ("wa10", "wa11")
-BACK = ("wd0", "wd1", "moves", "wc", "we", "place")
-UNITS = [(j, b) for b in range(HB) for j in range(LEAD)] + [(j, b) for j in range(LEAD, JT) for b in range(HB)]
+UNITS = [(j, b) for b in range(HB) for j in range(JT)]
+AHEAD = 2
+SPANS = ((0, 2), (2, 4), (4, 8))
+
 WIDE_A, WIDE_B = (0, 1, 4, 5), (2, 3, 6, 7)
-WIDE_UNITS = 10
+WIDE_UNITS = 12
 GATE_BANK, Y_BANK = 4, 5
-LAST_BANKS = (1, 3, 4, 6)
 PAIRS = ((6, 7), (0, 2))
 ROWS_PAIR = (1, 3)
-EARLY = 2
+LAST_BANKS = (1, 3, 4, 6)
+
 JOINED = (1, 2, 3)
 TURNED = (4, 5, 6, 7)
-WA1_AT = 2
-HELD_ACT = 1
-WA0_S = 54
-P2_V = 352
-G_COLS = (256, 256)
-WD_STEPS = (8, 9, 9, 10)
-WD_PIECES = [(b, piece) for b in range(HB) for piece in range((N - G_COLS[b]) // (4 * ROUND_ROWS))]
-Q0_AT = 8
-ACT1 = 0
-Q_AT = 9
-SECOND_AT = 9
-STEP = 2
-FIRST_T = 0
-RUNS = (((0, 1), (1, 2), (2, 3), (3, 4), (4, 5), (5, 6), (6, 7), (7, 8)), ((0, 1), (1, 2), (2, 3), (3, 4), (4, 5), (5, 6), (6, 8)), ((0, 2), (2, 3), (3, 4), (4, 5), (5, 7), (7, 8)), ((0, 1), (1, 2), (2, 3), (3, 8)))
 
-SPANS = ((0, 2), (2, 4), (4, 8))
+WA0_ON_SCALAR = 54
+PAGE2_ON_VECTOR = 352
+WD_ON_SCALAR = N // 2
+WD_PIECE = P
+
+WA1_AT = 2
+WD_FROM = 7
+WD_AT = (9, 10)
+EARLY_AT = (12, 14)
+EARLY = len(EARLY_AT)
+
+SINGLE = tuple((j, j + 1) for j in range(JT))
+RUNS = (SINGLE, SINGLE[:6] + ((6, 8),), SINGLE[:5] + ((5, 7), (7, 8)), SINGLE[:3] + ((3, 8),))
 
 AT = {
     "wa_raw11": 0,
     "wg": 0,
     "got_s": 4032,
     "wa_raw10": 4992,
-    "act2": 5056,
+    "act1": 5056,
+    "wb_raw": 10240,
+    "page1": 12224,
     "wd_raw0": 24640,
     "wa_raw00": 32768,
-    "late_rows": 32832,
-    "wb_w": 121856,
     "we_w": 36416,
     "wc_w": 38464,
     "wd_raw1": 40896,
-    "wd_bf0": 59392,
-    "wa_bf1": 59392,
     "wd_bf1": 49152,
-    "wb_raw": 10240,
-    "page1": 10240 + 2048 - 64,
-    "page2": 105472 + 8192,
-    "h_last": 49152 + 8192 - 64,
-    "page3": 105472,
+    "h_last": 57280,
+    "wa_bf1": 59392,
+    "wd_bf0": 59392,
     "act": 67584,
-    "v_w0": 123904,
+    "page3": 105472,
+    "page2": 113664,
+    "wb_w": 121856,
     "wa_bf0": 123840,
+    "v_w0": 123904,
     "v_w2": 124928,
     "v_w4": 125952,
 }
@@ -108,10 +102,6 @@ def tile_list_sniff_correction_kernel(
         def bank(number, shape):
             return psum.tile(shape, F32, name="bank%d" % number)
 
-        def clear_page(i, tile):
-            pages[i] = tile
-            nc.vector.memset(tile[:].bitcast(I32), 0)
-
         pick = held([P, S // 16], U16, "pick")
         place = held([P, S // 16], U16, "place")
         tab_w = held([P, T], U32, "tab_w")
@@ -119,20 +109,16 @@ def tile_list_sniff_correction_kernel(
         wb_s_raw = held([P, H], U8, "wb_s_raw")
         wb_raw = staged([P, 2 * H], U8, "wb_raw")
         got_s = staged([P, S], U8, "got_s")
-        rows = held([P, S + H + N * RIDE], U8, "rows")
+        rows = held([P, S + H], U8, "rows")
         pages = {}
 
-
         wa_rows = wa.rearrange("(p i) c -> p i c", i=PACK)
-        wa_raw = {}
 
         def load_wa(b, half, halves):
             cols = halves * KP // 2
             raw = staged([P, PACK, cols], F32, "wa_raw%d%d" % (b, half))
             c0 = b * KP + half * KP // 2
             nc.sync.dma_start(out=raw[:], in_=wa_rows[:, :, c0 : c0 + cols])
-            for h in range(halves):
-                wa_raw[b, half + h] = raw[:, :, h * KP // 2 : (h + 1) * KP // 2]
             return raw
 
         def load_repeated(tile, scales):
@@ -144,78 +130,39 @@ def tile_list_sniff_correction_kernel(
         def move_rows(dst, src):
             for r in range(4):
                 nc.sync.dma_start(
-                    out=dst.bitcast(I32)[r:P:32, :], in_=src.bitcast(I32)[8 * r : P : 32, :]
+                    out=dst[:].bitcast(I32)[r:P:32, :], in_=src[:].bitcast(I32)[8 * r : P : 32, :]
                 )
 
         nc.sync.dma_start(pick[:], offs)
         load_repeated(tab_s, tab_scales[0])
         load_repeated(wb_s_raw, wb_scales[0])
-        late_rows = staged([P, LATE], U8, "late_rows") if "we_s" in BACK and "wc_s" in BACK else held([P, LATE], U8, "late_rows")
-        extra = N * RIDE
-
-        def load_named(name):
-            if name == "place":
-                nc.sync.dma_start(place[:], offs2)
-            elif name == "wc_s" and RIDE:
-                nc.sync.dma_start(out=rows[0:P:8, S + H : S + H + N].bitcast(I32), in_=wc_scales[0].bitcast(I32))
-            elif name == "wc_s":
-                nc.sync.dma_start(out=late_rows[0:P:8, 0:N].bitcast(I32), in_=wc_scales[0].bitcast(I32))
-            elif name == "we_s" and RIDE == 3:
-                nc.sync.dma_start(
-                    out=rows[0:P:8, S + H + N : S + H + LATE].bitcast(I32).rearrange("q (a w) -> q a w", a=HB),
-                    in_=we_scales.bitcast(I32).rearrange("a q w -> q a w"),
-                )
-            elif name == "we_s":
-                nc.sync.dma_start(
-                    out=late_rows[0:P:8, N:LATE].bitcast(I32).rearrange("q (a w) -> q a w", a=HB),
-                    in_=we_scales.bitcast(I32).rearrange("a q w -> q a w"),
-                )
-            elif name == "wb":
-                nc.sync.dma_start(out=wb_raw[:].bitcast(I32), in_=wb_words[0].bitcast(I32))
-            elif name == "wa10":
-                load_wa(1, 0, 1)
-            elif name == "wa11":
-                load_wa(1, 1, 1)
-            elif name == "wd0":
-                load_wd(0)
-            elif name == "wd1":
-                load_wd(1)
-            elif name == "wc":
-                nc.sync.dma_start(
-                    out=wc_w[:].bitcast(I32),
-                    in_=wc_words[0].rearrange("p c i -> p (c i)").bitcast(I32),
-                )
-            elif name == "we":
-                nc.sync.dma_start(
-                    out=we_w[:].bitcast(I32).rearrange("p (a w) -> p a w", a=HB),
-                    in_=we_words.bitcast(I32).rearrange("a p w -> p a w"),
-                )
-            elif name == "moves":
-                c0 = N * RIDE
-                move_rows(late_planes[:, c0:LATE], late_rows[:, c0:LATE])
-
-        for name in PRE:
-            load_named(name)
+        late_rows = held([P, LATE], U8, "late_rows")
+        late_planes = held([P, LATE], U8, "late_planes")
+        nc.sync.dma_start(out=late_rows[0:P:8, 0:N].bitcast(I32), in_=wc_scales[0].bitcast(I32))
         wa0 = load_wa(0, 0, 2)
         nc.sync.dma_start(
             out=tab_w[:].bitcast(I32),
             in_=tab_words[0].rearrange("p t i -> p (t i)").bitcast(I32),
         )
-        for name in FRONT:
-            load_named(name)
+        nc.sync.dma_start(out=wb_raw[:].bitcast(I32), in_=wb_words[0].bitcast(I32))
+        nc.sync.dma_start(
+            out=late_rows[0:P:8, N:LATE].bitcast(I32).rearrange("q (a w) -> q a w", a=HB),
+            in_=we_scales.bitcast(I32).rearrange("a q w -> q a w"),
+        )
 
+        def clear_on_vector(page, cols):
+            nc.vector.memset(page[:, 0 : cols // 2 - 1].bitcast(I32), 0)
+            nc.vector.memset(page[:, cols // 2 - 1 : cols].bitcast(I32), 0)
 
         pages[0] = held([P, T2], F32, "page0")
-        nc.vector.memset(pages[0][:, 0 : T2 // 2 - 1].bitcast(I32), 0)
-        nc.vector.memset(pages[0][:, T2 // 2 - 1 : T2].bitcast(I32), 0)
+        clear_on_vector(pages[0], T2)
         ident = held([P, P], F32, "ident")
         make_identity(nc, ident[:])
         pages[3] = staged([P, T2], F32, "page3")
         nc.gpsimd.memset(pages[3][:].bitcast(I32), 0)
         pages[2] = staged([P, T2], F32, "page2")
-        nc.vector.memset(pages[2][:, 0 : P2_V // 2 - 1].bitcast(I32), 0)
-        nc.vector.memset(pages[2][:, P2_V // 2 - 1 : P2_V].bitcast(I32), 0)
-        nc.gpsimd.memset(pages[2][:, P2_V:T2].bitcast(I32), 0)
+        clear_on_vector(pages[2], PAGE2_ON_VECTOR)
+        nc.gpsimd.memset(pages[2][:, PAGE2_ON_VECTOR:T2].bitcast(I32), 0)
 
         nc.vector.tensor_copy(got_s[:], tab_s[:].indirect(pick[:]))
         nc.vector.tensor_copy(
@@ -223,23 +170,21 @@ def tile_list_sniff_correction_kernel(
             wb_s_raw[:].rearrange("p (b m t) -> p b t m", b=HB, t=PACK),
         )
         nc.vector.tensor_copy(rows[:, 0:S].bitcast(I32), got_s[:].bitcast(I32))
-        planes = held([P, S + H + extra], U8, "planes")
+        planes = held([P, S + H], U8, "planes")
         v_s = planes[:, 0:S]
         wb_s = planes[:, S : S + H]
-        move_rows(planes[:], rows[:])
-        for name in MID:
-            load_named(name)
-
+        move_rows(planes, rows)
+        wa1 = [load_wa(1, half, 1) for half in range(2)]
 
         wa_bf = [staged([P, KP * PACK], BF16, "wa_bf0")]
         wa_q = [held([P, KP], U32, "wa_q%d" % b) for b in range(HB)]
         wa_s = [held([P, KP], U8, "wa_s%d" % b) for b in range(HB)]
         wd_s = [held([P, N], U8, "wd_s%d" % b) for b in range(HB)]
 
-        def round_wa(copy, b, half):
-            dst = wa_bf[b][:].rearrange("p (t m i) -> p m i t", t=PACK, i=PACK)[:, half * P // 2 : (half + 1) * P // 2]
-            src = wa_raw[b, half].rearrange("p i (m t) -> p m i t", t=PACK)
-            copy(dst, src)
+        def round_wa(copy, b, raw, first, m0, m1):
+            dst = wa_bf[b][:].rearrange("p (t m i) -> p m i t", t=PACK, i=PACK)
+            src = raw[:].rearrange("p i (m t) -> p m i t", t=PACK)
+            copy(dst[:, m0:m1], src[:, m0 - first : m1 - first])
 
         def quantize_wa(b):
             nc.vector.quantize_mx(
@@ -253,10 +198,8 @@ def tile_list_sniff_correction_kernel(
             nc.vector.tensor_copy(words[:], tab_w[:].indirect(pick[:, j0 * LIST_COLS : j1 * LIST_COLS]))
             v_w.extend(words[:, c : c + P] for c in range(0, (j1 - j0) * P, P))
 
-        wa0_dst = wa_bf[0][:].rearrange("p (t m i) -> p m i t", t=PACK, i=PACK)
-        wa0_src = wa0[:].rearrange("p i (m t) -> p m i t", t=PACK)
-        nc.scalar.copy(wa0_dst[:, 0:WA0_S], wa0_src[:, 0:WA0_S])
-        nc.vector.tensor_copy(wa0_dst[:, WA0_S:P], wa0_src[:, WA0_S:P])
+        round_wa(nc.scalar.copy, 0, wa0, 0, 0, WA0_ON_SCALAR)
+        round_wa(nc.vector.tensor_copy, 0, wa0, 0, WA0_ON_SCALAR, P)
         quantize_wa(0)
         gather_words(*SPANS[0])
         wb_w = staged([P, 2 * H], U8, "wb_w")
@@ -275,41 +218,56 @@ def tile_list_sniff_correction_kernel(
         wc_w = staged([P, N], U32, "wc_w")
         wg = staged([P, S], F32, "wg")
 
-        def load_wd(b):
+        for b in range(HB):
             nc.sync.dma_start(
                 out=wd_raw[b][:],
                 in_=wd[b * KP : (b + 1) * KP, :].rearrange("(p i) n -> p i n", i=PACK),
             )
+        move_rows(late_planes, late_rows)
+        wc_s = late_planes[:, 0:N]
+        we_s = late_planes[:, N:LATE]
+        nc.sync.dma_start(
+            out=wc_w[:].bitcast(I32),
+            in_=wc_words[0].rearrange("p c i -> p (c i)").bitcast(I32),
+        )
+        nc.sync.dma_start(
+            out=we_w[:].bitcast(I32).rearrange("p (a w) -> p a w", a=HB),
+            in_=we_words.bitcast(I32).rearrange("a p w -> p a w"),
+        )
+        nc.sync.dma_start(place[:], offs2)
 
-        late_planes = held([P, LATE], U8, "late_planes")
-        wc_s = planes[:, S + H : S + H + N] if RIDE else late_planes[:, 0:N]
-        we_s = planes[:, S + H + N : S + H + LATE] if RIDE == 3 else late_planes[:, N:LATE]
-        for name in BACK:
-            load_named(name)
+        wd_bf = []
 
-        wd_bf = {}
+        def round_wd_on_gpsimd():
+            wd_bf.extend(staged([P, N, PACK], BF16, "wd_bf%d" % b) for b in range(HB))
+            for b in range(HB):
+                nc.gpsimd.tensor_scalar(
+                    wd_bf[b][:, WD_ON_SCALAR:N], wd_raw[b][:, :, WD_ON_SCALAR:N].rearrange("p i n -> p n i"),
+                    -1.0, 0.0, ALU.mult, ALU.add,
+                )
 
-        def round_wd(b, c0, c1, on_vector=False):
-            if b not in wd_bf:
-                wd_bf[b] = staged([P, N, PACK], BF16, "wd_bf%d" % b)
-            dst = wd_bf[b][:].rearrange("p (c u) i -> p c i u", u=4)[:, c0:c1]
-            src = wd_raw[b][:].rearrange("p i (c u) -> p c i u", u=4)[:, c0:c1]
-            if on_vector:
-                nc.vector.tensor_scalar(dst, src, -1.0, None, ALU.mult)
-            else:
-                nc.scalar.activation(dst, src, ACT.Copy, scale=-1.0)
+        def round_wd_on_scalar(piece):
+            b, part = divmod(piece, WD_ON_SCALAR // WD_PIECE)
+            groups = slice(part * WD_PIECE // 4, (part + 1) * WD_PIECE // 4)
+            nc.scalar.activation(
+                wd_bf[b][:].rearrange("p (c u) i -> p c i u", u=4)[:, groups],
+                wd_raw[b][:].rearrange("p i (c u) -> p c i u", u=4)[:, groups],
+                ACT.Copy, scale=-1.0,
+            )
 
         wd_q = [held([P, N], U32, "wd_q%d" % b) for b in range(HB)]
 
         def quantize_wd(b):
-            nc.vector.quantize_mx(out=wd_q[b][:].bitcast(FP8X4), scales=wd_s[b][:], in_=wd_bf[b][:].rearrange("p n i -> p (n i)"))
+            nc.vector.quantize_mx(
+                out=wd_q[b][:].bitcast(FP8X4), scales=wd_s[b][:], in_=wd_bf[b][:].rearrange("p n i -> p (n i)")
+            )
 
         y = held([P, PACK, S], F32, "y")
         h_bf = [held([P, HB, P, PACK], BF16, "h_bf%d" % j) for j in range(JT - 1)]
         h_bf.append(staged([P, HB, P, PACK], BF16, "h_last"))
         h_q = [held([P, HB * P], U32, "h_q%d" % j) for j in range(JT)]
         h_s = [held([P, HB * P], U8, "h_s%d" % j) for j in range(JT)]
-        unit_parts, gate, copied, sums, terms = {}, {}, {}, {}, {}
+        unit_parts, gate, copied, e_sum, d_sum, terms = {}, {}, {}, {}, {}, {}
 
         def table_tile(j):
             return v_w[j].bitcast(FP8X4), v_s[:, j * P : (j + 1) * P]
@@ -336,7 +294,10 @@ def tile_list_sniff_correction_kernel(
                     lhsT_scale=wb_s[:, c0 : c0 + P],
                     rhs=codes, rhs_scale=scales, start=True, stop=True,
                 )
-            act = stage.tile([P, P, PACK], F32, name="act%d" % k, align_bytes=64, offset=(AT["act"] if ACT1 else AT["act2"]) if k == HELD_ACT else AT["act"] + 2048 * k)
+            name = "act%d" % k
+            act = stage.tile(
+                [P, P, PACK], F32, name=name, align_bytes=64, offset=AT.get(name, AT["act"] + ACT_BYTES * k)
+            )
             nc.scalar.activation(act[:], a_ps[:].rearrange("p t j -> p j t"), ACT.Silu)
             unit_parts[k] = (b_ps, act)
 
@@ -404,136 +365,129 @@ def tile_list_sniff_correction_kernel(
                     start=(first and b == 0), stop=(b == HB - 1),
                 )
 
-        def second_products(j):
-            pair = PAIRS[0 if j <= EARLY else (j - EARLY) % 2]
-            e_ps = bank(pair[0], [P, N])
-            d_ps = bank(pair[1], [P, N])
-            sums[j] = (e_ps, d_ps)
+        def e_products(j, number):
+            e_sum[j] = bank(number, [P, N])
+            if j in TURNED:
+                for q in range(N // P):
+                    transpose(e_sum[j][:, q * P : (q + 1) * P], copied[j][0][:, q, :], True, True)
+            else:
+                we_passes(j, e_sum[j], True)
+
+        def d_products(j, number):
+            d_sum[j] = bank(number, [P, N])
             if j in TURNED:
                 e_sb, d_sb = copied[j]
                 for q in range(N // P):
-                    transpose(e_ps[:, q * P : (q + 1) * P], e_sb[:, q, :], True, True)
-                for q in range(N // P):
-                    transpose(d_ps[:, q * P : (q + 1) * P], e_sb[:, q, :], True, False)
-                    transpose(d_ps[:, q * P : (q + 1) * P], d_sb[:, q, :], False, True)
+                    transpose(d_sum[j][:, q * P : (q + 1) * P], e_sb[:, q, :], True, False)
+                    transpose(d_sum[j][:, q * P : (q + 1) * P], d_sb[:, q, :], False, True)
                 return
-            we_passes(j, e_ps, True)
             for b in range(HB):
                 codes, scales = h_pass(j, b)
                 nc.tensor.matmul_mx(
-                    out=d_ps[:], lhsT=codes, lhsT_scale=scales,
+                    out=d_sum[j][:], lhsT=codes, lhsT_scale=scales,
                     rhs=wd_q[b][:].bitcast(FP8X4), rhs_scale=wd_s[b][:],
                     start=(b == 0), stop=(b == HB - 1 and j not in JOINED),
                 )
             if j in JOINED:
-                we_passes(j, d_ps, False)
+                we_passes(j, d_sum[j], False)
+
+        def second_products(j):
+            pair = PAIRS[j % 2]
+            e_products(j, pair[0])
+            d_products(j, pair[1])
 
         def interpolate(j):
-            e_ps, d_ps = sums[j]
+            e_view = e_sum[j][:].rearrange("j (p i) -> j i p", i=PACK)
+            d_view = d_sum[j][:].rearrange("j (p i) -> j i p", i=PACK)
             e_part = ring.tile([P, PACK, P], F32, name="e_part", bufs=3)
             d_part = ring.tile([P, PACK, P], F32, name="d_part", bufs=3)
             if j in JOINED + TURNED:
-                nc.scalar.activation(
-                    e_part[:], e_ps[:].rearrange("j (p i) -> j i p", i=PACK), ACT.Copy, scale=-2.0
-                )
+                nc.scalar.activation(e_part[:], e_view, ACT.Copy, scale=-2.0)
             else:
-                nc.vector.scalar_tensor_tensor(
-                    e_part[:], gate[j][:], 1.0, e_ps[:].rearrange("j (p i) -> j i p", i=PACK),
-                    ALU.subtract, ALU.mult,
-                )
-            nc.vector.scalar_tensor_tensor(
-                d_part[:], gate[j][:], 1.0, d_ps[:].rearrange("j (p i) -> j i p", i=PACK),
-                ALU.add, ALU.mult,
-            )
+                nc.vector.scalar_tensor_tensor(e_part[:], gate[j][:], 1.0, e_view, ALU.subtract, ALU.mult)
+            nc.vector.scalar_tensor_tensor(d_part[:], gate[j][:], 1.0, d_view, ALU.add, ALU.mult)
             terms[j] = (e_part, d_part)
 
-        def add_terms(j):
+        def add_page(j, i, dst):
             e_part, d_part = terms[j]
-            if j == JT - 1:
-                for i in range(PACK):
-                    y_ps = bank(LAST_BANKS[i], [P, P])
-                    transpose(y_ps[:], d_part[:, i, :], True, False)
-                    transpose(y_ps[:], e_part[:, i, :], False, True)
-                    nc.scalar.activation(y[:, i, j * P : (j + 1) * P], y_ps[:], ACT.Copy, scale=-0.5)
-                return
-            y_ps = bank(Y_BANK, [P, PACK, P])
+            transpose(dst, d_part[:, i, :], True, False)
+            transpose(dst, e_part[:, i, :], False, True)
+
+        def add_terms(j, number):
+            y_ps = bank(number, [P, PACK, P])
             for i in range(PACK):
-                transpose(y_ps[:, i, :], d_part[:, i, :], True, False)
-                transpose(y_ps[:, i, :], e_part[:, i, :], False, True)
+                add_page(j, i, y_ps[:, i, :])
             nc.scalar.activation(y[:, :, j * P : (j + 1) * P], y_ps[:], ACT.Copy, scale=-0.5)
 
-        def put(i, j0, j1):
-            cols = slice(j0 * P, j1 * P)
-            nc.vector.tensor_tensor(
-                pages[i][:].indirect(place[:, j0 * LIST_COLS : j1 * LIST_COLS]),
-                y[:, i, cols], wg[:, cols], ALU.mult,
-            )
+        def add_last_terms(j):
+            for i in range(PACK):
+                y_ps = bank(LAST_BANKS[i], [P, P])
+                add_page(j, i, y_ps[:])
+                nc.scalar.activation(y[:, i, j * P : (j + 1) * P], y_ps[:], ACT.Copy, scale=-0.5)
+
+        out_rows = out.rearrange("(p i) t -> p i t", i=PACK)
 
         def place_ready(j):
             for i in range(PACK):
                 for j0, j1 in RUNS[i]:
                     if j1 - 1 == j:
-                        put(i, j0, j1)
+                        cols = slice(j0 * P, j1 * P)
+                        nc.vector.tensor_tensor(
+                            pages[i][:].indirect(place[:, j0 * LIST_COLS : j1 * LIST_COLS]),
+                            y[:, i, cols], wg[:, cols], ALU.mult,
+                        )
                 if j == JT - 1:
                     nc.sync.dma_start(out=out_rows[:, i, :], in_=pages[i][:])
 
-        out_rows = out.rearrange("(p i) t -> p i t", i=PACK)
+        def early_stage(j):
+            if j == 0:
+                gate_of(1)
+                d_products(1, Y_BANK)
+                interpolate(0)
+            else:
+                add_terms(0, PAIRS[0][1])
+                e_products(1, PAIRS[0][0])
+                place_ready(0)
+                gate_of(2)
+                interpolate(1)
+                second_products(2)
 
         def second_stage(j):
-            if j > 0:
-                if j > FIRST_T:
-                    add_terms(j - 1)
-                place_ready(j - 1)
+            add_terms(j - 1, Y_BANK)
+            place_ready(j - 1)
             if j + 2 in TURNED:
                 turned_products(j + 2)
             if j + 1 < JT:
                 gate_of(j + 1)
-                if j >= EARLY:
-                    second_products(j + 1)
-            interpolate(j)
-            if j < FIRST_T:
-                add_terms(j)
-            if j < EARLY:
                 second_products(j + 1)
+            interpolate(j)
 
-        for k in range(-2, len(UNITS)):
+        for k in range(-AHEAD, len(UNITS)):
             if k >= 0:
                 hidden(k)
-            if k + 2 < len(UNITS):
-                first_products(k + 2)
-            for at, (b, piece) in zip(WD_STEPS, WD_PIECES):
-                if k + 2 == at:
-                    round_wd(b, piece * ROUND_ROWS, (piece + 1) * ROUND_ROWS)
-            if k == -1:
-                round_wa(nc.scalar.copy, 1, 0)
+            if k + AHEAD < len(UNITS):
+                first_products(k + AHEAD)
+            if 0 <= k - WD_FROM < HB * WD_ON_SCALAR // WD_PIECE:
+                round_wd_on_scalar(k - WD_FROM)
+            if k == 1 - AHEAD:
+                round_wa(nc.scalar.copy, 1, wa1[0], 0, 0, P // 2)
             if k == WA1_AT - 1:
-                round_wa(nc.vector.tensor_copy, 1, 1)
+                round_wa(nc.vector.tensor_copy, 1, wa1[1], P // 2, P // 2, P)
             if k == WA1_AT:
                 quantize_wa(1)
-                wd_bf[0] = staged([P, N, PACK], BF16, "wd_bf0")
-                wd_bf[1] = staged([P, N, PACK], BF16, "wd_bf1")
-                for b in range(HB):
-                    cols = slice(N - G_COLS[b], N)
-                    nc.gpsimd.tensor_scalar(
-                        wd_bf[b][:, cols], wd_raw[b][:, :, cols].rearrange("p i n -> p n i"),
-                        -1.0, 0.0, ALU.mult, ALU.add,
-                    )
+                round_wd_on_gpsimd()
                 nc.sync.dma_start(out=wg[:], in_=wgo)
-            if k == Q0_AT:
-                quantize_wd(0)
-            if k == Q_AT:
-                quantize_wd(1)
-            if k > LEAD:
-                quantize_hidden(k - 1 - LEAD)
-            if k == SECOND_AT:
+            if k in WD_AT:
+                quantize_wd(WD_AT.index(k))
+            if k > JT:
+                quantize_hidden(k - 1 - JT)
+            if k == WD_AT[-1]:
                 gate_of(0)
                 second_products(0)
-            for j in range(EARLY):
-                if k == SECOND_AT + STEP * (j + 1):
-                    second_stage(j)
+            if k in EARLY_AT:
+                early_stage(EARLY_AT.index(k))
         quantize_hidden(JT - 1)
         for j in range(EARLY, JT):
             second_stage(j)
-
-        add_terms(JT - 1)
+        add_last_terms(JT - 1)
         place_ready(JT - 1)

@@ -35,7 +35,7 @@ WIDE_UNITS = 12
 GATE_BANK, Y_BANK = 4, 5
 PAIRS = ((6, 7), (0, 2))
 ROWS_PAIR = (1, 3)
-LAST_BANKS = (1, 3, 4, 6)
+LAST_PARTS = ((1, 0, 1), (3, 1, 2), (Y_BANK, 2, 4))
 
 JOINED = (1, 2, 3)
 TURNED = (4, 5, 6, 7)
@@ -52,7 +52,7 @@ EARLY_AT = (12, 14)
 EARLY = len(EARLY_AT)
 
 SINGLE = tuple((j, j + 1) for j in range(JT))
-RUNS = (SINGLE, SINGLE[:6] + ((6, 8),), SINGLE[:5] + ((5, 7), (7, 8)), SINGLE[:3] + ((3, 8),))
+RUNS = (SINGLE, SINGLE, SINGLE[:5] + ((5, 8),), SINGLE[:4] + ((4, 8),))
 
 AT = {
     "wa_raw11": 0,
@@ -420,10 +420,11 @@ def tile_list_sniff_correction_kernel(
             nc.scalar.activation(y[:, :, j * P : (j + 1) * P], y_ps[:], ACT.Copy, scale=-0.5)
 
         def add_last_terms(j):
-            for i in range(PACK):
-                y_ps = bank(LAST_BANKS[i], [P, P])
-                add_page(j, i, y_ps[:])
-                nc.scalar.activation(y[:, i, j * P : (j + 1) * P], y_ps[:], ACT.Copy, scale=-0.5)
+            for number, i0, i1 in LAST_PARTS:
+                y_ps = bank(number, [P, i1 - i0, P])
+                for i in range(i0, i1):
+                    add_page(j, i, y_ps[:, i - i0, :])
+                nc.scalar.activation(y[:, i0:i1, j * P : (j + 1) * P], y_ps[:], ACT.Copy, scale=-0.5)
 
         out_rows = out.rearrange("(p i) t -> p i t", i=PACK)
 

@@ -24,7 +24,6 @@ HB = H // KP
 JT = S // P
 LIST_COLS = P // 16
 LATE = N + HB * N
-ACT_BYTES = 4 * KP
 
 UNITS = [(j, b) for b in range(HB) for j in range(JT)]
 AHEAD = 2
@@ -33,52 +32,53 @@ SPANS = ((0, 2), (2, 4), (4, 8))
 WIDE_A, WIDE_B = (0, 1, 4, 5), (2, 3, 6, 7)
 WIDE_UNITS = 12
 GATE_BANK, Y_BANK = 4, 5
-PAIRS = ((6, 7), (0, 2))
+PAIRS = ((6, 7), (2, 0))
 ROWS_PAIR = (1, 3)
 LAST_PARTS = ((1, 0, 1), (3, 1, 2), (Y_BANK, 2, 4))
 
 JOINED = (1, 2, 3)
 TURNED = (4, 5, 6, 7)
 
-WA0_ON_SCALAR = 54
-PAGE2_ON_VECTOR = 352
-WD_ON_SCALAR = N // 2
+WA0_ON_SCALAR = 72
+PAGE0_ON_VECTOR = 1600
+WD_ON_SCALAR = (2 * P, 0)
 WD_PIECE = P
 
-WA1_AT = 2
-WD_FROM = 7
-WD_AT = (9, 10)
-EARLY_AT = (12, 14)
-EARLY = len(EARLY_AT)
+WA1_AT = 3
+WD_PIECES_AT = ((7, 9), ())
+WD_AT = 13
+EARLY = 2
 
 SINGLE = tuple((j, j + 1) for j in range(JT))
 RUNS = (SINGLE, SINGLE, SINGLE[:5] + ((5, 8),), SINGLE[:4] + ((4, 8),))
 
 AT = {
-    "wa_raw11": 0,
-    "wg": 0,
-    "got_s": 4032,
-    "wa_raw10": 4992,
-    "act1": 5056,
-    "wb_raw": 10240,
-    "page1": 12224,
-    "wd_raw0": 24640,
-    "wa_raw00": 32768,
-    "we_w": 36416,
-    "wc_w": 38464,
-    "wd_raw1": 40896,
-    "wd_bf1": 49152,
-    "h_last": 57280,
-    "wa_bf1": 59392,
-    "wd_bf0": 59392,
-    "act": 67584,
-    "page3": 105472,
-    "page2": 113664,
-    "wb_w": 121856,
-    "wa_bf0": 123840,
-    "v_w0": 123904,
-    "v_w2": 124928,
-    "v_w4": 125952,
+    "wb_raw1": 0,
+    "got_s": 960,
+    "wa_raw10": 1920,
+    "wg": 1920 - 1024,
+    "wd_raw0": 10240,
+    "wa_raw00": 18368,
+    "we_w": 18432,
+    "wa_raw11": 20480,
+    "late_planes": 24576,
+    "wd_raw1": 26496,
+    "wd_q0": 26624,
+    "h_q01": 28672,
+    "h_q20": 29696,
+    "h_q11": 31744,
+    "wc_w": 5952,
+    "page1": 34816,
+    "wa_bf0": 42944,
+    "h_bf10": 47104,
+    "wd_bf0": 49088,
+    "h_bf01": 63488,
+    "h_bf31": 63488,
+    "act15": 65536,
+    "h_q30": 65536,
+    "h_q21": 66560,
+    "h_bf20": 53248,
+    "page2": 55232,
 }
 
 
@@ -99,6 +99,9 @@ def tile_list_sniff_correction_kernel(
         def staged(shape, dtype, name):
             return stage.tile(shape, dtype, name=name, align_bytes=64, offset=AT[name])
 
+        def placed(shape, dtype, name):
+            return staged(shape, dtype, name) if name in AT else held(shape, dtype, name)
+
         def bank(number, shape):
             return psum.tile(shape, F32, name="bank%d" % number)
 
@@ -106,75 +109,78 @@ def tile_list_sniff_correction_kernel(
         place = held([P, S // 16], U16, "place")
         tab_w = held([P, T], U32, "tab_w")
         tab_s = held([P, T], U8, "tab_s")
-        wb_s_raw = held([P, H], U8, "wb_s_raw")
-        wb_raw = staged([P, 2 * H], U8, "wb_raw")
         got_s = staged([P, S], U8, "got_s")
-        rows = held([P, S + H], U8, "rows")
+        wb_s_raw = held([P, H], U8, "wb_s_raw")
+        planes = held([P, S + KP], U8, "planes")
         pages = {}
 
-        wa_rows = wa.rearrange("(p i) c -> p i c", i=PACK)
+        def clear_on_vector(words):
+            cols = words.shape[1]
+            nc.vector.memset(words[:, 0 : cols // 2 - 1], 0)
+            nc.vector.memset(words[:, cols // 2 - 1 : cols], 0)
 
         def load_wa(b, half, halves):
             cols = halves * KP // 2
             raw = staged([P, PACK, cols], F32, "wa_raw%d%d" % (b, half))
             c0 = b * KP + half * KP // 2
-            nc.sync.dma_start(out=raw[:], in_=wa_rows[:, :, c0 : c0 + cols])
+            nc.sync.dma_start(out=raw[:], in_=wa.rearrange("(p i) c -> p i c", i=PACK)[:, :, c0 : c0 + cols])
             return raw
 
-        def load_repeated(tile, scales):
+        def load_wb(b):
+            raw = placed([P, 2 * KP], U8, "wb_raw%d" % b)
             nc.sync.dma_start(
-                out=tile[:].bitcast(I32),
-                in_=scales.bitcast(I32).unsqueeze(1).to_broadcast([16, 8, scales.shape[1] // 4]),
+                out=raw[:].bitcast(I32), in_=wb_words[0][:, 2 * b * KP : 2 * (b + 1) * KP].bitcast(I32)
             )
+            return raw
 
-        def move_rows(dst, src):
-            for r in range(4):
+        def move_rows(tile):
+            for r in range(1, 4):
                 nc.sync.dma_start(
-                    out=dst[:].bitcast(I32)[r:P:32, :], in_=src[:].bitcast(I32)[8 * r : P : 32, :]
+                    out=tile[:].bitcast(I32)[r:P:32, :], in_=tile[:].bitcast(I32)[8 * r : P : 32, :]
                 )
 
+        warm = held([P, 2], F32, "warm")
+        nc.vector.memset(warm[:, 0:1], 0.0)
+        nc.scalar.activation(warm[:, 1:2], warm[:, 0:1], ACT.Silu)
+        clear_on_vector(wb_s_raw[:].bitcast(I32))
+
         nc.sync.dma_start(pick[:], offs)
-        load_repeated(tab_s, tab_scales[0])
-        load_repeated(wb_s_raw, wb_scales[0])
-        late_rows = held([P, LATE], U8, "late_rows")
-        late_planes = held([P, LATE], U8, "late_planes")
-        nc.sync.dma_start(out=late_rows[0:P:8, 0:N].bitcast(I32), in_=wc_scales[0].bitcast(I32))
+        nc.sync.dma_start(
+            out=tab_s[:].bitcast(I32),
+            in_=tab_scales[0].bitcast(I32).unsqueeze(1).to_broadcast([16, 8, T // 4]),
+        )
+        nc.sync.dma_start(out=wb_s_raw[0:P:8, :].bitcast(I32), in_=wb_scales[0].bitcast(I32))
         wa0 = load_wa(0, 0, 2)
         nc.sync.dma_start(
             out=tab_w[:].bitcast(I32),
             in_=tab_words[0].rearrange("p t i -> p (t i)").bitcast(I32),
         )
-        nc.sync.dma_start(out=wb_raw[:].bitcast(I32), in_=wb_words[0].bitcast(I32))
-        nc.sync.dma_start(
-            out=late_rows[0:P:8, N:LATE].bitcast(I32).rearrange("q (a w) -> q a w", a=HB),
-            in_=we_scales.bitcast(I32).rearrange("a q w -> q a w"),
-        )
-
-        def clear_on_vector(page, cols):
-            nc.vector.memset(page[:, 0 : cols // 2 - 1].bitcast(I32), 0)
-            nc.vector.memset(page[:, cols // 2 - 1 : cols].bitcast(I32), 0)
+        wb_raw = [load_wb(0)]
+        nc.sync.dma_start(place[:], offs2)
 
         pages[0] = held([P, T2], F32, "page0")
-        clear_on_vector(pages[0], T2)
+        clear_on_vector(pages[0][:, 0:PAGE0_ON_VECTOR].bitcast(I32))
         ident = held([P, P], F32, "ident")
         make_identity(nc, ident[:])
-        pages[3] = staged([P, T2], F32, "page3")
+        pages[3] = held([P, T2], F32, "page3")
         nc.gpsimd.memset(pages[3][:].bitcast(I32), 0)
-        pages[2] = staged([P, T2], F32, "page2")
-        clear_on_vector(pages[2], PAGE2_ON_VECTOR)
-        nc.gpsimd.memset(pages[2][:, PAGE2_ON_VECTOR:T2].bitcast(I32), 0)
+        nc.gpsimd.memset(pages[0][:, PAGE0_ON_VECTOR:T2].bitcast(I32), 0)
 
         nc.vector.tensor_copy(got_s[:], tab_s[:].indirect(pick[:]))
-        nc.vector.tensor_copy(
-            rows[:, S : S + H].rearrange("p (b t m) -> p b t m", b=HB, t=PACK),
-            wb_s_raw[:].rearrange("p (b m t) -> p b t m", b=HB, t=PACK),
-        )
-        nc.vector.tensor_copy(rows[:, 0:S].bitcast(I32), got_s[:].bitcast(I32))
-        planes = held([P, S + H], U8, "planes")
         v_s = planes[:, 0:S]
-        wb_s = planes[:, S : S + H]
-        move_rows(planes, rows)
-        wa1 = [load_wa(1, half, 1) for half in range(2)]
+        wb_s = [planes[:, S : S + KP]]
+
+        def order_wb_scales(b):
+            nc.vector.tensor_copy(
+                wb_s[b].rearrange("p (t m) -> p t m", t=PACK),
+                wb_s_raw[:, b * KP : (b + 1) * KP].rearrange("p (m t) -> p t m", t=PACK),
+            )
+
+        order_wb_scales(0)
+        nc.vector.tensor_copy(v_s.bitcast(I32), got_s[:].bitcast(I32))
+        move_rows(planes)
+        wb_raw.append(load_wb(1))
+        wa1 = [load_wa(1, 0, 1)]
 
         wa_bf = [staged([P, KP * PACK], BF16, "wa_bf0")]
         wa_q = [held([P, KP], U32, "wa_q%d" % b) for b in range(HB)]
@@ -194,60 +200,74 @@ def tile_list_sniff_correction_kernel(
         v_w = []
 
         def gather_words(j0, j1):
-            words = staged([P, (j1 - j0) * P], U32, "v_w%d" % j0)
+            words = held([P, (j1 - j0) * P], U32, "v_w%d" % j0)
             nc.vector.tensor_copy(words[:], tab_w[:].indirect(pick[:, j0 * LIST_COLS : j1 * LIST_COLS]))
             v_w.extend(words[:, c : c + P] for c in range(0, (j1 - j0) * P, P))
+
+        wb_w = [held([P, 2 * KP], U8, "wb_w%d" % b) for b in range(HB)]
+
+        def order_wb(b):
+            nc.scalar.copy(
+                wb_w[b][:].bitcast(U16).rearrange("p (t m) -> p t m", t=PACK),
+                wb_raw[b][:].bitcast(U16).rearrange("p (m t) -> p t m", t=PACK),
+            )
 
         round_wa(nc.scalar.copy, 0, wa0, 0, 0, WA0_ON_SCALAR)
         round_wa(nc.vector.tensor_copy, 0, wa0, 0, WA0_ON_SCALAR, P)
         quantize_wa(0)
-        gather_words(*SPANS[0])
-        wb_w = staged([P, 2 * H], U8, "wb_w")
-        nc.vector.tensor_copy(
-            wb_w[:].bitcast(U16).rearrange("p (b t m) -> p b t m", b=HB, t=PACK),
-            wb_raw[:].bitcast(U16).rearrange("p (b m t) -> p b t m", b=HB, t=PACK),
-        )
+        wb_s1 = held([P, KP], U8, "wb_s1")
+        wb_s.append(wb_s1[:])
+        order_wb_scales(1)
+        for b in range(HB):
+            order_wb(b)
+        for span in SPANS:
+            gather_words(*span)
         pages[1] = staged([P, T2], F32, "page1")
         nc.gpsimd.memset(pages[1][:].bitcast(I32), 0)
-        for span in SPANS[1:]:
-            gather_words(*span)
-        wa_bf.append(staged([P, KP * PACK], BF16, "wa_bf1"))
+        wa_bf.append(held([P, KP * PACK], BF16, "wa_bf1"))
 
+        wa1.append(load_wa(1, 1, 1))
         wd_raw = [staged([P, PACK, N], F32, "wd_raw%d" % b) for b in range(HB)]
         we_w = staged([P, HB * 2 * N], U8, "we_w")
         wc_w = staged([P, N], U32, "wc_w")
         wg = staged([P, S], F32, "wg")
 
-        for b in range(HB):
-            nc.sync.dma_start(
-                out=wd_raw[b][:],
-                in_=wd[b * KP : (b + 1) * KP, :].rearrange("(p i) n -> p i n", i=PACK),
-            )
-        move_rows(late_planes, late_rows)
+        late_planes = staged([P, LATE], U8, "late_planes")
         wc_s = late_planes[:, 0:N]
         we_s = late_planes[:, N:LATE]
-        nc.sync.dma_start(
-            out=wc_w[:].bitcast(I32),
-            in_=wc_words[0].rearrange("p c i -> p (c i)").bitcast(I32),
-        )
-        nc.sync.dma_start(
-            out=we_w[:].bitcast(I32).rearrange("p (a w) -> p a w", a=HB),
-            in_=we_words.bitcast(I32).rearrange("a p w -> p a w"),
-        )
-        nc.sync.dma_start(place[:], offs2)
+
+        def load_second_stage():
+            nc.sync.dma_start(out=late_planes[0:P:8, 0:N].bitcast(I32), in_=wc_scales[0].bitcast(I32))
+            nc.sync.dma_start(
+                out=late_planes[0:P:8, N:LATE].bitcast(I32).rearrange("q (a w) -> q a w", a=HB),
+                in_=we_scales.bitcast(I32).rearrange("a q w -> q a w"),
+            )
+            for b in range(HB):
+                nc.sync.dma_start(
+                    out=wd_raw[b][:],
+                    in_=wd[b * KP : (b + 1) * KP, :].rearrange("(p i) n -> p i n", i=PACK),
+                )
+                move_rows((wb_s1, late_planes)[b])
+            nc.sync.dma_start(
+                out=wc_w[:].bitcast(I32),
+                in_=wc_words[0].rearrange("p c i -> p (c i)").bitcast(I32),
+            )
+            nc.sync.dma_start(
+                out=we_w[:].bitcast(I32).rearrange("p (a w) -> p a w", a=HB),
+                in_=we_words.bitcast(I32).rearrange("a p w -> p a w"),
+            )
 
         wd_bf = []
 
         def round_wd_on_gpsimd():
-            wd_bf.extend(staged([P, N, PACK], BF16, "wd_bf%d" % b) for b in range(HB))
+            wd_bf.extend(placed([P, N, PACK], BF16, "wd_bf%d" % b) for b in range(HB))
             for b in range(HB):
                 nc.gpsimd.tensor_scalar(
-                    wd_bf[b][:, WD_ON_SCALAR:N], wd_raw[b][:, :, WD_ON_SCALAR:N].rearrange("p i n -> p n i"),
+                    wd_bf[b][:, WD_ON_SCALAR[b] : N], wd_raw[b][:, :, WD_ON_SCALAR[b] : N].rearrange("p i n -> p n i"),
                     -1.0, 0.0, ALU.mult, ALU.add,
                 )
 
-        def round_wd_on_scalar(piece):
-            b, part = divmod(piece, WD_ON_SCALAR // WD_PIECE)
+        def round_wd_on_scalar(b, part):
             groups = slice(part * WD_PIECE // 4, (part + 1) * WD_PIECE // 4)
             nc.scalar.activation(
                 wd_bf[b][:].rearrange("p (c u) i -> p c i u", u=4)[:, groups],
@@ -255,26 +275,24 @@ def tile_list_sniff_correction_kernel(
                 ACT.Copy, scale=-1.0,
             )
 
-        wd_q = [held([P, N], U32, "wd_q%d" % b) for b in range(HB)]
+        wd_q = {}
 
         def quantize_wd(b):
+            wd_q[b] = placed([P, N], U32, "wd_q%d" % b)
             nc.vector.quantize_mx(
                 out=wd_q[b][:].bitcast(FP8X4), scales=wd_s[b][:], in_=wd_bf[b][:].rearrange("p n i -> p (n i)")
             )
 
         y = held([P, PACK, S], F32, "y")
-        h_bf = [held([P, HB, P, PACK], BF16, "h_bf%d" % j) for j in range(JT - 1)]
-        h_bf.append(staged([P, HB, P, PACK], BF16, "h_last"))
-        h_q = [held([P, HB * P], U32, "h_q%d" % j) for j in range(JT)]
-        h_s = [held([P, HB * P], U8, "h_s%d" % j) for j in range(JT)]
+        h_bf, h_q, h_s = {}, {}, {}
         unit_parts, gate, copied, e_sum, d_sum, terms = {}, {}, {}, {}, {}, {}
 
         def table_tile(j):
             return v_w[j].bitcast(FP8X4), v_s[:, j * P : (j + 1) * P]
 
         def h_pass(j, b):
-            m = slice(b * P, (b + 1) * P)
-            return h_q[j][:, m].bitcast(FP8X4), h_s[j][:, m]
+            m = slice(j % 2 * P, (j % 2 + 1) * P)
+            return h_q[j // 2, b][:, m].bitcast(FP8X4), h_s[j // 2, b][:, m]
 
         def first_products(k):
             j, b = UNITS[k]
@@ -288,30 +306,30 @@ def tile_list_sniff_correction_kernel(
                     rhs=codes, rhs_scale=scales, start=True, stop=True,
                 )
             for t in range(PACK):
-                c0 = b * KP + t * P
                 nc.tensor.matmul_mx(
-                    out=b_ps[:, t, :], lhsT=wb_w[:, 2 * c0 : 2 * (c0 + P)].bitcast(FP4X4),
-                    lhsT_scale=wb_s[:, c0 : c0 + P],
+                    out=b_ps[:, t, :], lhsT=wb_w[b][:, 2 * t * P : 2 * (t + 1) * P].bitcast(FP4X4),
+                    lhsT_scale=wb_s[b][:, t * P : (t + 1) * P],
                     rhs=codes, rhs_scale=scales, start=True, stop=True,
                 )
-            name = "act%d" % k
-            act = stage.tile(
-                [P, P, PACK], F32, name=name, align_bytes=64, offset=AT.get(name, AT["act"] + ACT_BYTES * k)
-            )
+            act = placed([P, P, PACK], F32, "act%d" % k)
             nc.scalar.activation(act[:], a_ps[:].rearrange("p t j -> p j t"), ACT.Silu)
             unit_parts[k] = (b_ps, act)
 
         def hidden(k):
             j, b = UNITS[k]
             b_ps, act = unit_parts[k]
+            if j % 2 == 0:
+                h_bf[j // 2, b] = placed([P, 2 * P, PACK], BF16, "h_bf%d%d" % (j // 2, b))
             nc.vector.tensor_tensor(
-                h_bf[j][:, b], act[:], b_ps[:].rearrange("p t j -> p j t"), ALU.mult
+                h_bf[j // 2, b][:, j % 2 * P : (j % 2 + 1) * P], act[:], b_ps[:].rearrange("p t j -> p j t"), ALU.mult
             )
 
-        def quantize_hidden(j):
+        def quantize_hidden(u, b):
+            h_q[u, b] = placed([P, 2 * P], U32, "h_q%d%d" % (u, b))
+            h_s[u, b] = held([P, 2 * P], U8, "h_s%d%d" % (u, b))
             nc.vector.quantize_mx(
-                out=h_q[j][:].bitcast(FP8X4), scales=h_s[j][:],
-                in_=h_bf[j][:].rearrange("p b j t -> p (b j t)"),
+                out=h_q[u, b][:].bitcast(FP8X4), scales=h_s[u, b][:],
+                in_=h_bf[u, b][:].rearrange("p j t -> p (j t)"),
             )
 
         def gate_of(j):
@@ -440,18 +458,26 @@ def tile_list_sniff_correction_kernel(
                 if j == JT - 1:
                     nc.sync.dma_start(out=out_rows[:, i, :], in_=pages[i][:])
 
-        def early_stage(j):
-            if j == 0:
-                gate_of(1)
-                d_products(1, Y_BANK)
-                interpolate(0)
-            else:
-                add_terms(0, PAIRS[0][1])
-                e_products(1, PAIRS[0][0])
-                place_ready(0)
-                gate_of(2)
-                interpolate(1)
-                second_products(2)
+        def open_second_stage():
+            quantize_hidden(0, 1)
+            quantize_wd(0)
+            quantize_wd(1)
+            second_products(0)
+            quantize_hidden(1, 1)
+            quantize_hidden(2, 0)
+            pages[2] = staged([P, T2], F32, "page2")
+            nc.gpsimd.memset(pages[2][:].bitcast(I32), 0)
+            gate_of(1)
+            d_products(1, Y_BANK)
+            interpolate(0)
+
+        def close_first_stage():
+            interpolate(1)
+            for u, b in ((3, 0), (2, 1), (3, 1)):
+                quantize_hidden(u, b)
+            place_ready(0)
+            gate_of(2)
+            second_products(2)
 
         def second_stage(j):
             add_terms(j - 1, Y_BANK)
@@ -468,26 +494,30 @@ def tile_list_sniff_correction_kernel(
                 hidden(k)
             if k + AHEAD < len(UNITS):
                 first_products(k + AHEAD)
-            if 0 <= k - WD_FROM < HB * WD_ON_SCALAR // WD_PIECE:
-                round_wd_on_scalar(k - WD_FROM)
-            if k == 1 - AHEAD:
-                round_wa(nc.scalar.copy, 1, wa1[0], 0, 0, P // 2)
+            for b in range(HB):
+                for part, at in enumerate(WD_PIECES_AT[b]):
+                    if k == at:
+                        round_wd_on_scalar(b, part)
+            if k == 0:
+                load_second_stage()
+            if k in (-1, 1):
+                m0 = (k + 1) * P // 4
+                round_wa(nc.vector.tensor_copy, 1, wa1[m0 * 2 // P], m0, m0, m0 + P // 2)
             if k == WA1_AT - 1:
-                round_wa(nc.vector.tensor_copy, 1, wa1[1], P // 2, P // 2, P)
-            if k == WA1_AT:
                 quantize_wa(1)
+            if k == WA1_AT:
+                quantize_hidden(0, 0)
+                quantize_hidden(1, 0)
                 round_wd_on_gpsimd()
                 nc.sync.dma_start(out=wg[:], in_=wgo)
-            if k in WD_AT:
-                quantize_wd(WD_AT.index(k))
-            if k > JT:
-                quantize_hidden(k - 1 - JT)
-            if k == WD_AT[-1]:
+            if k == WD_AT - 2:
                 gate_of(0)
-                second_products(0)
-            if k in EARLY_AT:
-                early_stage(EARLY_AT.index(k))
-        quantize_hidden(JT - 1)
+            if k == WD_AT:
+                open_second_stage()
+            if k == WD_AT + 1:
+                add_terms(0, GATE_BANK)
+                e_products(1, PAIRS[0][0])
+        close_first_stage()
         for j in range(EARLY, JT):
             second_stage(j)
         add_last_terms(JT - 1)

@@ -1,7 +1,6 @@
 from contextlib import ExitStack
 
 import concourse.mybir as mybir
-from concourse.masks import make_identity
 
 K, H, N, T, S, T2 = 512, 1024, 512, 2048, 1024, 2048
 FLOPS = 2 * S * (2 * K * H + K * N + 2 * H * N)
@@ -29,31 +28,35 @@ UNITS = [(j, b) for b in range(HB) for j in range(JT)]
 AHEAD = 2
 SPANS = ((0, 2), (2, 4), (4, 8))
 
-WIDE_A, WIDE_B = (0, 1, 4, 5), (2, 3, 6, 7)
-WIDE_UNITS = 12
-GATE_BANK, Y_BANK = 4, 5
-PAIRS = ((6, 7), (2, 0))
-ROWS_PAIR = (1, 3)
-LAST_PARTS = ((1, 0, 1), (3, 1, 2), (Y_BANK, 2, 4))
+A_BANKS = (0, 1, 4) * 3 + (0, 1) * 3 + (0,)
+B_BANKS = (2, 3, 6, 7) * 3 + (2, 3) * 2
+Y_BANK = 5
+GATE_BANKS = (Y_BANK,) + (7,) * (JT - 1)
+E_BANKS = (4,) + (4, 1) * 3 + (4,)
+D_BANKS = (Y_BANK,) + (6, 2) * 3 + (6,)
+ROWS_PAIR = (0, 3)
+LAST_PARTS = ((ROWS_PAIR[0], 0, 1), (ROWS_PAIR[1], 1, 2), (Y_BANK, 2, 4))
 
 JOINED = (1, 2, 3)
 TURNED = (4, 5, 6, 7)
 
 WA0_ON_SCALAR = 72
-PAGE0_ON_VECTOR = 1600
-WD_ON_SCALAR = (2 * P, 0)
+PAGE0_ON_VECTOR = 1504
 WD_PIECE = P
+WD0_ON_SCALAR = 2 * WD_PIECE
 
-WA1_AT = 3
-WD_PIECES_AT = ((7, 9), ())
-WD_AT = 13
+WA1_AT = 2
+WD_PIECES_AT = {4: ((0, 0), (0, 1)), 7: ((1, 0), (1, 1)), 8: ((1, 2),), 9: ((1, 3),)}
+ACT_ON_WD = {7: (0, 0), 8: (0, 1), 9: (0, 2), 10: (1, 0), 11: (1, 1), 12: (1, 2), 13: (1, 3)}
+WD0_ON_VECTOR_AT = 5
+WD_AT = (9, 11)
+QUANTISE_AT = {2: (0, 0), 4: (1, 0), 6: (2, 0), 8: (3, 0), 9: (0, 1), 12: (1, 1), 14: (2, 1)}
 EARLY = 2
 
 SINGLE = tuple((j, j + 1) for j in range(JT))
-RUNS = (SINGLE, SINGLE, SINGLE[:5] + ((5, 8),), SINGLE[:4] + ((4, 8),))
+RUNS = (SINGLE, SINGLE, ((0, 2),) + SINGLE[2:5] + ((5, 8),), SINGLE[:4] + ((4, 8),))
 
 AT = {
-    "wb_raw1": 0,
     "got_s": 960,
     "wa_raw10": 1920,
     "wg": 1920 - 1024,
@@ -61,24 +64,16 @@ AT = {
     "wa_raw00": 18368,
     "we_w": 18432,
     "wa_raw11": 20480,
-    "late_planes": 24576,
     "wd_raw1": 26496,
-    "wd_q0": 26624,
-    "h_q01": 28672,
-    "h_q20": 29696,
-    "h_q11": 31744,
     "wc_w": 5952,
     "page1": 34816,
     "wa_bf0": 42944,
-    "h_bf10": 47104,
-    "wd_bf0": 49088,
-    "h_bf01": 63488,
-    "h_bf31": 63488,
-    "act15": 65536,
-    "h_q30": 65536,
-    "h_q21": 66560,
-    "h_bf20": 53248,
-    "page2": 55232,
+    "h_bf31": 47104,
+    "page2": 49088,
+    "zeros": 63488,
+    "page3": 63488,
+    "h_bf30": 61440,
+    "wd_q0": 61440,
 }
 
 
@@ -126,13 +121,6 @@ def tile_list_sniff_correction_kernel(
             nc.sync.dma_start(out=raw[:], in_=wa.rearrange("(p i) c -> p i c", i=PACK)[:, :, c0 : c0 + cols])
             return raw
 
-        def load_wb(b):
-            raw = placed([P, 2 * KP], U8, "wb_raw%d" % b)
-            nc.sync.dma_start(
-                out=raw[:].bitcast(I32), in_=wb_words[0][:, 2 * b * KP : 2 * (b + 1) * KP].bitcast(I32)
-            )
-            return raw
-
         def move_rows(tile):
             for r in range(1, 4):
                 nc.sync.dma_start(
@@ -142,6 +130,8 @@ def tile_list_sniff_correction_kernel(
         warm = held([P, 2], F32, "warm")
         nc.vector.memset(warm[:, 0:1], 0.0)
         nc.scalar.activation(warm[:, 1:2], warm[:, 0:1], ACT.Silu)
+        zeros = staged([P, P + 1], F32, "zeros")
+        nc.vector.memset(zeros[:].bitcast(I32), 0)
         clear_on_vector(wb_s_raw[:].bitcast(I32))
 
         nc.sync.dma_start(pick[:], offs)
@@ -155,20 +145,31 @@ def tile_list_sniff_correction_kernel(
             out=tab_w[:].bitcast(I32),
             in_=tab_words[0].rearrange("p t i -> p (t i)").bitcast(I32),
         )
-        wb_raw = [load_wb(0)]
-        nc.sync.dma_start(place[:], offs2)
+        wb_raw = held([P, 2 * H], U8, "wb_raw")
+        nc.sync.dma_start(out=wb_raw[:].bitcast(I32), in_=wb_words[0].bitcast(I32))
+        late_planes = held([P, KP + LATE], U8, "late_planes")
+        wc_s = late_planes[:, KP : KP + N]
+        we_s = late_planes[:, KP + N : KP + LATE]
+        nc.sync.dma_start(out=wc_s[0:P:8, :].bitcast(I32), in_=wc_scales[0].bitcast(I32))
+        nc.sync.dma_start(
+            out=we_s[0:P:8, :].bitcast(I32).rearrange("q (a w) -> q a w", a=HB),
+            in_=we_scales.bitcast(I32).rearrange("a q w -> q a w"),
+        )
 
         pages[0] = held([P, T2], F32, "page0")
         clear_on_vector(pages[0][:, 0:PAGE0_ON_VECTOR].bitcast(I32))
         ident = held([P, P], F32, "ident")
-        make_identity(nc, ident[:])
-        pages[3] = held([P, T2], F32, "page3")
+        nc.gpsimd.affine_select(
+            out=ident[:], in_=zeros[:, 0:P], pattern=[[-1, P]], compare_op=ALU.not_equal, fill=1.0,
+            base=0, channel_multiplier=1,
+        )
+        pages[3] = staged([P, T2], F32, "page3")
         nc.gpsimd.memset(pages[3][:].bitcast(I32), 0)
         nc.gpsimd.memset(pages[0][:, PAGE0_ON_VECTOR:T2].bitcast(I32), 0)
 
         nc.vector.tensor_copy(got_s[:], tab_s[:].indirect(pick[:]))
         v_s = planes[:, 0:S]
-        wb_s = [planes[:, S : S + KP]]
+        wb_s = [planes[:, S : S + KP], late_planes[:, 0:KP]]
 
         def order_wb_scales(b):
             nc.vector.tensor_copy(
@@ -179,8 +180,7 @@ def tile_list_sniff_correction_kernel(
         order_wb_scales(0)
         nc.vector.tensor_copy(v_s.bitcast(I32), got_s[:].bitcast(I32))
         move_rows(planes)
-        wb_raw.append(load_wb(1))
-        wa1 = [load_wa(1, 0, 1)]
+        wa1 = [load_wa(1, half, 1) for half in range(2)]
 
         wa_bf = [staged([P, KP * PACK], BF16, "wa_bf0")]
         wa_q = [held([P, KP], U32, "wa_q%d" % b) for b in range(HB)]
@@ -209,15 +209,14 @@ def tile_list_sniff_correction_kernel(
         def order_wb(b):
             nc.scalar.copy(
                 wb_w[b][:].bitcast(U16).rearrange("p (t m) -> p t m", t=PACK),
-                wb_raw[b][:].bitcast(U16).rearrange("p (m t) -> p t m", t=PACK),
+                wb_raw[:, 2 * b * KP : 2 * (b + 1) * KP].bitcast(U16).rearrange("p (m t) -> p t m", t=PACK),
             )
 
         round_wa(nc.scalar.copy, 0, wa0, 0, 0, WA0_ON_SCALAR)
         round_wa(nc.vector.tensor_copy, 0, wa0, 0, WA0_ON_SCALAR, P)
         quantize_wa(0)
-        wb_s1 = held([P, KP], U8, "wb_s1")
-        wb_s.append(wb_s1[:])
         order_wb_scales(1)
+        move_rows(late_planes)
         for b in range(HB):
             order_wb(b)
         for span in SPANS:
@@ -226,54 +225,44 @@ def tile_list_sniff_correction_kernel(
         nc.gpsimd.memset(pages[1][:].bitcast(I32), 0)
         wa_bf.append(held([P, KP * PACK], BF16, "wa_bf1"))
 
-        wa1.append(load_wa(1, 1, 1))
         wd_raw = [staged([P, PACK, N], F32, "wd_raw%d" % b) for b in range(HB)]
         we_w = staged([P, HB * 2 * N], U8, "we_w")
         wc_w = staged([P, N], U32, "wc_w")
         wg = staged([P, S], F32, "wg")
 
-        late_planes = staged([P, LATE], U8, "late_planes")
-        wc_s = late_planes[:, 0:N]
-        we_s = late_planes[:, N:LATE]
-
-        def load_second_stage():
-            nc.sync.dma_start(out=late_planes[0:P:8, 0:N].bitcast(I32), in_=wc_scales[0].bitcast(I32))
+        def load_wd(b):
             nc.sync.dma_start(
-                out=late_planes[0:P:8, N:LATE].bitcast(I32).rearrange("q (a w) -> q a w", a=HB),
-                in_=we_scales.bitcast(I32).rearrange("a q w -> q a w"),
-            )
-            for b in range(HB):
-                nc.sync.dma_start(
-                    out=wd_raw[b][:],
-                    in_=wd[b * KP : (b + 1) * KP, :].rearrange("(p i) n -> p i n", i=PACK),
-                )
-                move_rows((wb_s1, late_planes)[b])
-            nc.sync.dma_start(
-                out=wc_w[:].bitcast(I32),
-                in_=wc_words[0].rearrange("p c i -> p (c i)").bitcast(I32),
-            )
-            nc.sync.dma_start(
-                out=we_w[:].bitcast(I32).rearrange("p (a w) -> p a w", a=HB),
-                in_=we_words.bitcast(I32).rearrange("a p w -> p a w"),
+                out=wd_raw[b][:],
+                in_=wd[b * KP : (b + 1) * KP, :].rearrange("(p i) n -> p i n", i=PACK),
             )
 
-        wd_bf = []
+        load_wd(0)
+        nc.sync.dma_start(
+            out=wc_w[:].bitcast(I32),
+            in_=wc_words[0].rearrange("p c i -> p (c i)").bitcast(I32),
+        )
+        load_wd(1)
+        nc.sync.dma_start(
+            out=we_w[:].bitcast(I32).rearrange("p (a w) -> p a w", a=HB),
+            in_=we_words.bitcast(I32).rearrange("a p w -> p a w"),
+        )
+        nc.sync.dma_start(place[:], offs2)
 
-        def round_wd_on_gpsimd():
-            wd_bf.extend(placed([P, N, PACK], BF16, "wd_bf%d" % b) for b in range(HB))
-            for b in range(HB):
-                nc.gpsimd.tensor_scalar(
-                    wd_bf[b][:, WD_ON_SCALAR[b] : N], wd_raw[b][:, :, WD_ON_SCALAR[b] : N].rearrange("p i n -> p n i"),
-                    -1.0, 0.0, ALU.mult, ALU.add,
-                )
+        wd_bf = [placed([P, N, PACK], BF16, "wd_bf%d" % b) for b in range(HB)]
 
-        def round_wd_on_scalar(b, part):
-            groups = slice(part * WD_PIECE // 4, (part + 1) * WD_PIECE // 4)
-            nc.scalar.activation(
+        def wd_views(b, n0, n1):
+            groups = slice(n0 // 4, n1 // 4)
+            return (
                 wd_bf[b][:].rearrange("p (c u) i -> p c i u", u=4)[:, groups],
                 wd_raw[b][:].rearrange("p i (c u) -> p c i u", u=4)[:, groups],
-                ACT.Copy, scale=-1.0,
             )
+
+        def wd_piece(b, piece):
+            return wd_raw[b][:, :, piece * WD_PIECE : (piece + 1) * WD_PIECE]
+
+        def round_wd_on_scalar(b, piece):
+            n0 = piece * WD_PIECE
+            nc.scalar.activation(*wd_views(b, n0, n0 + WD_PIECE), ACT.Copy, scale=-1.0)
 
         wd_q = {}
 
@@ -285,7 +274,7 @@ def tile_list_sniff_correction_kernel(
 
         y = held([P, PACK, S], F32, "y")
         h_bf, h_q, h_s = {}, {}, {}
-        unit_parts, gate, copied, e_sum, d_sum, terms = {}, {}, {}, {}, {}, {}
+        unit_parts, gate, copied, e_sum, d_sum, e_part, d_part = {}, {}, {}, {}, {}, {}, {}
 
         def table_tile(j):
             return v_w[j].bitcast(FP8X4), v_s[:, j * P : (j + 1) * P]
@@ -294,11 +283,14 @@ def tile_list_sniff_correction_kernel(
             m = slice(j % 2 * P, (j % 2 + 1) * P)
             return h_q[j // 2, b][:, m].bitcast(FP8X4), h_s[j // 2, b][:, m]
 
+        def by_entry(sums):
+            return sums[:].rearrange("p t (u j) -> p u j t", u=PACK)
+
         def first_products(k):
             j, b = UNITS[k]
             codes, scales = table_tile(j)
-            a_ps = bank(WIDE_A[k % 4] if k < WIDE_UNITS else k % 2, [P, PACK, P])
-            b_ps = bank(WIDE_B[k % 4] if k < WIDE_UNITS else 2 + k % 2, [P, PACK, P])
+            a_ps = bank(A_BANKS[k], [P, PACK, P])
+            b_ps = bank(B_BANKS[k], [P, PACK, P])
             for t in range(PACK):
                 m = slice(t * P, (t + 1) * P)
                 nc.tensor.matmul_mx(
@@ -311,8 +303,12 @@ def tile_list_sniff_correction_kernel(
                     lhsT_scale=wb_s[b][:, t * P : (t + 1) * P],
                     rhs=codes, rhs_scale=scales, start=True, stop=True,
                 )
-            act = placed([P, P, PACK], F32, "act%d" % k)
-            nc.scalar.activation(act[:], a_ps[:].rearrange("p t j -> p j t"), ACT.Silu)
+            if k in ACT_ON_WD:
+                act = wd_piece(*ACT_ON_WD[k])
+            else:
+                act = placed([P, PACK, P], F32, "act%d" % k)[:]
+            act = act.rearrange("p u (j t) -> p u j t", t=PACK)
+            nc.scalar.activation(act, by_entry(a_ps), ACT.Silu)
             unit_parts[k] = (b_ps, act)
 
         def hidden(k):
@@ -321,7 +317,8 @@ def tile_list_sniff_correction_kernel(
             if j % 2 == 0:
                 h_bf[j // 2, b] = placed([P, 2 * P, PACK], BF16, "h_bf%d%d" % (j // 2, b))
             nc.vector.tensor_tensor(
-                h_bf[j // 2, b][:, j % 2 * P : (j % 2 + 1) * P], act[:], b_ps[:].rearrange("p t j -> p j t"), ALU.mult
+                h_bf[j // 2, b][:, j % 2 * P : (j % 2 + 1) * P].rearrange("p (u j) t -> p u j t", u=PACK),
+                act, by_entry(b_ps), ALU.mult,
             )
 
         def quantize_hidden(u, b):
@@ -334,7 +331,7 @@ def tile_list_sniff_correction_kernel(
 
         def gate_of(j):
             codes, scales = table_tile(j)
-            c_ps = bank(GATE_BANK, [P, N])
+            c_ps = bank(GATE_BANKS[j], [P, N])
             gate[j] = ring.tile([P, PACK, P], F32, name="gate", bufs=3)
             nc.tensor.matmul_mx(
                 out=c_ps[:], lhsT=codes, lhsT_scale=scales,
@@ -373,63 +370,67 @@ def tile_list_sniff_correction_kernel(
         def transpose(dst, src, first, last):
             nc.tensor.matmul(dst, src, ident[:], start=first, stop=last, is_transpose=True)
 
-        def we_passes(j, dst, first):
+        def we_passes(j, dst, last):
             for b in range(HB):
                 codes, scales = h_pass(j, b)
                 nc.tensor.matmul_mx(
                     out=dst[:], lhsT=codes, lhsT_scale=scales,
                     rhs=we_w[:, 2 * b * N : 2 * (b + 1) * N].bitcast(FP4X4),
                     rhs_scale=we_s[:, b * N : (b + 1) * N],
-                    start=(first and b == 0), stop=(b == HB - 1),
+                    start=(b == 0), stop=(last and b == HB - 1),
                 )
 
-        def e_products(j, number):
-            e_sum[j] = bank(number, [P, N])
+        def e_products(j):
+            e_sum[j] = bank(E_BANKS[j], [P, N])
             if j in TURNED:
                 for q in range(N // P):
                     transpose(e_sum[j][:, q * P : (q + 1) * P], copied[j][0][:, q, :], True, True)
             else:
                 we_passes(j, e_sum[j], True)
 
-        def d_products(j, number):
-            d_sum[j] = bank(number, [P, N])
+        def d_products(j):
+            d_sum[j] = bank(D_BANKS[j], [P, N])
             if j in TURNED:
                 e_sb, d_sb = copied[j]
                 for q in range(N // P):
                     transpose(d_sum[j][:, q * P : (q + 1) * P], e_sb[:, q, :], True, False)
                     transpose(d_sum[j][:, q * P : (q + 1) * P], d_sb[:, q, :], False, True)
                 return
+            if j in JOINED:
+                we_passes(j, d_sum[j], False)
             for b in range(HB):
                 codes, scales = h_pass(j, b)
                 nc.tensor.matmul_mx(
                     out=d_sum[j][:], lhsT=codes, lhsT_scale=scales,
                     rhs=wd_q[b][:].bitcast(FP8X4), rhs_scale=wd_s[b][:],
-                    start=(b == 0), stop=(b == HB - 1 and j not in JOINED),
+                    start=(b == 0 and j not in JOINED), stop=(b == HB - 1),
                 )
-            if j in JOINED:
-                we_passes(j, d_sum[j], False)
 
         def second_products(j):
-            pair = PAIRS[j % 2]
-            e_products(j, pair[0])
-            d_products(j, pair[1])
+            e_products(j)
+            d_products(j)
+
+        def e_term(j):
+            e_view = e_sum[j][:].rearrange("j (p i) -> j i p", i=PACK)
+            if j in JOINED + TURNED:
+                e_part[j] = ring.tile([P, PACK, P], F32, name="e_part", bufs=3)[:]
+                nc.scalar.activation(e_part[j], e_view, ACT.Copy, scale=-2.0)
+            else:
+                e_part[j] = wd_piece(*ACT_ON_WD[11])
+                nc.vector.scalar_tensor_tensor(e_part[j], gate[j][:], 1.0, e_view, ALU.subtract, ALU.mult)
+
+        def d_term(j):
+            d_view = d_sum[j][:].rearrange("j (p i) -> j i p", i=PACK)
+            d_part[j] = ring.tile([P, PACK, P], F32, name="d_part", bufs=3)
+            nc.vector.scalar_tensor_tensor(d_part[j][:], gate[j][:], 1.0, d_view, ALU.add, ALU.mult)
 
         def interpolate(j):
-            e_view = e_sum[j][:].rearrange("j (p i) -> j i p", i=PACK)
-            d_view = d_sum[j][:].rearrange("j (p i) -> j i p", i=PACK)
-            e_part = ring.tile([P, PACK, P], F32, name="e_part", bufs=3)
-            d_part = ring.tile([P, PACK, P], F32, name="d_part", bufs=3)
-            if j in JOINED + TURNED:
-                nc.scalar.activation(e_part[:], e_view, ACT.Copy, scale=-2.0)
-            else:
-                nc.vector.scalar_tensor_tensor(e_part[:], gate[j][:], 1.0, e_view, ALU.subtract, ALU.mult)
-            nc.vector.scalar_tensor_tensor(d_part[:], gate[j][:], 1.0, d_view, ALU.add, ALU.mult)
-            terms[j] = (e_part, d_part)
+            e_term(j)
+            d_term(j)
 
         def add_page(j, i, dst):
-            e_part, d_part = terms[j]
-            transpose(dst, d_part[:, i, :], True, False)
-            transpose(dst, e_part[:, i, :], False, True)
+            transpose(dst, e_part[j][:, i, :], True, False)
+            transpose(dst, d_part[j][:, i, :], False, True)
 
         def add_terms(j, number):
             y_ps = bank(number, [P, PACK, P])
@@ -458,23 +459,11 @@ def tile_list_sniff_correction_kernel(
                 if j == JT - 1:
                     nc.sync.dma_start(out=out_rows[:, i, :], in_=pages[i][:])
 
-        def open_second_stage():
-            quantize_hidden(0, 1)
-            quantize_wd(0)
-            quantize_wd(1)
-            second_products(0)
-            quantize_hidden(1, 1)
-            quantize_hidden(2, 0)
-            pages[2] = staged([P, T2], F32, "page2")
-            nc.gpsimd.memset(pages[2][:].bitcast(I32), 0)
-            gate_of(1)
-            d_products(1, Y_BANK)
-            interpolate(0)
-
         def close_first_stage():
             interpolate(1)
-            for u, b in ((3, 0), (2, 1), (3, 1)):
-                quantize_hidden(u, b)
+            quantize_hidden(3, 1)
+            pages[2] = staged([P, T2], F32, "page2")
+            nc.gpsimd.memset(pages[2][:].bitcast(I32), 0)
             place_ready(0)
             gate_of(2)
             second_products(2)
@@ -494,29 +483,34 @@ def tile_list_sniff_correction_kernel(
                 hidden(k)
             if k + AHEAD < len(UNITS):
                 first_products(k + AHEAD)
-            for b in range(HB):
-                for part, at in enumerate(WD_PIECES_AT[b]):
-                    if k == at:
-                        round_wd_on_scalar(b, part)
-            if k == 0:
-                load_second_stage()
-            if k in (-1, 1):
-                m0 = (k + 1) * P // 4
+            for b, piece in WD_PIECES_AT.get(k, ()):
+                round_wd_on_scalar(b, piece)
+            if k in (0, 1):
+                m0 = k * P // 2
                 round_wa(nc.vector.tensor_copy, 1, wa1[m0 * 2 // P], m0, m0, m0 + P // 2)
-            if k == WA1_AT - 1:
-                quantize_wa(1)
             if k == WA1_AT:
-                quantize_hidden(0, 0)
-                quantize_hidden(1, 0)
-                round_wd_on_gpsimd()
+                quantize_wa(1)
                 nc.sync.dma_start(out=wg[:], in_=wgo)
-            if k == WD_AT - 2:
+            if k == WD0_ON_VECTOR_AT:
+                nc.vector.tensor_scalar(*wd_views(0, WD0_ON_SCALAR, N), -1.0, None, ALU.mult)
+            if k in WD_AT:
+                quantize_wd(WD_AT.index(k))
+            if k in QUANTISE_AT:
+                quantize_hidden(*QUANTISE_AT[k])
+            if k == 7:
                 gate_of(0)
-            if k == WD_AT:
-                open_second_stage()
-            if k == WD_AT + 1:
-                add_terms(0, GATE_BANK)
-                e_products(1, PAIRS[0][0])
+            if k == 10:
+                e_products(0)
+            if k == 11:
+                d_products(0)
+                e_term(0)
+            if k == 12:
+                d_term(0)
+                add_terms(0, Y_BANK)
+                gate_of(1)
+            if k == 13:
+                e_products(1)
+                d_products(1)
         close_first_stage()
         for j in range(EARLY, JT):
             second_stage(j)

@@ -28,33 +28,32 @@ UNITS = [(j, b) for b in range(HB) for j in range(JT)]
 AHEAD = 2
 SPANS = ((0, 2), (2, 4), (4, 8))
 
-A_BANKS = (0, 1, 4) * 3 + (0, 1) * 3 + (0,)
+A_BANKS = (0, 1, 4) * 4 + (0, 1) * 2
 B_BANKS = (2, 3, 6, 7) * 3 + (2, 3) * 2
-Y_BANK = 5
-GATE_BANKS = (Y_BANK,) + (7,) * (JT - 1)
-E_BANKS = (4,) + (4, 1) * 3 + (4,)
+Y_BANK = 4
+GATE_BANKS = (6, 7) + (5,) * (JT - 2)
+E_BANKS = (0,) + (1,) * (JT - 1)
+E_BANKS = (0, 1) + (5,) * (JT - 2)
+E_BANKS = (5,) + (0, 7) * 3 + (0,)
 D_BANKS = (Y_BANK,) + (6, 2) * 3 + (6,)
-ROWS_PAIR = (0, 3)
+ROWS_PAIR = (1, 3)
 LAST_PARTS = ((ROWS_PAIR[0], 0, 1), (ROWS_PAIR[1], 1, 2), (Y_BANK, 2, 4))
 
 JOINED = (1, 2, 3)
 TURNED = (4, 5, 6, 7)
 
-WA0_ON_SCALAR = 72
+WA0_ON_SCALAR = 64
 PAGE0_ON_VECTOR = 1504
-WD_PIECE = P
-WD0_ON_SCALAR = 2 * WD_PIECE
+
+WD_ON_SCALAR = (N // 4, 3 * N // 4)
 
 WA1_AT = 2
-WD_PIECES_AT = {4: ((0, 0), (0, 1)), 7: ((1, 0), (1, 1)), 8: ((1, 2),), 9: ((1, 3),)}
-ACT_ON_WD = {7: (0, 0), 8: (0, 1), 9: (0, 2), 10: (1, 0), 11: (1, 1), 12: (1, 2), 13: (1, 3)}
-WD0_ON_VECTOR_AT = 5
-WD_AT = (9, 11)
-QUANTISE_AT = {2: (0, 0), 4: (1, 0), 6: (2, 0), 8: (3, 0), 9: (0, 1), 12: (1, 1), 14: (2, 1)}
+WD_ROUNDED_AT = (5, 8)
+WD_AT = 11
 EARLY = 2
 
 SINGLE = tuple((j, j + 1) for j in range(JT))
-RUNS = (SINGLE, SINGLE, ((0, 2),) + SINGLE[2:5] + ((5, 8),), SINGLE[:4] + ((4, 8),))
+RUNS = (SINGLE, SINGLE, SINGLE[:5] + ((5, 8),), SINGLE[:4] + ((4, 8),))
 
 AT = {
     "got_s": 960,
@@ -65,15 +64,26 @@ AT = {
     "we_w": 18432,
     "wa_raw11": 20480,
     "wd_raw1": 26496,
+    "act12": 26496,
+    "act13": 28544,
     "wc_w": 5952,
     "page1": 34816,
     "wa_bf0": 42944,
-    "h_bf31": 47104,
+    "h_bf30": 47104,
     "page2": 49088,
+    "act14": 59392,
+    "h_s21": 59648,
+    "h_s31": 59904,
+    "act9": 61440,
+    "h_s10": 61440,
+    "h_s20": 61696,
+    "h_s30": 61952,
+    "h_s01": 62208,
+    "wd_s0": 62464,
+    "wa_bf1": 71680,
+    "wd_bf0": 71680,
     "zeros": 63488,
     "page3": 63488,
-    "h_bf30": 61440,
-    "wd_q0": 61440,
 }
 
 
@@ -106,7 +116,7 @@ def tile_list_sniff_correction_kernel(
         tab_s = held([P, T], U8, "tab_s")
         got_s = staged([P, S], U8, "got_s")
         wb_s_raw = held([P, H], U8, "wb_s_raw")
-        planes = held([P, S + KP], U8, "planes")
+        planes = held([P, S + H], U8, "planes")
         pages = {}
 
         def clear_on_vector(words):
@@ -132,13 +142,19 @@ def tile_list_sniff_correction_kernel(
         nc.scalar.activation(warm[:, 1:2], warm[:, 0:1], ACT.Silu)
         zeros = staged([P, P + 1], F32, "zeros")
         nc.vector.memset(zeros[:].bitcast(I32), 0)
+        nc.gpsimd.memset(tab_s[:].bitcast(I32), 0)
         clear_on_vector(wb_s_raw[:].bitcast(I32))
 
         nc.sync.dma_start(pick[:], offs)
+        late_planes = held([P, LATE], U8, "late_planes")
+        wc_s = late_planes[:, 0:N]
+        we_s = late_planes[:, N:LATE]
+        nc.sync.dma_start(out=wc_s[0:P:8, :].bitcast(I32), in_=wc_scales[0].bitcast(I32))
         nc.sync.dma_start(
-            out=tab_s[:].bitcast(I32),
-            in_=tab_scales[0].bitcast(I32).unsqueeze(1).to_broadcast([16, 8, T // 4]),
+            out=we_s[0:P:8, :].bitcast(I32).rearrange("q (a w) -> q a w", a=HB),
+            in_=we_scales.bitcast(I32).rearrange("a q w -> q a w"),
         )
+        nc.sync.dma_start(out=tab_s[0:P:8, :].bitcast(I32), in_=tab_scales[0].bitcast(I32))
         nc.sync.dma_start(out=wb_s_raw[0:P:8, :].bitcast(I32), in_=wb_scales[0].bitcast(I32))
         wa0 = load_wa(0, 0, 2)
         nc.sync.dma_start(
@@ -147,14 +163,6 @@ def tile_list_sniff_correction_kernel(
         )
         wb_raw = held([P, 2 * H], U8, "wb_raw")
         nc.sync.dma_start(out=wb_raw[:].bitcast(I32), in_=wb_words[0].bitcast(I32))
-        late_planes = held([P, KP + LATE], U8, "late_planes")
-        wc_s = late_planes[:, KP : KP + N]
-        we_s = late_planes[:, KP + N : KP + LATE]
-        nc.sync.dma_start(out=wc_s[0:P:8, :].bitcast(I32), in_=wc_scales[0].bitcast(I32))
-        nc.sync.dma_start(
-            out=we_s[0:P:8, :].bitcast(I32).rearrange("q (a w) -> q a w", a=HB),
-            in_=we_scales.bitcast(I32).rearrange("a q w -> q a w"),
-        )
 
         pages[0] = held([P, T2], F32, "page0")
         clear_on_vector(pages[0][:, 0:PAGE0_ON_VECTOR].bitcast(I32))
@@ -169,15 +177,11 @@ def tile_list_sniff_correction_kernel(
 
         nc.vector.tensor_copy(got_s[:], tab_s[:].indirect(pick[:]))
         v_s = planes[:, 0:S]
-        wb_s = [planes[:, S : S + KP], late_planes[:, 0:KP]]
-
-        def order_wb_scales(b):
-            nc.vector.tensor_copy(
-                wb_s[b].rearrange("p (t m) -> p t m", t=PACK),
-                wb_s_raw[:, b * KP : (b + 1) * KP].rearrange("p (m t) -> p t m", t=PACK),
-            )
-
-        order_wb_scales(0)
+        wb_s = planes[:, S : S + H]
+        nc.vector.tensor_copy(
+            wb_s.rearrange("p (b t m) -> p b t m", b=HB, t=PACK),
+            wb_s_raw[:].rearrange("p (b m t) -> p b t m", b=HB, t=PACK),
+        )
         nc.vector.tensor_copy(v_s.bitcast(I32), got_s[:].bitcast(I32))
         move_rows(planes)
         wa1 = [load_wa(1, half, 1) for half in range(2)]
@@ -185,7 +189,6 @@ def tile_list_sniff_correction_kernel(
         wa_bf = [staged([P, KP * PACK], BF16, "wa_bf0")]
         wa_q = [held([P, KP], U32, "wa_q%d" % b) for b in range(HB)]
         wa_s = [held([P, KP], U8, "wa_s%d" % b) for b in range(HB)]
-        wd_s = [held([P, N], U8, "wd_s%d" % b) for b in range(HB)]
 
         def round_wa(copy, b, raw, first, m0, m1):
             dst = wa_bf[b][:].rearrange("p (t m i) -> p m i t", t=PACK, i=PACK)
@@ -215,15 +218,13 @@ def tile_list_sniff_correction_kernel(
         round_wa(nc.scalar.copy, 0, wa0, 0, 0, WA0_ON_SCALAR)
         round_wa(nc.vector.tensor_copy, 0, wa0, 0, WA0_ON_SCALAR, P)
         quantize_wa(0)
-        order_wb_scales(1)
-        move_rows(late_planes)
         for b in range(HB):
             order_wb(b)
         for span in SPANS:
             gather_words(*span)
         pages[1] = staged([P, T2], F32, "page1")
         nc.gpsimd.memset(pages[1][:].bitcast(I32), 0)
-        wa_bf.append(held([P, KP * PACK], BF16, "wa_bf1"))
+        wa_bf.append(staged([P, KP * PACK], BF16, "wa_bf1"))
 
         wd_raw = [staged([P, PACK, N], F32, "wd_raw%d" % b) for b in range(HB)]
         we_w = staged([P, HB * 2 * N], U8, "we_w")
@@ -236,38 +237,40 @@ def tile_list_sniff_correction_kernel(
                 in_=wd[b * KP : (b + 1) * KP, :].rearrange("(p i) n -> p i n", i=PACK),
             )
 
-        load_wd(0)
+        for b in range(HB):
+            load_wd(b)
+        move_rows(late_planes)
         nc.sync.dma_start(
             out=wc_w[:].bitcast(I32),
             in_=wc_words[0].rearrange("p c i -> p (c i)").bitcast(I32),
         )
-        load_wd(1)
         nc.sync.dma_start(
             out=we_w[:].bitcast(I32).rearrange("p (a w) -> p a w", a=HB),
             in_=we_words.bitcast(I32).rearrange("a p w -> p a w"),
         )
         nc.sync.dma_start(place[:], offs2)
 
-        wd_bf = [placed([P, N, PACK], BF16, "wd_bf%d" % b) for b in range(HB)]
+        wd_bf = {}
 
-        def wd_views(b, n0, n1):
-            groups = slice(n0 // 4, n1 // 4)
-            return (
-                wd_bf[b][:].rearrange("p (c u) i -> p c i u", u=4)[:, groups],
-                wd_raw[b][:].rearrange("p i (c u) -> p c i u", u=4)[:, groups],
+        def round_wd_on_gpsimd(b):
+            nc.gpsimd.tensor_scalar(
+                wd_bf[b][:, WD_ON_SCALAR[b] : N], wd_raw[b][:, :, WD_ON_SCALAR[b] : N].rearrange("p i n -> p n i"),
+                -1.0, 0.0, ALU.mult, ALU.add,
             )
 
-        def wd_piece(b, piece):
-            return wd_raw[b][:, :, piece * WD_PIECE : (piece + 1) * WD_PIECE]
+        def round_wd_on_scalar(b):
+            groups = slice(0, WD_ON_SCALAR[b] // 4)
+            nc.scalar.activation(
+                wd_bf[b][:].rearrange("p (c u) i -> p c i u", u=4)[:, groups],
+                wd_raw[b][:].rearrange("p i (c u) -> p c i u", u=4)[:, groups],
+                ACT.Copy, scale=-1.0,
+            )
 
-        def round_wd_on_scalar(b, piece):
-            n0 = piece * WD_PIECE
-            nc.scalar.activation(*wd_views(b, n0, n0 + WD_PIECE), ACT.Copy, scale=-1.0)
-
-        wd_q = {}
+        wd_q, wd_s = {}, {}
 
         def quantize_wd(b):
-            wd_q[b] = placed([P, N], U32, "wd_q%d" % b)
+            wd_q[b] = held([P, N], U32, "wd_q%d" % b)
+            wd_s[b] = placed([P, N], U8, "wd_s%d" % b)
             nc.vector.quantize_mx(
                 out=wd_q[b][:].bitcast(FP8X4), scales=wd_s[b][:], in_=wd_bf[b][:].rearrange("p n i -> p (n i)")
             )
@@ -283,9 +286,6 @@ def tile_list_sniff_correction_kernel(
             m = slice(j % 2 * P, (j % 2 + 1) * P)
             return h_q[j // 2, b][:, m].bitcast(FP8X4), h_s[j // 2, b][:, m]
 
-        def by_entry(sums):
-            return sums[:].rearrange("p t (u j) -> p u j t", u=PACK)
-
         def first_products(k):
             j, b = UNITS[k]
             codes, scales = table_tile(j)
@@ -300,15 +300,11 @@ def tile_list_sniff_correction_kernel(
             for t in range(PACK):
                 nc.tensor.matmul_mx(
                     out=b_ps[:, t, :], lhsT=wb_w[b][:, 2 * t * P : 2 * (t + 1) * P].bitcast(FP4X4),
-                    lhsT_scale=wb_s[b][:, t * P : (t + 1) * P],
+                    lhsT_scale=wb_s[:, b * KP + t * P : b * KP + (t + 1) * P],
                     rhs=codes, rhs_scale=scales, start=True, stop=True,
                 )
-            if k in ACT_ON_WD:
-                act = wd_piece(*ACT_ON_WD[k])
-            else:
-                act = placed([P, PACK, P], F32, "act%d" % k)[:]
-            act = act.rearrange("p u (j t) -> p u j t", t=PACK)
-            nc.scalar.activation(act, by_entry(a_ps), ACT.Silu)
+            act = placed([P, P, PACK], F32, "act%d" % k)
+            nc.scalar.activation(act[:], a_ps[:].rearrange("p t j -> p j t"), ACT.Silu)
             unit_parts[k] = (b_ps, act)
 
         def hidden(k):
@@ -317,13 +313,12 @@ def tile_list_sniff_correction_kernel(
             if j % 2 == 0:
                 h_bf[j // 2, b] = placed([P, 2 * P, PACK], BF16, "h_bf%d%d" % (j // 2, b))
             nc.vector.tensor_tensor(
-                h_bf[j // 2, b][:, j % 2 * P : (j % 2 + 1) * P].rearrange("p (u j) t -> p u j t", u=PACK),
-                act, by_entry(b_ps), ALU.mult,
+                h_bf[j // 2, b][:, j % 2 * P : (j % 2 + 1) * P], act[:], b_ps[:].rearrange("p t j -> p j t"), ALU.mult
             )
 
         def quantize_hidden(u, b):
             h_q[u, b] = placed([P, 2 * P], U32, "h_q%d%d" % (u, b))
-            h_s[u, b] = held([P, 2 * P], U8, "h_s%d%d" % (u, b))
+            h_s[u, b] = placed([P, 2 * P], U8, "h_s%d%d" % (u, b))
             nc.vector.quantize_mx(
                 out=h_q[u, b][:].bitcast(FP8X4), scales=h_s[u, b][:],
                 in_=h_bf[u, b][:].rearrange("p j t -> p (j t)"),
@@ -412,12 +407,11 @@ def tile_list_sniff_correction_kernel(
 
         def e_term(j):
             e_view = e_sum[j][:].rearrange("j (p i) -> j i p", i=PACK)
+            e_part[j] = held([P, PACK, P], F32, "e_part%d" % (j % 2))
             if j in JOINED + TURNED:
-                e_part[j] = ring.tile([P, PACK, P], F32, name="e_part", bufs=3)[:]
-                nc.scalar.activation(e_part[j], e_view, ACT.Copy, scale=-2.0)
+                nc.scalar.activation(e_part[j][:], e_view, ACT.Copy, scale=-2.0)
             else:
-                e_part[j] = wd_piece(*ACT_ON_WD[11])
-                nc.vector.scalar_tensor_tensor(e_part[j], gate[j][:], 1.0, e_view, ALU.subtract, ALU.mult)
+                nc.vector.scalar_tensor_tensor(e_part[j][:], gate[j][:], 1.0, e_view, ALU.subtract, ALU.mult)
 
         def d_term(j):
             d_view = d_sum[j][:].rearrange("j (p i) -> j i p", i=PACK)
@@ -459,11 +453,21 @@ def tile_list_sniff_correction_kernel(
                 if j == JT - 1:
                     nc.sync.dma_start(out=out_rows[:, i, :], in_=pages[i][:])
 
+        def open_second_stage():
+            quantize_hidden(0, 1)
+            quantize_wd(0)
+            quantize_hidden(1, 0)
+            quantize_hidden(2, 0)
+            quantize_wd(1)
+            gate_of(0)
+            second_products(0)
+
         def close_first_stage():
-            interpolate(1)
-            quantize_hidden(3, 1)
-            pages[2] = staged([P, T2], F32, "page2")
-            nc.gpsimd.memset(pages[2][:].bitcast(I32), 0)
+            d_term(1)
+            for u in range(2, JT // 2):
+                quantize_hidden(u, 1)
+            e_products(1)
+            e_term(1)
             place_ready(0)
             gate_of(2)
             second_products(2)
@@ -481,35 +485,30 @@ def tile_list_sniff_correction_kernel(
         for k in range(-AHEAD, len(UNITS)):
             if k >= 0:
                 hidden(k)
+            if k == WD_AT:
+                open_second_stage()
             if k + AHEAD < len(UNITS):
                 first_products(k + AHEAD)
-            for b, piece in WD_PIECES_AT.get(k, ()):
-                round_wd_on_scalar(b, piece)
             if k in (0, 1):
                 m0 = k * P // 2
                 round_wa(nc.vector.tensor_copy, 1, wa1[m0 * 2 // P], m0, m0, m0 + P // 2)
             if k == WA1_AT:
+                quantize_hidden(0, 0)
                 quantize_wa(1)
+                for b in range(HB):
+                    wd_bf[b] = placed([P, N, PACK], BF16, "wd_bf%d" % b)
+                    round_wd_on_gpsimd(b)
                 nc.sync.dma_start(out=wg[:], in_=wgo)
-            if k == WD0_ON_VECTOR_AT:
-                nc.vector.tensor_scalar(*wd_views(0, WD0_ON_SCALAR, N), -1.0, None, ALU.mult)
-            if k in WD_AT:
-                quantize_wd(WD_AT.index(k))
-            if k in QUANTISE_AT:
-                quantize_hidden(*QUANTISE_AT[k])
-            if k == 7:
-                gate_of(0)
-            if k == 10:
-                e_products(0)
-            if k == 11:
-                d_products(0)
-                e_term(0)
-            if k == 12:
-                d_term(0)
+            if k in WD_ROUNDED_AT:
+                round_wd_on_scalar(WD_ROUNDED_AT.index(k))
+            if k == WD_AT + 1:
+                quantize_hidden(1, 1)
+                quantize_hidden(3, 0)
+                pages[2] = staged([P, T2], F32, "page2")
+                nc.gpsimd.memset(pages[2][:].bitcast(I32), 0)
+                interpolate(0)
                 add_terms(0, Y_BANK)
                 gate_of(1)
-            if k == 13:
-                e_products(1)
                 d_products(1)
         close_first_stage()
         for j in range(EARLY, JT):

@@ -53,7 +53,7 @@ WD_AT = 11
 EARLY = 2
 
 SINGLE = tuple((j, j + 1) for j in range(JT))
-RUNS = (SINGLE, SINGLE, SINGLE[:5] + ((5, 8),), SINGLE[:4] + ((4, 8),))
+RUNS = (SINGLE, SINGLE) + (SINGLE[:4] + ((4, 8),),) * 2
 
 AT = {
     "got_s": 960,

@@ -39,7 +39,7 @@ D_BANKS = (Y_BANK,) + (6, 2) * 3 + (6,)
 ROWS_PAIR = (1, 3)
 LAST_PARTS = ((ROWS_PAIR[0], 0, 1), (ROWS_PAIR[1], 1, 2), (Y_BANK, 2, 4))
 
-JOINED = (1, 2, 3)
+JOINED = {0: N // 2, 1: N, 2: N, 3: N}
 TURNED = (4, 5, 6, 7)
 
 WA0_ON_SCALAR = 64
@@ -365,13 +365,13 @@ def tile_list_sniff_correction_kernel(
         def transpose(dst, src, first, last):
             nc.tensor.matmul(dst, src, ident[:], start=first, stop=last, is_transpose=True)
 
-        def we_passes(j, dst, last):
+        def we_passes(j, dst, cols, last):
             for b in range(HB):
                 codes, scales = h_pass(j, b)
                 nc.tensor.matmul_mx(
-                    out=dst[:], lhsT=codes, lhsT_scale=scales,
-                    rhs=we_w[:, 2 * b * N : 2 * (b + 1) * N].bitcast(FP4X4),
-                    rhs_scale=we_s[:, b * N : (b + 1) * N],
+                    out=dst[:, 0:cols], lhsT=codes, lhsT_scale=scales,
+                    rhs=we_w[:, 2 * b * N : 2 * (b * N + cols)].bitcast(FP4X4),
+                    rhs_scale=we_s[:, b * N : b * N + cols],
                     start=(b == 0), stop=(last and b == HB - 1),
                 )
 
@@ -381,7 +381,7 @@ def tile_list_sniff_correction_kernel(
                 for q in range(N // P):
                     transpose(e_sum[j][:, q * P : (q + 1) * P], copied[j][0][:, q, :], True, True)
             else:
-                we_passes(j, e_sum[j], True)
+                we_passes(j, e_sum[j], N, True)
 
         def d_products(j):
             d_sum[j] = bank(D_BANKS[j], [P, N])
@@ -391,15 +391,16 @@ def tile_list_sniff_correction_kernel(
                     transpose(d_sum[j][:, q * P : (q + 1) * P], e_sb[:, q, :], True, False)
                     transpose(d_sum[j][:, q * P : (q + 1) * P], d_sb[:, q, :], False, True)
                 return
-            if j in JOINED:
-                we_passes(j, d_sum[j], False)
-            for b in range(HB):
-                codes, scales = h_pass(j, b)
-                nc.tensor.matmul_mx(
-                    out=d_sum[j][:], lhsT=codes, lhsT_scale=scales,
-                    rhs=wd_q[b][:].bitcast(FP8X4), rhs_scale=wd_s[b][:],
-                    start=(b == 0 and j not in JOINED), stop=(b == HB - 1),
-                )
+            cols = JOINED[j]
+            we_passes(j, d_sum[j], cols, False)
+            for c0 in range(0, N, cols):
+                for b in range(HB):
+                    codes, scales = h_pass(j, b)
+                    nc.tensor.matmul_mx(
+                        out=d_sum[j][:, c0 : c0 + cols], lhsT=codes, lhsT_scale=scales,
+                        rhs=wd_q[b][:, c0 : c0 + cols].bitcast(FP8X4), rhs_scale=wd_s[b][:, c0 : c0 + cols],
+                        start=False, stop=(c0 + cols == N and b == HB - 1),
+                    )
 
         def second_products(j):
             e_products(j)
@@ -408,10 +409,12 @@ def tile_list_sniff_correction_kernel(
         def e_term(j):
             e_view = e_sum[j][:].rearrange("j (p i) -> j i p", i=PACK)
             e_part[j] = held([P, PACK, P], F32, "e_part%d" % (j % 2))
-            if j in JOINED + TURNED:
-                nc.scalar.activation(e_part[j][:], e_view, ACT.Copy, scale=-2.0)
-            else:
-                nc.vector.scalar_tensor_tensor(e_part[j][:], gate[j][:], 1.0, e_view, ALU.subtract, ALU.mult)
+            rows = JOINED.get(j, N) // PACK
+            nc.scalar.activation(e_part[j][:, :, 0:rows], e_view[:, :, 0:rows], ACT.Copy, scale=-2.0)
+            if rows < P:
+                nc.vector.scalar_tensor_tensor(
+                    e_part[j][:, :, rows:P], gate[j][:, :, rows:P], 1.0, e_view[:, :, rows:P], ALU.subtract, ALU.mult
+                )
 
         def d_term(j):
             d_view = d_sum[j][:].rearrange("j (p i) -> j i p", i=PACK)
@@ -441,6 +444,12 @@ def tile_list_sniff_correction_kernel(
 
         out_rows = out.rearrange("(p i) t -> p i t", i=PACK)
 
+        def store(i):
+            queues = (nc.sync, nc.scalar) if i == PACK - 1 else (nc.sync,)
+            cols = T2 // len(queues)
+            for c, queue in enumerate(queues):
+                queue.dma_start(out=out_rows[:, i, c * cols : (c + 1) * cols], in_=pages[i][:, c * cols : (c + 1) * cols])
+
         def place_ready(j):
             for i in range(PACK):
                 for j0, j1 in RUNS[i]:
@@ -451,7 +460,7 @@ def tile_list_sniff_correction_kernel(
                             y[:, i, cols], wg[:, cols], ALU.mult,
                         )
                 if j == JT - 1:
-                    nc.sync.dma_start(out=out_rows[:, i, :], in_=pages[i][:])
+                    store(i)
 
         def open_second_stage():
             quantize_hidden(0, 1)
@@ -506,9 +515,10 @@ def tile_list_sniff_correction_kernel(
                 quantize_hidden(3, 0)
                 pages[2] = staged([P, T2], F32, "page2")
                 nc.gpsimd.memset(pages[2][:].bitcast(I32), 0)
+                gate_of(1)
+            if k == WD_AT + 2:
                 interpolate(0)
                 add_terms(0, Y_BANK)
-                gate_of(1)
                 d_products(1)
         close_first_stage()
         for j in range(EARLY, JT):

@@ -32,8 +32,6 @@ A_BANKS = (0, 1, 4) * 4 + (0, 1) * 2
 B_BANKS = (2, 3, 6, 7) * 3 + (2, 3) * 2
 Y_BANK = 4
 GATE_BANKS = (6, 7) + (5,) * (JT - 2)
-E_BANKS = (0,) + (1,) * (JT - 1)
-E_BANKS = (0, 1) + (5,) * (JT - 2)
 E_BANKS = (5,) + (0, 7) * 3 + (0,)
 D_BANKS = (Y_BANK,) + (6, 2) * 3 + (6,)
 ROWS_PAIR = (1, 3)
@@ -140,8 +138,8 @@ def tile_list_sniff_correction_kernel(
         warm = held([P, 2], F32, "warm")
         nc.vector.memset(warm[:, 0:1], 0.0)
         nc.scalar.activation(warm[:, 1:2], warm[:, 0:1], ACT.Silu)
-        zeros = staged([P, P + 1], F32, "zeros")
-        nc.vector.memset(zeros[:].bitcast(I32), 0)
+        zeros = staged([P, P], F32, "zeros")
+        clear_on_vector(zeros[:].bitcast(I32))
         nc.gpsimd.memset(tab_s[:].bitcast(I32), 0)
         clear_on_vector(wb_s_raw[:].bitcast(I32))
 
@@ -168,7 +166,7 @@ def tile_list_sniff_correction_kernel(
         clear_on_vector(pages[0][:, 0:PAGE0_ON_VECTOR].bitcast(I32))
         ident = held([P, P], F32, "ident")
         nc.gpsimd.affine_select(
-            out=ident[:], in_=zeros[:, 0:P], pattern=[[-1, P]], compare_op=ALU.not_equal, fill=1.0,
+            out=ident[:], in_=zeros[:], pattern=[[-1, P]], compare_op=ALU.not_equal, fill=1.0,
             base=0, channel_multiplier=1,
         )
         pages[3] = staged([P, T2], F32, "page3")

@@ -41,7 +41,6 @@ JOINED = {0: N // 2, 1: N, 2: N, 3: N}
 TURNED = (4, 5, 6, 7)
 
 WA0_ON_SCALAR = 64
-PAGE0_ON_VECTOR = 1504
 
 WD_ON_SCALAR = (N // 4, 3 * N // 4)
 
@@ -163,7 +162,7 @@ def tile_list_sniff_correction_kernel(
         nc.sync.dma_start(out=wb_raw[:].bitcast(I32), in_=wb_words[0].bitcast(I32))
 
         pages[0] = held([P, T2], F32, "page0")
-        clear_on_vector(pages[0][:, 0:PAGE0_ON_VECTOR].bitcast(I32))
+        clear_on_vector(pages[0][:].bitcast(I32))
         ident = held([P, P], F32, "ident")
         nc.gpsimd.affine_select(
             out=ident[:], in_=zeros[:], pattern=[[-1, P]], compare_op=ALU.not_equal, fill=1.0,
@@ -171,7 +170,6 @@ def tile_list_sniff_correction_kernel(
         )
         pages[3] = staged([P, T2], F32, "page3")
         nc.gpsimd.memset(pages[3][:].bitcast(I32), 0)
-        nc.gpsimd.memset(pages[0][:, PAGE0_ON_VECTOR:T2].bitcast(I32), 0)
 
         nc.vector.tensor_copy(got_s[:], tab_s[:].indirect(pick[:]))
         v_s = planes[:, 0:S]

from contextlib import ExitStack

import concourse.mybir as mybir

K, H, N, T, S, T2 = 512, 1024, 512, 2048, 1024, 2048
FLOPS = 2 * S * (2 * K * H + K * N + 2 * H * N)

F32 = mybir.dt.float32
BF16 = mybir.dt.bfloat16
I32 = mybir.dt.int32
U32 = mybir.dt.uint32
U16 = mybir.dt.uint16
U8 = mybir.dt.uint8
FP8X4 = mybir.dt.float8_e4m3fn_x4
FP4X4 = mybir.dt.float4_e2m1fn_x4
ACT = mybir.ActivationFunctionType
ALU = mybir.AluOpType

P = 128
PACK = 4
KP = P * PACK
HB = H // KP
JT = S // P
LIST_COLS = P // 16
LATE = N + HB * N

UNITS = [(j, b) for b in range(HB) for j in range(JT)]
AHEAD = 2
SPANS = ((0, 2), (2, 4), (4, 8))

A_BANKS = (0, 1, 4) * 4 + (0, 1) * 2
B_BANKS = (2, 3, 6, 7) * 3 + (2, 3) * 2
Y_BANK = 4
GATE_BANKS = (6, 7) + (5,) * (JT - 2)
E_BANKS = (5,) + (0, 7) * 3 + (0,)
D_BANKS = (Y_BANK,) + (6, 2) * 3 + (6,)
ROWS_PAIR = (1, 3)
LAST_PARTS = ((ROWS_PAIR[0], 0, 1), (ROWS_PAIR[1], 1, 2), (Y_BANK, 2, 4))

JOINED = {0: N // 2, 1: N, 2: N, 3: N}
TURNED = (4, 5, 6, 7)

WA0_ON_SCALAR = 64

WD_ON_SCALAR = (N // 4, 3 * N // 4)

WA1_AT = 2
WD_ROUNDED_AT = (5, 8)
WD_AT = 11
EARLY = 2

SINGLE = tuple((j, j + 1) for j in range(JT))
RUNS = (SINGLE, SINGLE) + (SINGLE[:4] + ((4, 8),),) * 2

AT = {
    "got_s": 960,
    "wa_raw10": 1920,
    "wg": 1920 - 1024,
    "wd_raw0": 10240,
    "wa_raw00": 18368,
    "we_w": 18432,
    "wa_raw11": 20480,
    "wd_raw1": 26496,
    "act12": 26496,
    "act13": 28544,
    "wc_w": 5952,
    "page1": 34816,
    "wa_bf0": 42944,
    "h_bf30": 47104,
    "page2": 49088,
    "act14": 59392,
    "h_s21": 59648,
    "h_s31": 59904,
    "act9": 61440,
    "h_s10": 61440,
    "h_s20": 61696,
    "h_s30": 61952,
    "h_s01": 62208,
    "wd_s0": 62464,
    "wa_bf1": 71680,
    "wd_bf0": 71680,
    "zeros": 63488,
    "page3": 63488,
}


def tile_list_sniff_correction_kernel(
    tc, tab_words, tab_scales, offs, wa, wb_words, wb_scales, wc_words, wc_scales,
    wd, we_words, we_scales, offs2, wgo, out,
):
    nc = tc.nc
    with ExitStack() as ctx:
        keep = ctx.enter_context(tc.tile_pool(name="keep", bufs=1))
        stage = ctx.enter_context(tc.tile_pool(name="stage", bufs=1))
        ring = ctx.enter_context(tc.tile_pool(name="ring", bufs=2))
        psum = ctx.enter_context(tc.psum_pool(name="psum", bufs=1))

        def held(shape, dtype, name):
            return keep.tile(shape, dtype, name=name, tag=name, align_bytes=64)

        def staged(shape, dtype, name):
            return stage.tile(shape, dtype, name=name, align_bytes=64, offset=AT[name])

        def placed(shape, dtype, name):
            return staged(shape, dtype, name) if name in AT else held(shape, dtype, name)

        def bank(number, shape):
            return psum.tile(shape, F32, name="bank%d" % number)

        pick = held([P, S // 16], U16, "pick")
        place = held([P, S // 16], U16, "place")
        tab_w = held([P, T], U32, "tab_w")
        tab_s = held([P, T], U8, "tab_s")
        got_s = staged([P, S], U8, "got_s")
        wb_s_raw = held([P, H], U8, "wb_s_raw")
        planes = held([P, S + H], U8, "planes")
        pages = {}

        def clear_on_vector(words):
            cols = words.shape[1]
            nc.vector.memset(words[:, 0 : cols // 2 - 1], 0)
            nc.vector.memset(words[:, cols // 2 - 1 : cols], 0)

        def load_wa(b, half, halves):
            cols = halves * KP // 2
            raw = staged([P, PACK, cols], F32, "wa_raw%d%d" % (b, half))
            c0 = b * KP + half * KP // 2
            nc.sync.dma_start(out=raw[:], in_=wa.rearrange("(p i) c -> p i c", i=PACK)[:, :, c0 : c0 + cols])
            return raw

        def move_rows(tile):
            for r in range(1, 4):
                nc.sync.dma_start(
                    out=tile[:].bitcast(I32)[r:P:32, :], in_=tile[:].bitcast(I32)[8 * r : P : 32, :]
                )

        warm = held([P, 2], F32, "warm")
        nc.vector.memset(warm[:, 0:1], 0.0)
        nc.scalar.activation(warm[:, 1:2], warm[:, 0:1], ACT.Silu)
        zeros = staged([P, P], F32, "zeros")
        clear_on_vector(zeros[:].bitcast(I32))
        nc.gpsimd.memset(tab_s[:].bitcast(I32), 0)
        clear_on_vector(wb_s_raw[:].bitcast(I32))

        nc.sync.dma_start(pick[:], offs)
        late_planes = held([P, LATE], U8, "late_planes")
        wc_s = late_planes[:, 0:N]
        we_s = late_planes[:, N:LATE]
        nc.sync.dma_start(out=wc_s[0:P:8, :].bitcast(I32), in_=wc_scales[0].bitcast(I32))
        nc.sync.dma_start(
            out=we_s[0:P:8, :].bitcast(I32).rearrange("q (a w) -> q a w", a=HB),
            in_=we_scales.bitcast(I32).rearrange("a q w -> q a w"),
        )
        nc.sync.dma_start(out=tab_s[0:P:8, :].bitcast(I32), in_=tab_scales[0].bitcast(I32))
        nc.sync.dma_start(out=wb_s_raw[0:P:8, :].bitcast(I32), in_=wb_scales[0].bitcast(I32))
        wa0 = load_wa(0, 0, 2)
        nc.sync.dma_start(
            out=tab_w[:].bitcast(I32),
            in_=tab_words[0].rearrange("p t i -> p (t i)").bitcast(I32),
        )
        wb_raw = held([P, 2 * H], U8, "wb_raw")
        nc.sync.dma_start(out=wb_raw[:].bitcast(I32), in_=wb_words[0].bitcast(I32))

        pages[0] = held([P, T2], F32, "page0")
        clear_on_vector(pages[0][:].bitcast(I32))
        ident = held([P, P], F32, "ident")
        nc.gpsimd.affine_select(
            out=ident[:], in_=zeros[:], pattern=[[-1, P]], compare_op=ALU.not_equal, fill=1.0,
            base=0, channel_multiplier=1,
        )
        pages[3] = staged([P, T2], F32, "page3")
        nc.gpsimd.memset(pages[3][:].bitcast(I32), 0)

        nc.vector.tensor_copy(got_s[:], tab_s[:].indirect(pick[:]))
        v_s = planes[:, 0:S]
        wb_s = planes[:, S : S + H]
        nc.vector.tensor_copy(
            wb_s.rearrange("p (b t m) -> p b t m", b=HB, t=PACK),
            wb_s_raw[:].rearrange("p (b m t) -> p b t m", b=HB, t=PACK),
        )
        nc.vector.tensor_copy(v_s.bitcast(I32), got_s[:].bitcast(I32))
        move_rows(planes)
        wa1 = [load_wa(1, half, 1) for half in range(2)]

        wa_bf = [staged([P, KP * PACK], BF16, "wa_bf0")]
        wa_q = [held([P, KP], U32, "wa_q%d" % b) for b in range(HB)]
        wa_s = [held([P, KP], U8, "wa_s%d" % b) for b in range(HB)]

        def round_wa(copy, b, raw, first, m0, m1):
            dst = wa_bf[b][:].rearrange("p (t m i) -> p m i t", t=PACK, i=PACK)
            src = raw[:].rearrange("p i (m t) -> p m i t", t=PACK)
            copy(dst[:, m0:m1], src[:, m0 - first : m1 - first])

        def quantize_wa(b):
            nc.vector.quantize_mx(
                out=wa_q[b][:].bitcast(FP8X4), scales=wa_s[b][:], in_=wa_bf[b][:]
            )

        v_w = []

        def gather_words(j0, j1):
            words = held([P, (j1 - j0) * P], U32, "v_w%d" % j0)
            nc.vector.tensor_copy(words[:], tab_w[:].indirect(pick[:, j0 * LIST_COLS : j1 * LIST_COLS]))
            v_w.extend(words[:, c : c + P] for c in range(0, (j1 - j0) * P, P))

        wb_w = [held([P, 2 * KP], U8, "wb_w%d" % b) for b in range(HB)]

        def order_wb(b):
            nc.scalar.copy(
                wb_w[b][:].bitcast(U16).rearrange("p (t m) -> p t m", t=PACK),
                wb_raw[:, 2 * b * KP : 2 * (b + 1) * KP].bitcast(U16).rearrange("p (m t) -> p t m", t=PACK),
            )

        round_wa(nc.scalar.copy, 0, wa0, 0, 0, WA0_ON_SCALAR)
        round_wa(nc.vector.tensor_copy, 0, wa0, 0, WA0_ON_SCALAR, P)
        quantize_wa(0)
        for b in range(HB):
            order_wb(b)
        for span in SPANS:
            gather_words(*span)
        pages[1] = staged([P, T2], F32, "page1")
        nc.gpsimd.memset(pages[1][:].bitcast(I32), 0)
        wa_bf.append(staged([P, KP * PACK], BF16, "wa_bf1"))

        wd_raw = [staged([P, PACK, N], F32, "wd_raw%d" % b) for b in range(HB)]
        we_w = staged([P, HB * 2 * N], U8, "we_w")
        wc_w = staged([P, N], U32, "wc_w")
        wg = staged([P, S], F32, "wg")

        def load_wd(b):
            nc.sync.dma_start(
                out=wd_raw[b][:],
                in_=wd[b * KP : (b + 1) * KP, :].rearrange("(p i) n -> p i n", i=PACK),
            )

        for b in range(HB):
            load_wd(b)
        move_rows(late_planes)
        nc.sync.dma_start(
            out=wc_w[:].bitcast(I32),
            in_=wc_words[0].rearrange("p c i -> p (c i)").bitcast(I32),
        )
        nc.sync.dma_start(
            out=we_w[:].bitcast(I32).rearrange("p (a w) -> p a w", a=HB),
            in_=we_words.bitcast(I32).rearrange("a p w -> p a w"),
        )
        nc.sync.dma_start(place[:], offs2)

        wd_bf = {}

        def round_wd_on_gpsimd(b):
            nc.gpsimd.tensor_scalar(
                wd_bf[b][:, WD_ON_SCALAR[b] : N], wd_raw[b][:, :, WD_ON_SCALAR[b] : N].rearrange("p i n -> p n i"),
                -1.0, 0.0, ALU.mult, ALU.add,
            )

        def round_wd_on_scalar(b):
            groups = slice(0, WD_ON_SCALAR[b] // 4)
            nc.scalar.activation(
                wd_bf[b][:].rearrange("p (c u) i -> p c i u", u=4)[:, groups],
                wd_raw[b][:].rearrange("p i (c u) -> p c i u", u=4)[:, groups],
                ACT.Copy, scale=-1.0,
            )

        wd_q, wd_s = {}, {}

        def quantize_wd(b):
            wd_q[b] = held([P, N], U32, "wd_q%d" % b)
            wd_s[b] = placed([P, N], U8, "wd_s%d" % b)
            nc.vector.quantize_mx(
                out=wd_q[b][:].bitcast(FP8X4), scales=wd_s[b][:], in_=wd_bf[b][:].rearrange("p n i -> p (n i)")
            )

        y = held([P, PACK, S], F32, "y")
        h_bf, h_q, h_s = {}, {}, {}
        unit_parts, gate, copied, e_sum, d_sum, e_part, d_part = {}, {}, {}, {}, {}, {}, {}

        def table_tile(j):
            return v_w[j].bitcast(FP8X4), v_s[:, j * P : (j + 1) * P]

        def h_pass(j, b):
            m = slice(j % 2 * P, (j % 2 + 1) * P)
            return h_q[j // 2, b][:, m].bitcast(FP8X4), h_s[j // 2, b][:, m]

        def first_products(k):
            j, b = UNITS[k]
            codes, scales = table_tile(j)
            a_ps = bank(A_BANKS[k], [P, PACK, P])
            b_ps = bank(B_BANKS[k], [P, PACK, P])
            for t in range(PACK):
                m = slice(t * P, (t + 1) * P)
                nc.tensor.matmul_mx(
                    out=a_ps[:, t, :], lhsT=wa_q[b][:, m].bitcast(FP8X4), lhsT_scale=wa_s[b][:, m],
                    rhs=codes, rhs_scale=scales, start=True, stop=True,
                )
            for t in range(PACK):
                nc.tensor.matmul_mx(
                    out=b_ps[:, t, :], lhsT=wb_w[b][:, 2 * t * P : 2 * (t + 1) * P].bitcast(FP4X4),
                    lhsT_scale=wb_s[:, b * KP + t * P : b * KP + (t + 1) * P],
                    rhs=codes, rhs_scale=scales, start=True, stop=True,
                )
            act = placed([P, P, PACK], F32, "act%d" % k)
            nc.scalar.activation(act[:], a_ps[:].rearrange("p t j -> p j t"), ACT.Silu)
            unit_parts[k] = (b_ps, act)

        def hidden(k):
            j, b = UNITS[k]
            b_ps, act = unit_parts[k]
            if j % 2 == 0:
                h_bf[j // 2, b] = placed([P, 2 * P, PACK], BF16, "h_bf%d%d" % (j // 2, b))
            nc.vector.tensor_tensor(
                h_bf[j // 2, b][:, j % 2 * P : (j % 2 + 1) * P], act[:], b_ps[:].rearrange("p t j -> p j t"), ALU.mult
            )

        def quantize_hidden(u, b):
            h_q[u, b] = placed([P, 2 * P], U32, "h_q%d%d" % (u, b))
            h_s[u, b] = placed([P, 2 * P], U8, "h_s%d%d" % (u, b))
            nc.vector.quantize_mx(
                out=h_q[u, b][:].bitcast(FP8X4), scales=h_s[u, b][:],
                in_=h_bf[u, b][:].rearrange("p j t -> p (j t)"),
            )

        def gate_of(j):
            codes, scales = table_tile(j)
            c_ps = bank(GATE_BANKS[j], [P, N])
            gate[j] = ring.tile([P, PACK, P], F32, name="gate", bufs=3)
            nc.tensor.matmul_mx(
                out=c_ps[:], lhsT=codes, lhsT_scale=scales,
                rhs=wc_w[:].bitcast(FP8X4), rhs_scale=wc_s, start=True, stop=True,
            )
            nc.scalar.activation(
                gate[j][:], c_ps[:].rearrange("j (p i) -> j i p", i=PACK), ACT.Tanh, scale=0.5
            )

        def turned_products(j):
            e_rows = bank(ROWS_PAIR[0], [P, PACK, P])
            d_rows = bank(ROWS_PAIR[1], [P, PACK, P])
            for q in range(N // P):
                for b in range(HB):
                    c0 = b * N + q * P
                    codes, scales = h_pass(j, b)
                    nc.tensor.matmul_mx(
                        out=e_rows[:, q, :], lhsT=we_w[:, 2 * c0 : 2 * (c0 + P)].bitcast(FP4X4),
                        lhsT_scale=we_s[:, c0 : c0 + P], rhs=codes, rhs_scale=scales,
                        start=(b == 0), stop=(b == HB - 1),
                    )
            for q in range(N // P):
                for b in range(HB):
                    n = slice(q * P, (q + 1) * P)
                    codes, scales = h_pass(j, b)
                    nc.tensor.matmul_mx(
                        out=d_rows[:, q, :], lhsT=wd_q[b][:, n].bitcast(FP8X4), lhsT_scale=wd_s[b][:, n],
                        rhs=codes, rhs_scale=scales, start=(b == 0), stop=(b == HB - 1),
                    )
            e_sb = ring.tile([P, PACK, P], F32, name="e_sb")
            d_sb = ring.tile([P, PACK, P], F32, name="d_sb")
            nc.scalar.copy(e_sb[:], e_rows[:])
            nc.scalar.copy(d_sb[:], d_rows[:])
            copied[j] = (e_sb, d_sb)

        def transpose(dst, src, first, last):
            nc.tensor.matmul(dst, src, ident[:], start=first, stop=last, is_transpose=True)

        def we_passes(j, dst, cols, last):
            for b in range(HB):
                codes, scales = h_pass(j, b)
                nc.tensor.matmul_mx(
                    out=dst[:, 0:cols], lhsT=codes, lhsT_scale=scales,
                    rhs=we_w[:, 2 * b * N : 2 * (b * N + cols)].bitcast(FP4X4),
                    rhs_scale=we_s[:, b * N : b * N + cols],
                    start=(b == 0), stop=(last and b == HB - 1),
                )

        def e_products(j):
            e_sum[j] = bank(E_BANKS[j], [P, N])
            if j in TURNED:
                for q in range(N // P):
                    transpose(e_sum[j][:, q * P : (q + 1) * P], copied[j][0][:, q, :], True, True)
            else:
                we_passes(j, e_sum[j], N, True)

        def d_products(j):
            d_sum[j] = bank(D_BANKS[j], [P, N])
            if j in TURNED:
                e_sb, d_sb = copied[j]
                for q in range(N // P):
                    transpose(d_sum[j][:, q * P : (q + 1) * P], e_sb[:, q, :], True, False)
                    transpose(d_sum[j][:, q * P : (q + 1) * P], d_sb[:, q, :], False, True)
                return
            cols = JOINED[j]
            we_passes(j, d_sum[j], cols, False)
            for c0 in range(0, N, cols):
                for b in range(HB):
                    codes, scales = h_pass(j, b)
                    nc.tensor.matmul_mx(
                        out=d_sum[j][:, c0 : c0 + cols], lhsT=codes, lhsT_scale=scales,
                        rhs=wd_q[b][:, c0 : c0 + cols].bitcast(FP8X4), rhs_scale=wd_s[b][:, c0 : c0 + cols],
                        start=False, stop=(c0 + cols == N and b == HB - 1),
                    )

        def second_products(j):
            e_products(j)
            d_products(j)

        def e_term(j):
            e_view = e_sum[j][:].rearrange("j (p i) -> j i p", i=PACK)
            e_part[j] = held([P, PACK, P], F32, "e_part%d" % (j % 2))
            rows = JOINED.get(j, N) // PACK
            nc.scalar.activation(e_part[j][:, :, 0:rows], e_view[:, :, 0:rows], ACT.Copy, scale=-2.0)
            if rows < P:
                nc.vector.scalar_tensor_tensor(
                    e_part[j][:, :, rows:P], gate[j][:, :, rows:P], 1.0, e_view[:, :, rows:P], ALU.subtract, ALU.mult
                )

        def d_term(j):
            d_view = d_sum[j][:].rearrange("j (p i) -> j i p", i=PACK)
            d_part[j] = ring.tile([P, PACK, P], F32, name="d_part", bufs=3)
            nc.vector.scalar_tensor_tensor(d_part[j][:], gate[j][:], 1.0, d_view, ALU.add, ALU.mult)

        def interpolate(j):
            e_term(j)
            d_term(j)

        def add_page(j, i, dst):
            transpose(dst, e_part[j][:, i, :], True, False)
            transpose(dst, d_part[j][:, i, :], False, True)

        def add_terms(j, number):
            y_ps = bank(number, [P, PACK, P])
            for i in range(PACK):
                add_page(j, i, y_ps[:, i, :])
            nc.scalar.activation(y[:, :, j * P : (j + 1) * P], y_ps[:], ACT.Copy, scale=-0.5)

        def add_last_terms(j):
            for number, i0, i1 in LAST_PARTS:
                y_ps = bank(number, [P, i1 - i0, P])
                for i in range(i0, i1):
                    add_page(j, i, y_ps[:, i - i0, :])
                nc.scalar.activation(y[:, i0:i1, j * P : (j + 1) * P], y_ps[:], ACT.Copy, scale=-0.5)

        out_rows = out.rearrange("(p i) t -> p i t", i=PACK)

        def store(i):
            queues = (nc.sync, nc.scalar) if i == PACK - 1 else (nc.sync,)
            cols = T2 // len(queues)
            for c, queue in enumerate(queues):
                queue.dma_start(out=out_rows[:, i, c * cols : (c + 1) * cols], in_=pages[i][:, c * cols : (c + 1) * cols])

        def place_ready(j):
            for i in range(PACK):
                for j0, j1 in RUNS[i]:
                    if j1 - 1 == j:
                        cols = slice(j0 * P, j1 * P)
                        nc.vector.tensor_tensor(
                            pages[i][:].indirect(place[:, j0 * LIST_COLS : j1 * LIST_COLS]),
                            y[:, i, cols], wg[:, cols], ALU.mult,
                        )
                if j == JT - 1:
                    store(i)

        def open_second_stage():
            quantize_hidden(0, 1)
            quantize_wd(0)
            quantize_hidden(1, 0)
            quantize_hidden(2, 0)
            quantize_wd(1)
            gate_of(0)
            second_products(0)

        def close_first_stage():
            d_term(1)
            for u in range(2, JT // 2):
                quantize_hidden(u, 1)
            e_products(1)
            e_term(1)
            place_ready(0)
            gate_of(2)
            second_products(2)

        def second_stage(j):
            add_terms(j - 1, Y_BANK)
            place_ready(j - 1)
            if j + 2 in TURNED:
                turned_products(j + 2)
            if j + 1 < JT:
                gate_of(j + 1)
                second_products(j + 1)
            interpolate(j)

        for k in range(-AHEAD, len(UNITS)):
            if k >= 0:
                hidden(k)
            if k == WD_AT:
                open_second_stage()
            if k + AHEAD < len(UNITS):
                first_products(k + AHEAD)
            if k in (0, 1):
                m0 = k * P // 2
                round_wa(nc.vector.tensor_copy, 1, wa1[m0 * 2 // P], m0, m0, m0 + P // 2)
            if k == WA1_AT:
                quantize_hidden(0, 0)
                quantize_wa(1)
                for b in range(HB):
                    wd_bf[b] = placed([P, N, PACK], BF16, "wd_bf%d" % b)
                    round_wd_on_gpsimd(b)
                nc.sync.dma_start(out=wg[:], in_=wgo)
            if k in WD_ROUNDED_AT:
                round_wd_on_scalar(WD_ROUNDED_AT.index(k))
            if k == WD_AT + 1:
                quantize_hidden(1, 1)
                quantize_hidden(3, 0)
                pages[2] = staged([P, T2], F32, "page2")
                nc.gpsimd.memset(pages[2][:].bitcast(I32), 0)
                gate_of(1)
            if k == WD_AT + 2:
                interpolate(0)
                add_terms(0, Y_BANK)
                d_products(1)
        close_first_stage()
        for j in range(EARLY, JT):
            second_stage(j)
        add_last_terms(JT - 1)
        place_ready(JT - 1)
